import numpy as np
import ml_dtypes


def mxq(x, axis, fmt="e4m3"):
    dtype, down = {"e4m3": (ml_dtypes.float8_e4m3fn, 7), "e5m2": (ml_dtypes.float8_e5m2, 14)}[fmt]
    v = np.moveaxis(np.asarray(x, np.float32).astype(ml_dtypes.bfloat16).astype(np.float64), axis, -1)
    blocks = v.reshape(v.shape[:-1] + (-1, 32))
    amax = np.abs(blocks).max(-1, keepdims=True)
    byte = np.maximum(np.where(amax > 0, np.frexp(amax)[1] - 1 + 127, 0) - down, 1)
    scale = np.exp2(byte - 127.0)
    codes = (blocks / scale).astype(np.float32).astype(dtype).astype(np.float64)
    return np.moveaxis((codes * scale).reshape(v.shape), -1, axis)


WIDE = False


def mx_kscale(k):
    if not WIDE:
        return np.ones(k)
    levels = np.array([10, -10, 5, -5, 0])
    if k % 512:
        return np.exp2(np.random.permutation(np.resize(levels, k // 32))).repeat(32)
    a = np.empty((k // 512, 16))
    for p in range(k // 512):
        a[p, :8] = np.random.permutation(np.resize(levels, 8))
        for g in range(8):
            far = levels[np.abs(levels - a[p, g]) >= 10]
            a[p, g + 8] = far[np.random.randint(len(far))]
    return np.exp2(a.ravel()).repeat(32)


def f64(x):
    return np.asarray(x).astype(np.float64)


def striped(idx):
    return np.tile(idx.reshape(-1, 16).T, (8, 1)).astype(np.uint16)


def unstriped(offs):
    return offs[:16].T.reshape(-1).astype(np.int64)


E2M1 = np.array([0.0, 0.5, 1.0, 1.5, 2.0, 3.0, 4.0, 6.0, -0.0, -0.5, -1.0, -1.5, -2.0, -3.0, -4.0, -6.0])


def pack_weight(w, fmt):
    k, n = w.shape
    w = f64(np.asarray(w, np.float32).astype(ml_dtypes.bfloat16)).reshape(k // 32, 32, n)
    amax = np.abs(w).max(1)
    if fmt == "e4m3":
        byte = np.frexp(amax)[1] - 1 + 127 - 7
    else:
        mant, ex = np.frexp(amax / 6.0)
        byte = np.where(mant > 0.5, ex, ex - 1) + 127
    byte = np.clip(np.where(amax > 0, byte, 1), 1, 254)
    scaled = (w * np.exp2(127.0 - byte)[:, None, :]).reshape(k, n).astype(np.float32)
    by_word = np.ascontiguousarray(scaled.reshape(k // 512, 128, 4, n).transpose(0, 1, 3, 2))
    if fmt == "e4m3":
        words = by_word.astype(ml_dtypes.float8_e4m3fn).view(np.uint8)
    else:
        c = by_word.astype(ml_dtypes.float4_e2m1fn).view(np.uint8) & 0xF
        words = (c[..., 0::2] | (c[..., 1::2] << 4)).reshape(k // 512, 128, 2 * n)
    return np.ascontiguousarray(words), np.ascontiguousarray(byte.astype(np.uint8).reshape(k // 512, 16, n))


def unpack_weight(words, scales, fmt):
    g, _, n = scales.shape
    words = np.ascontiguousarray(words).reshape(g, 128, n, -1)
    if fmt == "e4m3":
        vals = words.view(ml_dtypes.float8_e4m3fn).astype(np.float64)
    else:
        nib = np.empty((g, 128, n, 4), np.uint8)
        nib[..., 0::2] = words & 0xF
        nib[..., 1::2] = words >> 4
        vals = E2M1[nib]
    vals = vals * np.repeat(np.exp2(scales.astype(np.float64) - 127.0), 8, axis=1)[..., None]
    return vals.transpose(0, 1, 3, 2).reshape(g * 512, n)


def gelu(v):
    return 0.5 * v * (1.0 + np.tanh(np.sqrt(2.0 / np.pi) * (v + 0.044715 * v**3)))


def striped8(idx):
    return np.concatenate([v.reshape(-1, 16).T for v in idx]).astype(np.uint16)


def unstriped8(offs):
    return np.stack([offs[16 * g:16 * g + 16].T.reshape(-1) for g in range(8)]).astype(np.int64)


def runs(v, idx8):
    k = np.arange(v.shape[0])
    return v[k[:, None], idx8[k % 512 // 64]]


def often(T, S):
    return np.random.permutation(T)[(T * np.random.uniform(0, 1, S) ** 4).astype(np.int64)]


K, H, T, S = 1024, 1024, 2048, 512

def setup_inputs():
    n = np.random.standard_normal
    s = mx_kscale(K)[:, None]
    u = mx_kscale(H)[:, None]
    tab_words, tab_scales = pack_weight(n((K, T)) * s, "e4m3")
    offs = striped8(np.stack([often(T, S) for _ in range(8)]))
    w1_words, w1_scales = pack_weight(n((K, H)) / np.sqrt(K) / s, "e2m1")
    b1 = (0.5 * n(H)).astype(np.float32)
    w2 = (n((K, H)) / np.sqrt(K) / s * u.T).astype(np.float32)
    w3_words, w3_scales = pack_weight(n((H, K)) / np.sqrt(H) / u, "e4m3")
    wr = ((np.eye(K) + 0.5 * n((K, K)) / np.sqrt(K)) / s).astype(np.float32)
    return {"tab_words": tab_words, "tab_scales": tab_scales, "offs": offs,
            "w1_words": w1_words, "w1_scales": w1_scales, "b1": b1, "w2": w2,
            "w3_words": w3_words, "w3_scales": w3_scales, "wr": wr}

def reference(tab_words, tab_scales, offs, w1_words, w1_scales, b1, w2,
              w3_words, w3_scales, wr):
    v = runs(unpack_weight(tab_words, tab_scales, "e4m3"), unstriped8(offs))
    w1 = unpack_weight(w1_words, w1_scales, "e2m1")
    w3 = unpack_weight(w3_words, w3_scales, "e4m3")
    w2q = mxq(f64(w2), 0, "e4m3")
    wrq = mxq(f64(wr), 0, "e4m3")
    a = (w1.T @ v) + f64(b1)[:, None]
    gate = 0.5 * a * (1.0 + np.tanh(np.sqrt(2.0 / np.pi) * (a + 0.044715 * a * a * a)))
    h = gate * (w2q.T @ v)
    hq = mxq(h, 0, "e4m3")
    return w3.T @ hq + wrq.T @ v

@@ -1,0 +1,290 @@
+from contextlib import ExitStack
+
+import concourse.mybir as mybir
+
+K, H, T, S = 1024, 1024, 2048, 512
+FLOPS = 2 * S * (K * H + K * H + H * K + K * K)
+
+F32 = mybir.dt.float32
+BF16 = mybir.dt.bfloat16
+I32 = mybir.dt.int32
+U32 = mybir.dt.uint32
+U16 = mybir.dt.uint16
+U8 = mybir.dt.uint8
+E4M3 = mybir.dt.float8_e4m3fn_x4
+E2M1 = mybir.dt.float4_e2m1fn_x4
+GELU = mybir.ActivationFunctionType.Gelu_apprx_tanh
+MULT = mybir.AluOpType.mult
+
+P = 128
+PACK = 4
+KP = P * PACK
+PASSES = K // KP
+JQ = 128
+REUSES = {
+    "w2_raw00a": "tab_rows0",
+    "w2_raw00b": "tab_rows1",
+    "w3_code0": "tab_rows1",
+    "w2_raw01": "tab0",
+    "w3_code1": "tab0",
+    "w2_raw10": "w1_rows",
+    "wr_raw2": "w1_rows",
+    "w2_raw11": "tab1",
+    "wr_raw4": "tab1",
+    "w3_scale": "picked_rows",
+    "wr_raw0": "w2_bf00",
+    "wr_raw1": "w2_bf01",
+    "w2_bf10": "w2_00_code",
+    "wr_raw3": "w2_00_code",
+    "result0": "w2_00_code",
+    "w2_bf11": "gate0",
+    "wr_bf0": "w1_scale1",
+    "wr_bf3": "w1_scale1",
+    "w2_10_code": "w2_01_code",
+    "wr_0_code": "w2_11_code",
+    "wr_bf1": "gate1",
+    "wr_bf4": "gate1",
+    "wr_bf2": "h_bf1",
+}
+WR_PIECES = [(0, 0, 512), (1, 0, 512), (0, 512, 512), (1, 512, 256), (1, 768, 256)]
+WR_VECTOR_C = (0, 128, 384, 0, 256)
+
+
+def tile_list_ast_slot_block_kernel(
+    tc, tab_words, tab_scales, offs, w1_words, w1_scales, b1, w2, w3_words, w3_scales, wr, out
+):
+    nc = tc.nc
+    with ExitStack() as ctx:
+        keep = ctx.enter_context(tc.tile_pool(name="keep", bufs=1))
+        psum = ctx.enter_context(tc.psum_pool(name="psum", bufs=1))
+
+        def sb(shape, dtype, name):
+            return keep.tile(shape, dtype, name=name, tag=REUSES.get(name, name), align_bytes=64)
+
+        def bank(n):
+            return psum.tile([P, S], F32, name=f"bank{n}")
+
+        def zeroed(width, name):
+            tile = sb([P, width], U8, name)
+            nc.vector.memset(tile[:].bitcast(I32), 0)
+            return tile
+
+        def load_words(words, dtype, width, name):
+            tile = sb([P, width], dtype, name)
+            nc.sync.dma_start(tile[:].bitcast(I32), words.bitcast(I32))
+            return tile
+
+        def load_e4m3(words, a, name):
+            return load_words(words[a].rearrange("p c i -> p (c i)"), U32, words.shape[2], name)
+
+        def load_rows(w, a, c0, width, name):
+            raw = sb([P, PACK, width], F32, name)
+            rows = w[a * KP : (a + 1) * KP, c0 : c0 + width]
+            nc.sync.dma_start(raw[:], rows.rearrange("(p j) c -> p j c", j=PACK))
+            return raw
+
+        def load_wr(n):
+            return load_rows(wr, *WR_PIECES[n], f"wr_raw{n}")
+
+        offsets = keep.tile([P, S // 16], U16, name="offsets")
+        nc.sync.dma_start(offsets[:], offs)
+
+        tab_rows = [zeroed(T, f"tab_rows{a}") for a in range(PASSES)]
+        w1_rows = zeroed(PASSES * H, "w1_rows")
+        v_scale = zeroed(PASSES * S, "v_scale")
+        for a in range(PASSES):
+            nc.sync.dma_start(tab_rows[a][:].bitcast(I32)[0:P:8, :], tab_scales[a].bitcast(I32))
+        bias = sb([P, H // KP, PACK], F32, "bias")
+        nc.sync.dma_start(bias[:], b1.rearrange("(b p t) -> p b t", p=P, t=PACK))
+        w1_raw = [load_words(w1_words[0], U16, H, "w1_raw0")]
+        tab = [load_e4m3(tab_words, 0, "tab0")]
+        for r in range(4):
+            nc.sync.dma_start(
+                w1_rows[:].bitcast(I32).rearrange("p (a c) -> p a c", a=PASSES)[r:P:32],
+                w1_scales.bitcast(I32).rearrange("a (d r) c -> r d a c", r=4)[r],
+            )
+        w1_raw.append(load_words(w1_words[1], U16, H, "w1_raw1"))
+        tab.append(load_e4m3(tab_words, 1, "tab1"))
+
+        picked_rows = sb([P, PASSES * S], U8, "picked_rows")
+        for a in range(PASSES):
+            nc.vector.tensor_copy(picked_rows[:, a * S : (a + 1) * S], tab_rows[a][:].indirect(offsets[:]))
+        first_a = load_rows(w2, 0, 0, KP // 2, "w2_raw00a")
+        for d in range(4):
+            nc.scalar.dma_start(
+                v_scale[:].bitcast(I32)[32 * d : 32 * d + 4, :],
+                picked_rows[:].bitcast(I32)[32 * d : 32 * d + 32 : 8, :],
+            )
+        first_b = load_rows(w2, 0, KP // 2, KP // 2, "w2_raw00b")
+
+        def order_w1(a):
+            code, scale = sb([P, H], U16, f"w1_code{a}"), sb([P, H], U8, f"w1_scale{a}")
+            for dst, src in ((code, w1_raw[a][:]), (scale, w1_rows[:, a * H : (a + 1) * H])):
+                nc.vector.tensor_copy(
+                    dst[:].rearrange("p (b t m) -> p b m t", t=PACK, m=P),
+                    src.rearrange("p (b m t) -> p b m t", t=PACK, m=P),
+                )
+            return code, scale
+
+        def gather_words(a):
+            code = sb([P, S], U32, f"v_code{a}")
+            nc.vector.tensor_copy(code[:], tab[a][:].indirect(offsets[:]))
+            return code
+
+        def times_v(acc, code, scale, a, j0, width, start, stop):
+            nc.tensor.matmul_mx(
+                acc,
+                lhsT=code,
+                lhsT_scale=scale,
+                rhs=v_code[a][:, j0 : j0 + width].bitcast(E4M3),
+                rhs_scale=v_scale[:, a * S + j0 : a * S + j0 + width],
+                start=start,
+                stop=stop,
+            )
+
+        def w1_pass(acc, b, t, a):
+            code, scale = w1_q[a]
+            cols = slice(b * KP + t * P, b * KP + (t + 1) * P)
+            times_v(acc[:], code[:, cols].bitcast(E2M1), scale[:, cols], a, 0, S, a == 0, a == PASSES - 1)
+
+        def gelu(gate, acc, b, t):
+            nc.scalar.activation(gate[:, t, :], acc[:], GELU, bias=bias[:, b, t : t + 1])
+
+        def w2_views(grouped, raw):
+            return (
+                grouped[:].rearrange("p (t m j) -> p m j t", t=PACK, j=PACK),
+                raw[:].rearrange("p j (m t) -> p m j t", t=PACK),
+            )
+
+        def quantise(grouped, width, name):
+            code = sb([P, width], U32, name + "_code")
+            scale = sb([P, width], U8, name + "_scale")
+            nc.vector.quantize_mx(code[:].bitcast(E4M3), scale[:], grouped[:])
+            return code, scale
+
+        def w2_passes(accs, quantised):
+            for jq in range(S // JQ):
+                for a, (code, scale) in enumerate(quantised):
+                    for t in range(PACK):
+                        times_v(
+                            accs[jq][:, t * JQ : (t + 1) * JQ],
+                            code[:, t * P : (t + 1) * P].bitcast(E4M3), scale[:, t * P : (t + 1) * P],
+                            a, jq * JQ, JQ, a == 0 and t == 0, a == PASSES - 1 and t == PACK - 1,
+                        )
+
+        def gate_quarter(h_bf, accs, gate, jq):
+            nc.vector.tensor_tensor(
+                h_bf[:, jq * JQ * PACK : (jq + 1) * JQ * PACK].rearrange("p (c i t) -> p c t i", i=4, t=PACK),
+                accs[jq][:].rearrange("p (t c i) -> p c t i", t=PACK, i=4),
+                gate[:, :, jq * JQ : (jq + 1) * JQ].rearrange("p t (c i) -> p c t i", i=4),
+                MULT,
+            )
+
+        def gate_times(accs, gate, b):
+            h_bf = sb([P, S * PACK], BF16, f"h_bf{b}")
+            for jq in range(S // JQ):
+                gate_quarter(h_bf, accs, gate, jq)
+            return h_bf
+
+        w1_q = [order_w1(0)]
+        v_code = [gather_words(0)]
+        raw01 = load_rows(w2, 1, 0, KP, "w2_raw01")
+        w1_q.append(order_w1(1))
+        raw10 = load_rows(w2, 0, KP, KP, "w2_raw10")
+        v_code.append(gather_words(1))
+        raw11 = load_rows(w2, 1, KP, KP, "w2_raw11")
+        w3_scale = zeroed(K, "w3_scale")
+        for d in range(4):
+            nc.sync.dma_start(
+                w3_scale[:].bitcast(I32)[32 * d : 32 * d + 8, :],
+                w3_scales.bitcast(I32)[:, 4 * d : 4 * d + 4, :],
+            )
+
+        def first_product(gate, b, t, n):
+            acc = bank(n)
+            for a in range(PASSES):
+                w1_pass(acc, b, t, a)
+            gelu(gate, acc, b, t)
+
+        gate0 = sb([P, PACK, S], F32, "gate0")
+        for t in range(PACK):
+            first_product(gate0, 0, t, t)
+        bf00 = sb([P, KP * PACK], BF16, "w2_bf00")
+        for half, raw in enumerate((first_a, first_b)):
+            dst, src = w2_views(bf00, raw)
+            nc.vector.tensor_copy(dst[:, half * (P // 2) : (half + 1) * (P // 2)], src)
+        w3_code = [load_e4m3(w3_words, 0, "w3_code0")]
+        q00 = quantise(bf00, KP, "w2_00")
+        wr_raw = [load_wr(0)]
+        bf01 = sb([P, KP * PACK], BF16, "w2_bf01")
+        nc.vector.tensor_copy(*w2_views(bf01, raw01))
+        w3_code.append(load_e4m3(w3_words, 1, "w3_code1"))
+        q01 = quantise(bf01, KP, "w2_01")
+        wr_raw.append(load_wr(1))
+        g_accs = [bank(PACK + jq) for jq in range(S // JQ)]
+        w2_passes(g_accs, (q00, q01))
+        gate1 = sb([P, PACK, S], F32, "gate1")
+        for t in (0, 1):
+            first_product(gate1, 1, t, t)
+        bf10 = sb([P, KP * PACK], BF16, "w2_bf10")
+        nc.scalar.copy(*w2_views(bf10, raw10))
+        wr_raw.append(load_wr(2))
+        h_bf0 = gate_times(g_accs, gate0, 0)
+        for t in (2, 3):
+            first_product(gate1, 1, t, t + 2)
+        q10 = quantise(bf10, KP, "w2_10")
+        wr_raw.append(load_wr(3))
+        bf11 = sb([P, KP * PACK], BF16, "w2_bf11")
+        nc.vector.tensor_copy(*w2_views(bf11, raw11))
+        wr_raw.append(load_wr(4))
+        q11 = quantise(bf11, KP, "w2_11")
+        g_accs = [bank(n) for n in (2, 3, 6, 7)]
+        w2_passes(g_accs, (q10, q11))
+        h_q = [quantise(h_bf0, S, "h_0")]
+        h_bf1 = sb([P, S * PACK], BF16, "h_bf1")
+        h1_code, h1_scale = sb([P, S], U32, "h_1_code"), sb([P, S], U8, "h_1_scale")
+        h_q.append((h1_code, h1_scale))
+        for jq in range(S // JQ):
+            gate_quarter(h_bf1, g_accs, gate1, jq)
+            if jq in (2, 3):
+                cols = slice((jq - 2) * 256, (jq - 1) * 256)
+                nc.vector.quantize_mx(
+                    h1_code[:, cols].bitcast(E4M3), h1_scale[:, cols],
+                    h_bf1[:, (jq - 2) * 1024 : (jq - 1) * 1024],
+                )
+
+        wr_q = {}
+        for n, (a, c0, width) in enumerate(WR_PIECES):
+            grouped = sb([P, width * PACK], BF16, f"wr_bf{n}")
+            dst = grouped[:].rearrange("p (c i j) -> p c j i", i=4, j=PACK)
+            src = wr_raw[n][:].rearrange("p j (c i) -> p c j i", i=4)
+            cut = WR_VECTOR_C[n] // 4
+            if cut > 0:
+                nc.vector.tensor_copy(dst[:, :cut], src[:, :cut])
+            if cut < width // 4:
+                nc.scalar.copy(dst[:, cut:], src[:, cut:])
+            code, scale = quantise(grouped, width, f"wr_{n}")
+            for c in range(0, width, P):
+                wr_q[a, (c0 + c) // P] = (code[:, c : c + P], scale[:, c : c + P])
+
+        for n in range(K // P):
+            acc = bank((0, 1, 4, 5, 2, 3, 6, 7)[n])
+            for a, j0, width in ((0, 0, S), (1, 0, S // 2), (1, S // 2, S // 2)):
+                nc.tensor.matmul_mx(
+                    acc[:, j0 : j0 + width],
+                    lhsT=w3_code[a][:, n * P : (n + 1) * P].bitcast(E4M3),
+                    lhsT_scale=w3_scale[4 * a :, n * P : (n + 1) * P],
+                    rhs=h_q[a][0][:, j0 : j0 + width].bitcast(E4M3),
+                    rhs_scale=h_q[a][1][:, j0 : j0 + width],
+                    start=a == 0,
+                    stop=False,
+                )
+            for a in range(PASSES):
+                code, scale = wr_q[a, n]
+                times_v(acc[:], code.bitcast(E4M3), scale, a, 0, S, False, a == PASSES - 1)
+            result = sb([P, S], F32, f"result{n}")
+            if n % 2 == 0 or n < 4:
+                nc.scalar.copy(result[:], acc[:])
+            else:
+                nc.vector.tensor_copy(result[:], acc[:])
+            nc.sync.dma_start(out[n * P : (n + 1) * P, :], result[:])

@@ -21,33 +21,14 @@ PACK = 4
 KP = P * PACK
 PASSES = K // KP
 JQ = 128
-REUSES = {
-    "w2_raw00a": "tab_rows0",
-    "w2_raw00b": "tab_rows1",
-    "w3_code0": "tab_rows1",
-    "w2_raw01": "tab0",
-    "w3_code1": "tab0",
-    "w2_raw10": "w1_rows",
-    "wr_raw2": "w1_rows",
-    "w2_raw11": "tab1",
-    "wr_raw4": "tab1",
-    "w3_scale": "picked_rows",
-    "wr_raw0": "w2_bf00",
-    "wr_raw1": "w2_bf01",
-    "w2_bf10": "w2_00_code",
-    "wr_raw3": "w2_00_code",
-    "result0": "w2_00_code",
-    "w2_bf11": "gate0",
-    "wr_bf0": "w1_scale1",
-    "wr_bf3": "w1_scale1",
-    "w2_10_code": "w2_01_code",
-    "wr_0_code": "w2_11_code",
-    "wr_bf1": "gate1",
-    "wr_bf4": "gate1",
-    "wr_bf2": "h_bf1",
-}
+REUSES = {"h_bf11":"wr_bf0","h_11_code":"wr_bf1"}
 WR_PIECES = [(0, 0, 512), (1, 0, 512), (0, 512, 512), (1, 512, 256), (1, 768, 256)]
-WR_VECTOR_C = (0, 128, 384, 0, 256)
+WR_VECTOR_C = (0,0,128,256,256)
+W2_VECTOR_M = (128,128,0,64)
+H_SPLIT = (4, 1)
+H_PART = (512, 256)
+OUT_BANKS = (4,5,0,1,6,7,2,3)
+OUT_ON_VECTOR = (5,7)
 
 
 def tile_list_ast_slot_block_kernel(
@@ -83,53 +64,60 @@ def tile_list_ast_slot_block_kernel(
             nc.sync.dma_start(raw[:], rows.rearrange("(p j) c -> p j c", j=PACK))
             return raw
 
+        def load_w2(b, a):
+            w2_raw[b, a] = load_rows(w2, a, b * KP, KP, f"w2_raw{b}{a}")
+
         def load_wr(n):
-            return load_rows(wr, *WR_PIECES[n], f"wr_raw{n}")
+            wr_raw[n] = load_rows(wr, *WR_PIECES[n], f"wr_raw{n}")
 
-        offsets = keep.tile([P, S // 16], U16, name="offsets")
-        nc.sync.dma_start(offsets[:], offs)
+        def load_w3(a, half):
+            words = w3_words[a][:, half * KP : (half + 1) * KP, :].rearrange("p c i -> p (c i)")
+            w3_code[a, half] = load_words(words, U32, KP, f"w3_code{a}{half}")
 
-        tab_rows = [zeroed(T, f"tab_rows{a}") for a in range(PASSES)]
-        w1_rows = zeroed(PASSES * H, "w1_rows")
-        v_scale = zeroed(PASSES * S, "v_scale")
-        for a in range(PASSES):
-            nc.sync.dma_start(tab_rows[a][:].bitcast(I32)[0:P:8, :], tab_scales[a].bitcast(I32))
-        bias = sb([P, H // KP, PACK], F32, "bias")
-        nc.sync.dma_start(bias[:], b1.rearrange("(b p t) -> p b t", p=P, t=PACK))
-        w1_raw = [load_words(w1_words[0], U16, H, "w1_raw0")]
-        tab = [load_e4m3(tab_words, 0, "tab0")]
-        for r in range(4):
-            nc.sync.dma_start(
-                w1_rows[:].bitcast(I32).rearrange("p (a c) -> p a c", a=PASSES)[r:P:32],
-                w1_scales.bitcast(I32).rearrange("a (d r) c -> r d a c", r=4)[r],
-            )
-        w1_raw.append(load_words(w1_words[1], U16, H, "w1_raw1"))
-        tab.append(load_e4m3(tab_words, 1, "tab1"))
+        def load_tab(a):
+            tab[a] = load_e4m3(tab_words, a, f"tab{a}")
 
-        picked_rows = sb([P, PASSES * S], U8, "picked_rows")
-        for a in range(PASSES):
-            nc.vector.tensor_copy(picked_rows[:, a * S : (a + 1) * S], tab_rows[a][:].indirect(offsets[:]))
-        first_a = load_rows(w2, 0, 0, KP // 2, "w2_raw00a")
-        for d in range(4):
-            nc.scalar.dma_start(
-                v_scale[:].bitcast(I32)[32 * d : 32 * d + 4, :],
-                picked_rows[:].bitcast(I32)[32 * d : 32 * d + 32 : 8, :],
-            )
-        first_b = load_rows(w2, 0, KP // 2, KP // 2, "w2_raw00b")
+        def load_w1(a):
+            w1_raw[a] = load_words(w1_words[a], U16, H, f"w1_raw{a}")
 
-        def order_w1(a):
-            code, scale = sb([P, H], U16, f"w1_code{a}"), sb([P, H], U8, f"w1_scale{a}")
-            for dst, src in ((code, w1_raw[a][:]), (scale, w1_rows[:, a * H : (a + 1) * H])):
-                nc.vector.tensor_copy(
-                    dst[:].rearrange("p (b t m) -> p b m t", t=PACK, m=P),
-                    src.rearrange("p (b m t) -> p b m t", t=PACK, m=P),
+        def load_w1_scales():
+            for r in range(4):
+                nc.sync.dma_start(
+                    w1_rows[:].bitcast(I32).rearrange("p (a c) -> p a c", a=PASSES)[r:P:32],
+                    w1_scales.bitcast(I32).rearrange("a (d r) c -> r d a c", r=4)[r],
                 )
-            return code, scale
+
+        def load_w3_scales():
+            for d in range(4):
+                nc.sync.dma_start(
+                    w3_scale[:].bitcast(I32)[32 * d : 32 * d + 8, :],
+                    w3_scales.bitcast(I32)[:, 4 * d : 4 * d + 4, :],
+                )
+
+        def move_scales():
+            for d in range(4):
+                nc.sync.dma_start(
+                    v_scale[:].bitcast(I32)[32 * d : 32 * d + 4, :],
+                    picked_rows[:].bitcast(I32)[32 * d : 32 * d + 32 : 8, :],
+                )
+
+        def order_w1(src, dtype, name):
+            dst = sb([P, H], dtype, name)
+            nc.vector.tensor_copy(
+                dst[:].rearrange("p (b t m) -> p b m t", t=PACK, m=P),
+                src.rearrange("p (b m t) -> p b m t", t=PACK, m=P),
+            )
+            return dst
+
+        def order_w1_code(a):
+            w1_code[a] = order_w1(w1_raw[a][:], U16, f"w1_code{a}")
+
+        def order_w1_scale(a):
+            w1_scale[a] = order_w1(w1_rows[:, a * H : (a + 1) * H], U8, f"w1_scale{a}")
 
         def gather_words(a):
-            code = sb([P, S], U32, f"v_code{a}")
-            nc.vector.tensor_copy(code[:], tab[a][:].indirect(offsets[:]))
-            return code
+            v_code[a] = sb([P, S], U32, f"v_code{a}")
+            nc.vector.tensor_copy(v_code[a][:], tab[a][:].indirect(offsets[:]))
 
         def times_v(acc, code, scale, a, j0, width, start, stop):
             nc.tensor.matmul_mx(
@@ -142,18 +130,28 @@ def tile_list_ast_slot_block_kernel(
                 stop=stop,
             )
 
-        def w1_pass(acc, b, t, a):
-            code, scale = w1_q[a]
+        def first_pass(b, t, a, n):
+            if a == 0:
+                pre[b, t] = bank(n)
             cols = slice(b * KP + t * P, b * KP + (t + 1) * P)
-            times_v(acc[:], code[:, cols].bitcast(E2M1), scale[:, cols], a, 0, S, a == 0, a == PASSES - 1)
+            times_v(pre[b, t][:], w1_code[a][:, cols].bitcast(E2M1), w1_scale[a][:, cols], a, 0, S, a == 0, a == PASSES - 1)
+            if a == PASSES - 1:
+                if t == 0:
+                    gate[b] = sb([P, PACK, S], F32, f"gate{b}")
+                nc.scalar.activation(gate[b][:, t, :], pre[b, t][:], GELU, bias=bias[:, b, t : t + 1])
 
-        def gelu(gate, acc, b, t):
-            nc.scalar.activation(gate[:, t, :], acc[:], GELU, bias=bias[:, b, t : t + 1])
+        def round_split(dst, src, cut):
+            if cut > 0:
+                nc.vector.tensor_copy(dst[:, :cut], src[:, :cut])
+            if cut < dst.shape[1]:
+                nc.scalar.copy(dst[:, cut:], src[:, cut:])
 
-        def w2_views(grouped, raw):
-            return (
-                grouped[:].rearrange("p (t m j) -> p m j t", t=PACK, j=PACK),
-                raw[:].rearrange("p j (m t) -> p m j t", t=PACK),
+        def round_w2(b, a):
+            w2_bf[b, a] = sb([P, KP * PACK], BF16, f"w2_bf{b}{a}")
+            round_split(
+                w2_bf[b, a][:].rearrange("p (t m j) -> p m j t", t=PACK, j=PACK),
+                w2_raw[b, a][:].rearrange("p j (m t) -> p m j t", t=PACK),
+                W2_VECTOR_M[b * PASSES + a],
             )
 
         def quantise(grouped, width, name):
@@ -162,129 +160,181 @@ def tile_list_ast_slot_block_kernel(
             nc.vector.quantize_mx(code[:].bitcast(E4M3), scale[:], grouped[:])
             return code, scale
 
-        def w2_passes(accs, quantised):
+        def quantise_w2(b, a):
+            w2_q[b, a] = quantise(w2_bf[b, a], KP, f"w2_{b}{a}")
+
+        def second_product(b, banks):
+            up[b] = [bank(n) for n in banks]
             for jq in range(S // JQ):
-                for a, (code, scale) in enumerate(quantised):
+                for a in range(PASSES):
+                    code, scale = w2_q[b, a]
                     for t in range(PACK):
                         times_v(
-                            accs[jq][:, t * JQ : (t + 1) * JQ],
+                            up[b][jq][:, t * JQ : (t + 1) * JQ],
                             code[:, t * P : (t + 1) * P].bitcast(E4M3), scale[:, t * P : (t + 1) * P],
                             a, jq * JQ, JQ, a == 0 and t == 0, a == PASSES - 1 and t == PACK - 1,
                         )
 
-        def gate_quarter(h_bf, accs, gate, jq):
+        def gate_quarter(b, jq):
+            cut = H_SPLIT[b]
+            if jq in (0, cut):
+                h_bf[b, jq] = sb([P, (cut if jq == 0 else 4 - cut) * JQ * PACK], BF16, f"h_bf{b}{jq}")
+            first = 0 if jq < cut else cut
             nc.vector.tensor_tensor(
-                h_bf[:, jq * JQ * PACK : (jq + 1) * JQ * PACK].rearrange("p (c i t) -> p c t i", i=4, t=PACK),
-                accs[jq][:].rearrange("p (t c i) -> p c t i", t=PACK, i=4),
-                gate[:, :, jq * JQ : (jq + 1) * JQ].rearrange("p t (c i) -> p c t i", i=4),
+                h_bf[b, first][:, (jq - first) * JQ * PACK : (jq - first + 1) * JQ * PACK].rearrange("p (c i t) -> p c t i", i=4, t=PACK),
+                up[b][jq][:].rearrange("p (t c i) -> p c t i", t=PACK, i=4),
+                gate[b][:, :, jq * JQ : (jq + 1) * JQ].rearrange("p t (c i) -> p c t i", i=4),
                 MULT,
             )
 
-        def gate_times(accs, gate, b):
-            h_bf = sb([P, S * PACK], BF16, f"h_bf{b}")
-            for jq in range(S // JQ):
-                gate_quarter(h_bf, accs, gate, jq)
-            return h_bf
-
-        w1_q = [order_w1(0)]
-        v_code = [gather_words(0)]
-        raw01 = load_rows(w2, 1, 0, KP, "w2_raw01")
-        w1_q.append(order_w1(1))
-        raw10 = load_rows(w2, 0, KP, KP, "w2_raw10")
-        v_code.append(gather_words(1))
-        raw11 = load_rows(w2, 1, KP, KP, "w2_raw11")
-        w3_scale = zeroed(K, "w3_scale")
-        for d in range(4):
-            nc.sync.dma_start(
-                w3_scale[:].bitcast(I32)[32 * d : 32 * d + 8, :],
-                w3_scales.bitcast(I32)[:, 4 * d : 4 * d + 4, :],
+        def quantise_h(b, j0, width):
+            part = H_PART[b]
+            if j0 % part == 0:
+                h_q[b, j0 // part] = sb([P, part], U32, f"h_{b}{j0 // part}_code"), sb([P, part], U8, f"h_{b}{j0 // part}_scale")
+            code, scale = h_q[b, j0 // part]
+            first = 0 if j0 < H_SPLIT[b] * JQ else H_SPLIT[b]
+            nc.vector.quantize_mx(
+                code[:, j0 % part : j0 % part + width].bitcast(E4M3), scale[:, j0 % part : j0 % part + width],
+                h_bf[b, first][:, (j0 - first * JQ) * PACK : (j0 - first * JQ + width) * PACK],
             )
 
-        def first_product(gate, b, t, n):
-            acc = bank(n)
-            for a in range(PASSES):
-                w1_pass(acc, b, t, a)
-            gelu(gate, acc, b, t)
+        def round_wr(n):
+            width = WR_PIECES[n][2]
+            wr_bf[n] = sb([P, width * PACK], BF16, f"wr_bf{n}")
+            round_split(
+                wr_bf[n][:].rearrange("p (c i j) -> p c j i", i=4, j=PACK),
+                wr_raw[n][:].rearrange("p j (c i) -> p c j i", i=4),
+                WR_VECTOR_C[n] // 4,
+            )
 
-        gate0 = sb([P, PACK, S], F32, "gate0")
-        for t in range(PACK):
-            first_product(gate0, 0, t, t)
-        bf00 = sb([P, KP * PACK], BF16, "w2_bf00")
-        for half, raw in enumerate((first_a, first_b)):
-            dst, src = w2_views(bf00, raw)
-            nc.vector.tensor_copy(dst[:, half * (P // 2) : (half + 1) * (P // 2)], src)
-        w3_code = [load_e4m3(w3_words, 0, "w3_code0")]
-        q00 = quantise(bf00, KP, "w2_00")
-        wr_raw = [load_wr(0)]
-        bf01 = sb([P, KP * PACK], BF16, "w2_bf01")
-        nc.vector.tensor_copy(*w2_views(bf01, raw01))
-        w3_code.append(load_e4m3(w3_words, 1, "w3_code1"))
-        q01 = quantise(bf01, KP, "w2_01")
-        wr_raw.append(load_wr(1))
-        g_accs = [bank(PACK + jq) for jq in range(S // JQ)]
-        w2_passes(g_accs, (q00, q01))
-        gate1 = sb([P, PACK, S], F32, "gate1")
-        for t in (0, 1):
-            first_product(gate1, 1, t, t)
-        bf10 = sb([P, KP * PACK], BF16, "w2_bf10")
-        nc.scalar.copy(*w2_views(bf10, raw10))
-        wr_raw.append(load_wr(2))
-        h_bf0 = gate_times(g_accs, gate0, 0)
-        for t in (2, 3):
-            first_product(gate1, 1, t, t + 2)
-        q10 = quantise(bf10, KP, "w2_10")
-        wr_raw.append(load_wr(3))
-        bf11 = sb([P, KP * PACK], BF16, "w2_bf11")
-        nc.vector.tensor_copy(*w2_views(bf11, raw11))
-        wr_raw.append(load_wr(4))
-        q11 = quantise(bf11, KP, "w2_11")
-        g_accs = [bank(n) for n in (2, 3, 6, 7)]
-        w2_passes(g_accs, (q10, q11))
-        h_q = [quantise(h_bf0, S, "h_0")]
-        h_bf1 = sb([P, S * PACK], BF16, "h_bf1")
-        h1_code, h1_scale = sb([P, S], U32, "h_1_code"), sb([P, S], U8, "h_1_scale")
-        h_q.append((h1_code, h1_scale))
-        for jq in range(S // JQ):
-            gate_quarter(h_bf1, g_accs, gate1, jq)
-            if jq in (2, 3):
-                cols = slice((jq - 2) * 256, (jq - 1) * 256)
-                nc.vector.quantize_mx(
-                    h1_code[:, cols].bitcast(E4M3), h1_scale[:, cols],
-                    h_bf1[:, (jq - 2) * 1024 : (jq - 1) * 1024],
-                )
-
-        wr_q = {}
-        for n, (a, c0, width) in enumerate(WR_PIECES):
-            grouped = sb([P, width * PACK], BF16, f"wr_bf{n}")
-            dst = grouped[:].rearrange("p (c i j) -> p c j i", i=4, j=PACK)
-            src = wr_raw[n][:].rearrange("p j (c i) -> p c j i", i=4)
-            cut = WR_VECTOR_C[n] // 4
-            if cut > 0:
-                nc.vector.tensor_copy(dst[:, :cut], src[:, :cut])
-            if cut < width // 4:
-                nc.scalar.copy(dst[:, cut:], src[:, cut:])
-            code, scale = quantise(grouped, width, f"wr_{n}")
+        def quantise_wr(n):
+            a, c0, width = WR_PIECES[n]
+            code, scale = quantise(wr_bf[n], width, f"wr_{n}")
             for c in range(0, width, P):
                 wr_q[a, (c0 + c) // P] = (code[:, c : c + P], scale[:, c : c + P])
 
-        for n in range(K // P):
-            acc = bank((0, 1, 4, 5, 2, 3, 6, 7)[n])
-            for a, j0, width in ((0, 0, S), (1, 0, S // 2), (1, S // 2, S // 2)):
-                nc.tensor.matmul_mx(
-                    acc[:, j0 : j0 + width],
-                    lhsT=w3_code[a][:, n * P : (n + 1) * P].bitcast(E4M3),
-                    lhsT_scale=w3_scale[4 * a :, n * P : (n + 1) * P],
-                    rhs=h_q[a][0][:, j0 : j0 + width].bitcast(E4M3),
-                    rhs_scale=h_q[a][1][:, j0 : j0 + width],
-                    start=a == 0,
-                    stop=False,
-                )
-            for a in range(PASSES):
-                code, scale = wr_q[a, n]
-                times_v(acc[:], code.bitcast(E4M3), scale, a, 0, S, False, a == PASSES - 1)
-            result = sb([P, S], F32, f"result{n}")
-            if n % 2 == 0 or n < 4:
-                nc.scalar.copy(result[:], acc[:])
+        def out_passes(n, passes):
+            for kind, a, j0, width in passes:
+                if n not in total:
+                    total[n] = bank(OUT_BANKS[n])
+                    done[n] = 0
+                start = done[n] == 0
+                done[n] = done[n] + width
+                stop = done[n] == 2 * PASSES * S
+                if kind == "wr":
+                    code, scale = wr_q[a, n]
+                    times_v(total[n][:, j0 : j0 + width], code.bitcast(E4M3), scale, a, j0, width, start, stop)
+                else:
+                    nc.tensor.matmul_mx(
+                        total[n][:, j0 : j0 + width],
+                        lhsT=w3_code[a, n // 4][:, n % 4 * P : (n % 4 + 1) * P].bitcast(E4M3),
+                        lhsT_scale=w3_scale[4 * a :, n * P : (n + 1) * P],
+                        rhs=h_q[a, j0 // H_PART[a]][0][:, j0 % H_PART[a] : j0 % H_PART[a] + width].bitcast(E4M3),
+                        rhs_scale=h_q[a, j0 // H_PART[a]][1][:, j0 % H_PART[a] : j0 % H_PART[a] + width],
+                        start=start,
+                        stop=stop,
+                    )
+
+        def store(n):
+            if n % 4 == 0:
+                results[n // 4] = sb([P, 4, S], F32, f"result{n // 4}")
+            result = results[n // 4][:, n % 4, :]
+            if n in OUT_ON_VECTOR:
+                nc.vector.tensor_copy(result, total[n][:])
             else:
-                nc.vector.tensor_copy(result[:], acc[:])
-            nc.sync.dma_start(out[n * P : (n + 1) * P, :], result[:])
+                nc.scalar.copy(result, total[n][:])
+            nc.sync.dma_start(out[n * P : (n + 1) * P, :], result)
+
+        tab, w1_raw, w1_code, w1_scale, v_code, gate, up = {}, {}, {}, {}, {}, {}, {}
+        w2_raw, w2_bf, w2_q, wr_raw, wr_bf, wr_q, w3_code = {}, {}, {}, {}, {}, {}, {}
+        h_bf, h_q, total, done, results, pre = {}, {}, {}, {}, {}, {}
+
+        offsets = keep.tile([P, S // 16], U16, name="offsets")
+        nc.sync.dma_start(offsets[:], offs)
+        tab_rows = [zeroed(T, f"tab_rows{a}") for a in range(PASSES)]
+        w1_rows = zeroed(PASSES * H, "w1_rows")
+        v_scale = zeroed(PASSES * S, "v_scale")
+        w3_scale = zeroed(K, "w3_scale")
+        load_w1(0)
+        for a in range(PASSES):
+            nc.sync.dma_start(tab_rows[a][:].bitcast(I32)[0:P:8, :], tab_scales[a].bitcast(I32))
+        picked_rows = sb([P, PASSES * S], U8, "picked_rows")
+        for a in range(PASSES):
+            nc.vector.tensor_copy(picked_rows[:, a * S : (a + 1) * S], tab_rows[a][:].indirect(offsets[:]))
+        bias = sb([P, H // KP, PACK], F32, "bias")
+
+        def load_bias():
+            nc.sync.dma_start(bias[:], b1.rearrange("(b p t) -> p b t", p=P, t=PACK))
+
+        load_tab(0)
+        load_w1_scales()
+        load_w1(1)
+        load_tab(1)
+        load_bias()
+        move_scales()
+        load_w2(0, 0)
+        load_w3_scales()
+        load_w2(0, 1)
+        load_w2(1, 0)
+        load_w2(1, 1)
+        load_w3(0, 0)
+        load_wr(0)
+        load_wr(1)
+        load_w3(0, 1)
+        load_w3(1, 0)
+        load_w3(1, 1)
+        for n in range(2, 5):
+            load_wr(n)
+        for a in range(2):
+            order_w1_code(a)
+            order_w1_scale(a)
+            gather_words(a)
+        for a in range(2):
+            for n in range(6):
+                first_pass(n // 4, n % 4, a, n)
+        for a in range(2):
+            round_w2(0, a)
+            quantise_w2(0, a)
+        second_product(0, (0, 1, 2, 3))
+        round_w2(1, 0)
+        for jq in range(4):
+            gate_quarter(0, jq)
+        for t in (2, 3):
+            for a in range(2):
+                first_pass(1, t, a, t - 2)
+        quantise_w2(1, 0)
+        quantise_h(0, 0, 512)
+        round_w2(1, 1)
+        quantise_w2(1, 1)
+        second_product(1, (6, 7, 2, 3))
+        round_wr(0)
+        gate_quarter(1, 0)
+        quantise_wr(0)
+        gate_quarter(1, 1)
+        quantise_h(1, 0, 128)
+        gate_quarter(1, 2)
+        quantise_h(1, 128, 128)
+        gate_quarter(1, 3)
+        round_wr(1)
+        quantise_wr(1)
+        quantise_h(1, 256, 256)
+        round_wr(2)
+        round_wr(3)
+        quantise_wr(3)
+        quantise_wr(2)
+        round_wr(4)
+        quantise_wr(4)
+        for n in range(4):
+            out_passes(n, [("w3", 0, 0, 512)])
+        for n in range(4):
+            out_passes(n, [("wr", 0, 0, 512)])
+        for n in range(4):
+            out_passes(n, [("w3", 1, 0, 256)])
+        for n in range(4, 8):
+            out_passes(n, [("w3", 0, 0, 512), ("w3", 1, 0, 256)])
+        for n in range(4):
+            out_passes(n, [("wr", 1, 0, 512), ("w3", 1, 256, 256)])
+            store(n)
+        for n in range(4, 8):
+            out_passes(n, [("w3", 1, 256, 256), ("wr", 0, 0, 512), ("wr", 1, 0, 512)])
+            store(n)

@@ -21,13 +21,13 @@ PACK = 4
 KP = P * PACK
 PASSES = K // KP
 JQ = 128
-REUSES = {"h_bf11":"wr_bf0","h_11_code":"wr_bf1"}
+REUSES = {}
 WR_PIECES = [(0, 0, 512), (1, 0, 512), (0, 512, 512), (1, 512, 256), (1, 768, 256)]
-WR_VECTOR_C = (0,0,128,256,256)
-W2_VECTOR_M = (128,128,0,64)
-H_SPLIT = (4, 1)
+WR_VECTOR_C = (0,192,384,256,256)
+W2_VECTOR_M = (128,128,80,64)
+H_SPLIT = (4, 4)
 H_PART = (512, 256)
-OUT_BANKS = (4,5,0,1,6,7,2,3)
+OUT_BANKS = (0,1,2,3,4,5,6,7)
 OUT_ON_VECTOR = (5,7)
 
 
@@ -65,14 +65,30 @@ def tile_list_ast_slot_block_kernel(
             return raw
 
         def load_w2(b, a):
-            w2_raw[b, a] = load_rows(w2, a, b * KP, KP, f"w2_raw{b}{a}")
+            w2_raw[b, a] = load_rows(w2, a, b * KP, KP, f"w2_raw{b}{a}")[:]
+
+        def load_w2_pass(a):
+            raw = load_rows(w2, a, 0, H, f"w2_raw{a}")
+            for b in range(H // KP):
+                w2_raw[b, a] = raw[:, :, b * KP : (b + 1) * KP]
 
         def load_wr(n):
-            wr_raw[n] = load_rows(wr, *WR_PIECES[n], f"wr_raw{n}")
+            wr_raw[n] = load_rows(wr, *WR_PIECES[n], f"wr_raw{n}")[:]
+
+        def load_wr_pass(a):
+            raw = load_rows(wr, a, 0, K, f"wr_pass{a}")
+            for n, (a2, c0, width) in enumerate(WR_PIECES):
+                if a2 == a:
+                    wr_raw[n] = raw[:, :, c0 : c0 + width]
+
+        def load_w3_pass(a):
+            code = load_e4m3(w3_words, a, f"w3_code{a}")
+            for half in range(2):
+                w3_code[a, half] = code[:, half * KP : (half + 1) * KP]
 
         def load_w3(a, half):
             words = w3_words[a][:, half * KP : (half + 1) * KP, :].rearrange("p c i -> p (c i)")
-            w3_code[a, half] = load_words(words, U32, KP, f"w3_code{a}{half}")
+            w3_code[a, half] = load_words(words, U32, KP, f"w3_code{a}{half}")[:]
 
         def load_tab(a):
             tab[a] = load_e4m3(tab_words, a, f"tab{a}")
@@ -90,7 +106,7 @@ def tile_list_ast_slot_block_kernel(
         def load_w3_scales():
             for d in range(4):
                 nc.sync.dma_start(
-                    w3_scale[:].bitcast(I32)[32 * d : 32 * d + 8, :],
+                    w3_scale[:].bitcast(I32)[32 * d + 4 : 32 * d + 12, :],
                     w3_scales.bitcast(I32)[:, 4 * d : 4 * d + 4, :],
                 )
 
@@ -150,7 +166,7 @@ def tile_list_ast_slot_block_kernel(
             w2_bf[b, a] = sb([P, KP * PACK], BF16, f"w2_bf{b}{a}")
             round_split(
                 w2_bf[b, a][:].rearrange("p (t m j) -> p m j t", t=PACK, j=PACK),
-                w2_raw[b, a][:].rearrange("p j (m t) -> p m j t", t=PACK),
+                w2_raw[b, a].rearrange("p j (m t) -> p m j t", t=PACK),
                 W2_VECTOR_M[b * PASSES + a],
             )
 
@@ -203,7 +219,7 @@ def tile_list_ast_slot_block_kernel(
             wr_bf[n] = sb([P, width * PACK], BF16, f"wr_bf{n}")
             round_split(
                 wr_bf[n][:].rearrange("p (c i j) -> p c j i", i=4, j=PACK),
-                wr_raw[n][:].rearrange("p j (c i) -> p c j i", i=4),
+                wr_raw[n].rearrange("p j (c i) -> p c j i", i=4),
                 WR_VECTOR_C[n] // 4,
             )
 
@@ -228,7 +244,7 @@ def tile_list_ast_slot_block_kernel(
                     nc.tensor.matmul_mx(
                         total[n][:, j0 : j0 + width],
                         lhsT=w3_code[a, n // 4][:, n % 4 * P : (n % 4 + 1) * P].bitcast(E4M3),
-                        lhsT_scale=w3_scale[4 * a :, n * P : (n + 1) * P],
+                        lhsT_scale=w3_scale[4 * a + 4 :, n * P : (n + 1) * P],
                         rhs=h_q[a, j0 // H_PART[a]][0][:, j0 % H_PART[a] : j0 % H_PART[a] + width].bitcast(E4M3),
                         rhs_scale=h_q[a, j0 // H_PART[a]][1][:, j0 % H_PART[a] : j0 % H_PART[a] + width],
                         start=start,
@@ -277,8 +293,8 @@ def tile_list_ast_slot_block_kernel(
         load_w2(0, 1)
         load_w2(1, 0)
         load_w2(1, 1)
-        load_w3(0, 0)
         load_wr(0)
+        load_w3(0, 0)
         load_wr(1)
         load_w3(0, 1)
         load_w3(1, 0)
@@ -290,46 +306,44 @@ def tile_list_ast_slot_block_kernel(
             order_w1_scale(a)
             gather_words(a)
         for a in range(2):
-            for n in range(6):
-                first_pass(n // 4, n % 4, a, n)
+            for t in range(4):
+                first_pass(0, t, a, t)
+        for t in range(4):
+            for a in range(2):
+                first_pass(1, t, a, 4 + t)
         for a in range(2):
             round_w2(0, a)
             quantise_w2(0, a)
         second_product(0, (0, 1, 2, 3))
         round_w2(1, 0)
-        for jq in range(4):
-            gate_quarter(0, jq)
-        for t in (2, 3):
-            for a in range(2):
-                first_pass(1, t, a, t - 2)
+        gate_quarter(0, 0)
+        gate_quarter(0, 1)
         quantise_w2(1, 0)
-        quantise_h(0, 0, 512)
+        gate_quarter(0, 2)
+        gate_quarter(0, 3)
         round_w2(1, 1)
         quantise_w2(1, 1)
-        second_product(1, (6, 7, 2, 3))
+        quantise_h(0, 0, 512)
+        second_product(1, (4, 5, 6, 7))
         round_wr(0)
         gate_quarter(1, 0)
-        quantise_wr(0)
         gate_quarter(1, 1)
-        quantise_h(1, 0, 128)
         gate_quarter(1, 2)
-        quantise_h(1, 128, 128)
+        quantise_h(1, 0, 256)
+        quantise_wr(0)
         gate_quarter(1, 3)
         round_wr(1)
         quantise_wr(1)
         quantise_h(1, 256, 256)
-        round_wr(2)
-        round_wr(3)
-        quantise_wr(3)
-        quantise_wr(2)
-        round_wr(4)
-        quantise_wr(4)
+        for n in range(2, 5):
+            round_wr(n)
+            quantise_wr(n)
         for n in range(4):
             out_passes(n, [("w3", 0, 0, 512)])
         for n in range(4):
-            out_passes(n, [("wr", 0, 0, 512)])
-        for n in range(4):
             out_passes(n, [("w3", 1, 0, 256)])
+        for n in range(4):
+            out_passes(n, [("wr", 0, 0, 512)])
         for n in range(4, 8):
             out_passes(n, [("w3", 0, 0, 512), ("w3", 1, 0, 256)])
         for n in range(4):

@@ -20,15 +20,18 @@ P = 128
 PACK = 4
 KP = P * PACK
 PASSES = K // KP
-JQ = 128
-REUSES = {}
-WR_PIECES = [(0, 0, 512), (1, 0, 512), (0, 512, 512), (1, 512, 256), (1, 768, 256)]
-WR_VECTOR_C = (0,192,384,256,256)
-W2_VECTOR_M = (128,128,80,64)
-H_SPLIT = (4, 4)
-H_PART = (512, 256)
-OUT_BANKS = (0,1,2,3,4,5,6,7)
-OUT_ON_VECTOR = (5,7)
+QUADS = 4
+QUAD = P // QUADS
+LINE = 4
+TOKENS = S // PACK
+HALF = S // 2
+TILES = K // P
+FIRST_TILES = range(TILES // 2)
+LAST_TILES = range(TILES // 2, TILES)
+
+WR_PIECES = [(0, 0, 512), (1, 0, 512), (0, 512, 256), (1, 512, 256), (0, 768, 256), (1, 768, 256)]
+WR_ON_SCALAR = 2
+W2_SHARED_M = 32
 
 
 def tile_list_ast_slot_block_kernel(
@@ -39,19 +42,19 @@ def tile_list_ast_slot_block_kernel(
         keep = ctx.enter_context(tc.tile_pool(name="keep", bufs=1))
         psum = ctx.enter_context(tc.psum_pool(name="psum", bufs=1))
 
-        def sb(shape, dtype, name):
-            return keep.tile(shape, dtype, name=name, tag=REUSES.get(name, name), align_bytes=64)
+        def sbuf(shape, dtype, name, reuse=None):
+            return keep.tile(shape, dtype, name=name, tag=reuse or name, align_bytes=64)
 
         def bank(n):
             return psum.tile([P, S], F32, name=f"bank{n}")
 
         def zeroed(width, name):
-            tile = sb([P, width], U8, name)
+            tile = sbuf([P, width], U8, name)
             nc.vector.memset(tile[:].bitcast(I32), 0)
             return tile
 
         def load_words(words, dtype, width, name):
-            tile = sb([P, width], dtype, name)
+            tile = sbuf([P, width], dtype, name)
             nc.sync.dma_start(tile[:].bitcast(I32), words.bitcast(I32))
             return tile
 
@@ -59,80 +62,67 @@ def tile_list_ast_slot_block_kernel(
             return load_words(words[a].rearrange("p c i -> p (c i)"), U32, words.shape[2], name)
 
         def load_rows(w, a, c0, width, name):
-            raw = sb([P, PACK, width], F32, name)
+            raw = sbuf([P, PACK, width], F32, name)
             rows = w[a * KP : (a + 1) * KP, c0 : c0 + width]
             nc.sync.dma_start(raw[:], rows.rearrange("(p j) c -> p j c", j=PACK))
             return raw
 
-        def load_w2(b, a):
-            w2_raw[b, a] = load_rows(w2, a, b * KP, KP, f"w2_raw{b}{a}")[:]
+        offsets = keep.tile([P, S // 16], U16, name="offsets")
+        nc.sync.dma_start(offsets[:], offs)
+        tab_rows = [zeroed(T, f"tab_rows{a}") for a in range(PASSES)]
+        w1_rows = zeroed(PASSES * H, "w1_rows")
+        v_scale = zeroed(PASSES * S, "v_scale")
+        w3_scale = zeroed(K, "w3_scale")
+        w1_raw = [load_words(w1_words[0], U16, H, "w1_raw0")]
+        for a in range(PASSES):
+            nc.sync.dma_start(tab_rows[a][:].bitcast(I32)[0:P:8, :], tab_scales[a].bitcast(I32))
+        picked_rows = sbuf([P, PASSES * S], U8, "picked_rows")
+        for a in range(PASSES):
+            nc.vector.tensor_copy(picked_rows[:, a * S : (a + 1) * S], tab_rows[a][:].indirect(offsets[:]))
+        bias = sbuf([P, H // KP, PACK], F32, "bias")
 
-        def load_w2_pass(a):
-            raw = load_rows(w2, a, 0, H, f"w2_raw{a}")
-            for b in range(H // KP):
-                w2_raw[b, a] = raw[:, :, b * KP : (b + 1) * KP]
+        tab = [load_e4m3(tab_words, 0, "tab0")]
+        for r in range(QUADS):
+            nc.sync.dma_start(
+                w1_rows[:].bitcast(I32).rearrange("p (a c) -> p a c", a=PASSES)[r:P:QUAD],
+                w1_scales.bitcast(I32).rearrange("a (d r) c -> r d a c", d=QUADS)[r],
+            )
+        w1_raw.append(load_words(w1_words[1], U16, H, "w1_raw1"))
+        tab.append(load_e4m3(tab_words, 1, "tab1"))
+        nc.sync.dma_start(bias[:], b1.rearrange("(b p t) -> p b t", p=P, t=PACK))
+        for d in range(QUADS):
+            nc.sync.dma_start(
+                v_scale[:].bitcast(I32)[QUAD * d : QUAD * d + 4, :],
+                picked_rows[:].bitcast(I32)[QUAD * d : QUAD * (d + 1) : 8, :],
+            )
+        w2_first = load_rows(w2, 0, 0, H, "w2_raw0")
+        w2_raw = {(b, 0): w2_first[:, :, b * KP : (b + 1) * KP] for b in range(H // KP)}
+        for b in range(H // KP):
+            w2_raw[b, 1] = load_rows(w2, 1, b * KP, KP, f"w2_raw{b}1")[:]
+        for d in range(QUADS):
+            nc.sync.dma_start(
+                w3_scale[:].bitcast(I32)[QUAD * d + 4 : QUAD * d + 12, :],
+                w3_scales.bitcast(I32)[:, 4 * d : 4 * d + 4, :],
+            )
+        wr_raw, w3_code = [], []
+        for n, (a, c0, width) in enumerate(WR_PIECES):
+            wr_raw.append(load_rows(wr, a, c0, width, f"wr_raw{n}"))
+            if n < PASSES:
+                w3_code.append(load_e4m3(w3_words, n, f"w3_code{n}"))
 
-        def load_wr(n):
-            wr_raw[n] = load_rows(wr, *WR_PIECES[n], f"wr_raw{n}")[:]
-
-        def load_wr_pass(a):
-            raw = load_rows(wr, a, 0, K, f"wr_pass{a}")
-            for n, (a2, c0, width) in enumerate(WR_PIECES):
-                if a2 == a:
-                    wr_raw[n] = raw[:, :, c0 : c0 + width]
-
-        def load_w3_pass(a):
-            code = load_e4m3(w3_words, a, f"w3_code{a}")
-            for half in range(2):
-                w3_code[a, half] = code[:, half * KP : (half + 1) * KP]
-
-        def load_w3(a, half):
-            words = w3_words[a][:, half * KP : (half + 1) * KP, :].rearrange("p c i -> p (c i)")
-            w3_code[a, half] = load_words(words, U32, KP, f"w3_code{a}{half}")[:]
-
-        def load_tab(a):
-            tab[a] = load_e4m3(tab_words, a, f"tab{a}")
-
-        def load_w1(a):
-            w1_raw[a] = load_words(w1_words[a], U16, H, f"w1_raw{a}")
-
-        def load_w1_scales():
-            for r in range(4):
-                nc.sync.dma_start(
-                    w1_rows[:].bitcast(I32).rearrange("p (a c) -> p a c", a=PASSES)[r:P:32],
-                    w1_scales.bitcast(I32).rearrange("a (d r) c -> r d a c", r=4)[r],
-                )
-
-        def load_w3_scales():
-            for d in range(4):
-                nc.sync.dma_start(
-                    w3_scale[:].bitcast(I32)[32 * d + 4 : 32 * d + 12, :],
-                    w3_scales.bitcast(I32)[:, 4 * d : 4 * d + 4, :],
-                )
-
-        def move_scales():
-            for d in range(4):
-                nc.sync.dma_start(
-                    v_scale[:].bitcast(I32)[32 * d : 32 * d + 4, :],
-                    picked_rows[:].bitcast(I32)[32 * d : 32 * d + 32 : 8, :],
-                )
-
-        def order_w1(src, dtype, name):
-            dst = sb([P, H], dtype, name)
+        def order_w1(src, dtype, name, reuse=None):
+            dst = sbuf([P, H], dtype, name, reuse)
             nc.vector.tensor_copy(
                 dst[:].rearrange("p (b t m) -> p b m t", t=PACK, m=P),
                 src.rearrange("p (b m t) -> p b m t", t=PACK, m=P),
             )
             return dst
 
-        def order_w1_code(a):
-            w1_code[a] = order_w1(w1_raw[a][:], U16, f"w1_code{a}")
-
-        def order_w1_scale(a):
-            w1_scale[a] = order_w1(w1_rows[:, a * H : (a + 1) * H], U8, f"w1_scale{a}")
-
-        def gather_words(a):
-            v_code[a] = sb([P, S], U32, f"v_code{a}")
+        w1_code, w1_scale, v_code = [], [], []
+        for a in range(PASSES):
+            w1_code.append(order_w1(w1_raw[a][:], U16, f"w1_code{a}", "tab_rows1" if a == 0 else None))
+            w1_scale.append(order_w1(w1_rows[:, a * H : (a + 1) * H], U8, f"w1_scale{a}"))
+            v_code.append(sbuf([P, S], U32, f"v_code{a}"))
             nc.vector.tensor_copy(v_code[a][:], tab[a][:].indirect(offsets[:]))
 
         def times_v(acc, code, scale, a, j0, width, start, stop):
@@ -146,209 +136,165 @@ def tile_list_ast_slot_block_kernel(
                 stop=stop,
             )
 
-        def first_pass(b, t, a, n):
+        pre, gate = {}, {}
+
+        def first_pass(b, t, a):
             if a == 0:
-                pre[b, t] = bank(n)
+                pre[b, t] = bank(PACK * b + t)
             cols = slice(b * KP + t * P, b * KP + (t + 1) * P)
-            times_v(pre[b, t][:], w1_code[a][:, cols].bitcast(E2M1), w1_scale[a][:, cols], a, 0, S, a == 0, a == PASSES - 1)
-            if a == PASSES - 1:
+            last = a == PASSES - 1
+            times_v(pre[b, t][:], w1_code[a][:, cols].bitcast(E2M1), w1_scale[a][:, cols], a, 0, S, a == 0, last)
+            if last:
                 if t == 0:
-                    gate[b] = sb([P, PACK, S], F32, f"gate{b}")
+                    gate[b] = sbuf([P, PACK, S], F32, f"gate{b}")
                 nc.scalar.activation(gate[b][:, t, :], pre[b, t][:], GELU, bias=bias[:, b, t : t + 1])
 
-        def round_split(dst, src, cut):
-            if cut > 0:
-                nc.vector.tensor_copy(dst[:, :cut], src[:, :cut])
-            if cut < dst.shape[1]:
-                nc.scalar.copy(dst[:, cut:], src[:, cut:])
+        for a in range(PASSES):
+            for t in range(PACK):
+                first_pass(0, t, a)
+        for t in range(PACK):
+            for a in range(PASSES):
+                first_pass(1, t, a)
 
-        def round_w2(b, a):
-            w2_bf[b, a] = sb([P, KP * PACK], BF16, f"w2_bf{b}{a}")
-            round_split(
-                w2_bf[b, a][:].rearrange("p (t m j) -> p m j t", t=PACK, j=PACK),
-                w2_raw[b, a].rearrange("p j (m t) -> p m j t", t=PACK),
-                W2_VECTOR_M[b * PASSES + a],
-            )
-
-        def quantise(grouped, width, name):
-            code = sb([P, width], U32, name + "_code")
-            scale = sb([P, width], U8, name + "_scale")
-            nc.vector.quantize_mx(code[:].bitcast(E4M3), scale[:], grouped[:])
+        def quantise(grouped, width, name, reuse=None):
+            code = sbuf([P, width], U32, name + "_code", reuse)
+            scale = sbuf([P, width], U8, name + "_scale")
+            nc.vector.quantize_mx(code[:].bitcast(E4M3), scale[:], grouped)
             return code, scale
 
-        def quantise_w2(b, a):
-            w2_q[b, a] = quantise(w2_bf[b, a], KP, f"w2_{b}{a}")
+        def round_w2(b, a, on_vector):
+            grouped = sbuf([P, KP * PACK], BF16, f"w2_bf{b}{a}")
+            dst = grouped[:].rearrange("p (t m j) -> p m j t", t=PACK, j=PACK)
+            src = w2_raw[b, a].rearrange("p j (m t) -> p m j t", t=PACK)
+            if on_vector > 0:
+                nc.vector.tensor_copy(dst[:, :on_vector], src[:, :on_vector])
+            if on_vector < P:
+                nc.scalar.copy(dst[:, on_vector:], src[:, on_vector:])
+            return grouped
 
-        def second_product(b, banks):
-            up[b] = [bank(n) for n in banks]
-            for jq in range(S // JQ):
+        w2_q, up, h_bf = {}, {}, {}
+
+        def second_product(b):
+            up[b] = [bank(PACK * b + u) for u in range(S // TOKENS)]
+            for u in range(S // TOKENS):
                 for a in range(PASSES):
                     code, scale = w2_q[b, a]
                     for t in range(PACK):
                         times_v(
-                            up[b][jq][:, t * JQ : (t + 1) * JQ],
-                            code[:, t * P : (t + 1) * P].bitcast(E4M3), scale[:, t * P : (t + 1) * P],
-                            a, jq * JQ, JQ, a == 0 and t == 0, a == PASSES - 1 and t == PACK - 1,
+                            up[b][u][:, t * TOKENS : (t + 1) * TOKENS],
+                            code[:, t * P : (t + 1) * P].bitcast(E4M3),
+                            scale[:, t * P : (t + 1) * P],
+                            a,
+                            u * TOKENS,
+                            TOKENS,
+                            a == 0 and t == 0,
+                            a == PASSES - 1 and t == PACK - 1,
                         )
 
-        def gate_quarter(b, jq):
-            cut = H_SPLIT[b]
-            if jq in (0, cut):
-                h_bf[b, jq] = sb([P, (cut if jq == 0 else 4 - cut) * JQ * PACK], BF16, f"h_bf{b}{jq}")
-            first = 0 if jq < cut else cut
+        def gate_times_up(b, u):
+            if u == 0:
+                h_bf[b] = sbuf([P, S * PACK], BF16, f"h_bf{b}0")
+            tokens = slice(u * TOKENS, (u + 1) * TOKENS)
             nc.vector.tensor_tensor(
-                h_bf[b, first][:, (jq - first) * JQ * PACK : (jq - first + 1) * JQ * PACK].rearrange("p (c i t) -> p c t i", i=4, t=PACK),
-                up[b][jq][:].rearrange("p (t c i) -> p c t i", t=PACK, i=4),
-                gate[b][:, :, jq * JQ : (jq + 1) * JQ].rearrange("p t (c i) -> p c t i", i=4),
+                h_bf[b][:, tokens.start * PACK : tokens.stop * PACK].rearrange("p (c i t) -> p c t i", i=LINE, t=PACK),
+                up[b][u][:].rearrange("p (t c i) -> p c t i", t=PACK, i=LINE),
+                gate[b][:, :, tokens].rearrange("p t (c i) -> p c t i", i=LINE),
                 MULT,
             )
 
-        def quantise_h(b, j0, width):
-            part = H_PART[b]
-            if j0 % part == 0:
-                h_q[b, j0 // part] = sb([P, part], U32, f"h_{b}{j0 // part}_code"), sb([P, part], U8, f"h_{b}{j0 // part}_scale")
-            code, scale = h_q[b, j0 // part]
-            first = 0 if j0 < H_SPLIT[b] * JQ else H_SPLIT[b]
-            nc.vector.quantize_mx(
-                code[:, j0 % part : j0 % part + width].bitcast(E4M3), scale[:, j0 % part : j0 % part + width],
-                h_bf[b, first][:, (j0 - first * JQ) * PACK : (j0 - first * JQ + width) * PACK],
-            )
+        for a in range(PASSES):
+            w2_q[0, a] = quantise(round_w2(0, a, P)[:], KP, f"w2_0{a}")
+        second_product(0)
+        w2_q[1, 0] = quantise(round_w2(1, 0, W2_SHARED_M)[:], KP, "w2_10", "w2_bf01")
+        gate_times_up(0, 0)
+        gate_times_up(0, 1)
+        w2_q[1, 1] = quantise(round_w2(1, 1, 0)[:], KP, "w2_11")
+        gate_times_up(0, 2)
+        gate_times_up(0, 3)
+        h_q = {(0, 0): quantise(h_bf[0][:], S, "h_00")}
+        second_product(1)
+
+        wr_bf, wr_q = {}, {}
 
         def round_wr(n):
-            width = WR_PIECES[n][2]
-            wr_bf[n] = sb([P, width * PACK], BF16, f"wr_bf{n}")
-            round_split(
-                wr_bf[n][:].rearrange("p (c i j) -> p c j i", i=4, j=PACK),
-                wr_raw[n].rearrange("p j (c i) -> p c j i", i=4),
-                WR_VECTOR_C[n] // 4,
-            )
+            wr_bf[n] = sbuf([P, WR_PIECES[n][2] * PACK], BF16, f"wr_bf{n}")
+            dst = wr_bf[n][:].rearrange("p (c i j) -> p c j i", i=LINE, j=PACK)
+            src = wr_raw[n][:].rearrange("p j (c i) -> p c j i", i=LINE)
+            if n < WR_ON_SCALAR:
+                nc.scalar.copy(dst, src)
+            else:
+                nc.vector.tensor_copy(dst, src)
 
         def quantise_wr(n):
             a, c0, width = WR_PIECES[n]
-            code, scale = quantise(wr_bf[n], width, f"wr_{n}")
+            code, scale = quantise(wr_bf[n][:], width, f"wr_{n}")
             for c in range(0, width, P):
                 wr_q[a, (c0 + c) // P] = (code[:, c : c + P], scale[:, c : c + P])
 
-        def out_passes(n, passes):
-            for kind, a, j0, width in passes:
-                if n not in total:
-                    total[n] = bank(OUT_BANKS[n])
-                    done[n] = 0
-                start = done[n] == 0
-                done[n] = done[n] + width
-                stop = done[n] == 2 * PASSES * S
-                if kind == "wr":
-                    code, scale = wr_q[a, n]
-                    times_v(total[n][:, j0 : j0 + width], code.bitcast(E4M3), scale, a, j0, width, start, stop)
-                else:
-                    nc.tensor.matmul_mx(
-                        total[n][:, j0 : j0 + width],
-                        lhsT=w3_code[a, n // 4][:, n % 4 * P : (n % 4 + 1) * P].bitcast(E4M3),
-                        lhsT_scale=w3_scale[4 * a + 4 :, n * P : (n + 1) * P],
-                        rhs=h_q[a, j0 // H_PART[a]][0][:, j0 % H_PART[a] : j0 % H_PART[a] + width].bitcast(E4M3),
-                        rhs_scale=h_q[a, j0 // H_PART[a]][1][:, j0 % H_PART[a] : j0 % H_PART[a] + width],
-                        start=start,
-                        stop=stop,
-                    )
+        def quantise_h_half(half):
+            j0 = half * HALF
+            h_q[1, j0] = quantise(h_bf[1][:, j0 * PACK : (j0 + HALF) * PACK], HALF, f"h_1{half}")
+
+        round_wr(0)
+        for u in range(3):
+            gate_times_up(1, u)
+        quantise_h_half(0)
+        quantise_wr(0)
+        gate_times_up(1, 3)
+        round_wr(1)
+        quantise_wr(1)
+        quantise_h_half(1)
+        for n in range(WR_ON_SCALAR, len(WR_PIECES)):
+            round_wr(n)
+            quantise_wr(n)
+
+        total, results = {}, {}
+
+        def w3_pass(n, a, j0, start=False, stop=False):
+            code, scale = h_q[a, j0]
+            width = S if a == 0 else HALF
+            if start:
+                total[n] = bank(n)
+            nc.tensor.matmul_mx(
+                total[n][:, j0 : j0 + width],
+                lhsT=w3_code[a][:, n * P : (n + 1) * P].bitcast(E4M3),
+                lhsT_scale=w3_scale[4 * (a + 1) :, n * P : (n + 1) * P],
+                rhs=code[:].bitcast(E4M3),
+                rhs_scale=scale[:],
+                start=start,
+                stop=stop,
+            )
+
+        def wr_pass(n, a, stop=False):
+            code, scale = wr_q[a, n]
+            times_v(total[n][:], code.bitcast(E4M3), scale, a, 0, S, False, stop)
 
         def store(n):
-            if n % 4 == 0:
-                results[n // 4] = sb([P, 4, S], F32, f"result{n // 4}")
-            result = results[n // 4][:, n % 4, :]
-            if n in OUT_ON_VECTOR:
+            group, place = divmod(n, len(FIRST_TILES))
+            if place == 0:
+                results[group] = sbuf([P, len(FIRST_TILES), S], F32, f"result{group}")
+            result = results[group][:, place, :]
+            if n == TILES - 1:
                 nc.vector.tensor_copy(result, total[n][:])
             else:
                 nc.scalar.copy(result, total[n][:])
             nc.sync.dma_start(out[n * P : (n + 1) * P, :], result)
 
-        tab, w1_raw, w1_code, w1_scale, v_code, gate, up = {}, {}, {}, {}, {}, {}, {}
-        w2_raw, w2_bf, w2_q, wr_raw, wr_bf, wr_q, w3_code = {}, {}, {}, {}, {}, {}, {}
-        h_bf, h_q, total, done, results, pre = {}, {}, {}, {}, {}, {}
-
-        offsets = keep.tile([P, S // 16], U16, name="offsets")
-        nc.sync.dma_start(offsets[:], offs)
-        tab_rows = [zeroed(T, f"tab_rows{a}") for a in range(PASSES)]
-        w1_rows = zeroed(PASSES * H, "w1_rows")
-        v_scale = zeroed(PASSES * S, "v_scale")
-        w3_scale = zeroed(K, "w3_scale")
-        load_w1(0)
-        for a in range(PASSES):
-            nc.sync.dma_start(tab_rows[a][:].bitcast(I32)[0:P:8, :], tab_scales[a].bitcast(I32))
-        picked_rows = sb([P, PASSES * S], U8, "picked_rows")
-        for a in range(PASSES):
-            nc.vector.tensor_copy(picked_rows[:, a * S : (a + 1) * S], tab_rows[a][:].indirect(offsets[:]))
-        bias = sb([P, H // KP, PACK], F32, "bias")
-
-        def load_bias():
-            nc.sync.dma_start(bias[:], b1.rearrange("(b p t) -> p b t", p=P, t=PACK))
-
-        load_tab(0)
-        load_w1_scales()
-        load_w1(1)
-        load_tab(1)
-        load_bias()
-        move_scales()
-        load_w2(0, 0)
-        load_w3_scales()
-        load_w2(0, 1)
-        load_w2(1, 0)
-        load_w2(1, 1)
-        load_wr(0)
-        load_w3(0, 0)
-        load_wr(1)
-        load_w3(0, 1)
-        load_w3(1, 0)
-        load_w3(1, 1)
-        for n in range(2, 5):
-            load_wr(n)
-        for a in range(2):
-            order_w1_code(a)
-            order_w1_scale(a)
-            gather_words(a)
-        for a in range(2):
-            for t in range(4):
-                first_pass(0, t, a, t)
-        for t in range(4):
-            for a in range(2):
-                first_pass(1, t, a, 4 + t)
-        for a in range(2):
-            round_w2(0, a)
-            quantise_w2(0, a)
-        second_product(0, (0, 1, 2, 3))
-        round_w2(1, 0)
-        gate_quarter(0, 0)
-        gate_quarter(0, 1)
-        quantise_w2(1, 0)
-        gate_quarter(0, 2)
-        gate_quarter(0, 3)
-        round_w2(1, 1)
-        quantise_w2(1, 1)
-        quantise_h(0, 0, 512)
-        second_product(1, (4, 5, 6, 7))
-        round_wr(0)
-        gate_quarter(1, 0)
-        gate_quarter(1, 1)
-        gate_quarter(1, 2)
-        quantise_h(1, 0, 256)
-        quantise_wr(0)
-        gate_quarter(1, 3)
-        round_wr(1)
-        quantise_wr(1)
-        quantise_h(1, 256, 256)
-        for n in range(2, 5):
-            round_wr(n)
-            quantise_wr(n)
-        for n in range(4):
-            out_passes(n, [("w3", 0, 0, 512)])
-        for n in range(4):
-            out_passes(n, [("w3", 1, 0, 256)])
-        for n in range(4):
-            out_passes(n, [("wr", 0, 0, 512)])
-        for n in range(4, 8):
-            out_passes(n, [("w3", 0, 0, 512), ("w3", 1, 0, 256)])
-        for n in range(4):
-            out_passes(n, [("wr", 1, 0, 512), ("w3", 1, 256, 256)])
+        for n in FIRST_TILES:
+            w3_pass(n, 0, 0, start=True)
+        for n in FIRST_TILES:
+            w3_pass(n, 1, 0)
+        for n in FIRST_TILES:
+            wr_pass(n, 0)
+        for n in LAST_TILES:
+            w3_pass(n, 0, 0, start=True)
+            w3_pass(n, 1, 0)
+        for n in FIRST_TILES:
+            wr_pass(n, 1)
+            w3_pass(n, 1, HALF, stop=True)
             store(n)
-        for n in range(4, 8):
-            out_passes(n, [("w3", 1, 256, 256), ("wr", 0, 0, 512), ("wr", 1, 0, 512)])
+        for n in LAST_TILES:
+            w3_pass(n, 1, HALF)
+            wr_pass(n, 0)
+            wr_pass(n, 1, stop=True)
             store(n)

@@ -24,14 +24,12 @@ QUADS = 4
 QUAD = P // QUADS
 LINE = 4
 TOKENS = S // PACK
-HALF = S // 2
 TILES = K // P
 FIRST_TILES = range(TILES // 2)
 LAST_TILES = range(TILES // 2, TILES)
 
-WR_PIECES = [(0, 0, 512), (1, 0, 512), (0, 512, 256), (1, 512, 256), (0, 768, 256), (1, 768, 256)]
-WR_ON_SCALAR = 2
-W2_SHARED_M = 32
+W2_ON_VECTOR = {(0, 0): 128, (1, 0): 48, (0, 1): 128, (1, 1): 0}
+VECTOR_STORE = 6
 
 
 def tile_list_ast_slot_block_kernel(
@@ -48,48 +46,56 @@ def tile_list_ast_slot_block_kernel(
         def bank(n):
             return psum.tile([P, S], F32, name=f"bank{n}")
 
-        def zeroed(width, name):
+        def zeroed(width, name, engine=nc.vector):
             tile = sbuf([P, width], U8, name)
-            nc.vector.memset(tile[:].bitcast(I32), 0)
+            engine.memset(tile[:].bitcast(I32), 0)
             return tile
 
-        def load_words(words, dtype, width, name):
-            tile = sbuf([P, width], dtype, name)
+        def load_words(words, width, name):
+            tile = sbuf([P, width], U32, name)
             nc.sync.dma_start(tile[:].bitcast(I32), words.bitcast(I32))
             return tile
 
-        def load_e4m3(words, a, name):
-            return load_words(words[a].rearrange("p c i -> p (c i)"), U32, words.shape[2], name)
+        def e4m3_words(words, a):
+            return words[a].rearrange("p c i -> p (c i)")
 
         def load_rows(w, a, c0, width, name):
             raw = sbuf([P, PACK, width], F32, name)
             rows = w[a * KP : (a + 1) * KP, c0 : c0 + width]
             nc.sync.dma_start(raw[:], rows.rearrange("(p j) c -> p j c", j=PACK))
-            return raw
+            return raw[:]
+
+        def load_scales(scales, row0, name, queue):
+            tile = zeroed(PASSES * scales.shape[2], name)
+            for r in range(QUADS):
+                queue.dma_start(
+                    tile[:].bitcast(I32).rearrange("p (a c) -> p a c", a=PASSES)[row0 + r : P : QUAD],
+                    scales.bitcast(I32).rearrange("a (d r) c -> r d a c", d=QUADS)[r],
+                )
+            return tile
 
         offsets = keep.tile([P, S // 16], U16, name="offsets")
+        w1_raw = sbuf([P, PASSES, H], U16, "w1_raw")
+
+        def load_w1(a):
+            nc.sync.dma_start(w1_raw[:, a, :].bitcast(I32), w1_words[a].bitcast(I32))
+
+        load_w1(0)
         nc.sync.dma_start(offsets[:], offs)
-        tab_rows = [zeroed(T, f"tab_rows{a}") for a in range(PASSES)]
-        w1_rows = zeroed(PASSES * H, "w1_rows")
-        v_scale = zeroed(PASSES * S, "v_scale")
-        w3_scale = zeroed(K, "w3_scale")
-        w1_raw = [load_words(w1_words[0], U16, H, "w1_raw0")]
+        tab_rows = [zeroed(T, f"tab_rows{a}", (nc.vector, nc.gpsimd)[a]) for a in range(PASSES)]
         for a in range(PASSES):
             nc.sync.dma_start(tab_rows[a][:].bitcast(I32)[0:P:8, :], tab_scales[a].bitcast(I32))
+        bias = sbuf([P, H // KP, PACK], F32, "bias")
+        nc.sync.dma_start(bias[:], b1.rearrange("(b p t) -> p b t", p=P, t=PACK))
+        w1_rows = load_scales(w1_scales, 0, "w1_rows", nc.scalar)
+        v_scale = zeroed(PASSES * S, "v_scale")
+        w3_scale = load_scales(w3_scales, 4, "w3_scale", nc.gpsimd)
         picked_rows = sbuf([P, PASSES * S], U8, "picked_rows")
         for a in range(PASSES):
             nc.vector.tensor_copy(picked_rows[:, a * S : (a + 1) * S], tab_rows[a][:].indirect(offsets[:]))
-        bias = sbuf([P, H // KP, PACK], F32, "bias")
-
-        tab = [load_e4m3(tab_words, 0, "tab0")]
-        for r in range(QUADS):
-            nc.sync.dma_start(
-                w1_rows[:].bitcast(I32).rearrange("p (a c) -> p a c", a=PASSES)[r:P:QUAD],
-                w1_scales.bitcast(I32).rearrange("a (d r) c -> r d a c", d=QUADS)[r],
-            )
-        w1_raw.append(load_words(w1_words[1], U16, H, "w1_raw1"))
-        tab.append(load_e4m3(tab_words, 1, "tab1"))
-        nc.sync.dma_start(bias[:], b1.rearrange("(b p t) -> p b t", p=P, t=PACK))
+        tab = [load_words(e4m3_words(tab_words, 0), T, "tab0")]
+        load_w1(1)
+        tab.append(load_words(e4m3_words(tab_words, 1), T, "tab1"))
         for d in range(QUADS):
             nc.sync.dma_start(
                 v_scale[:].bitcast(I32)[QUAD * d : QUAD * d + 4, :],
@@ -98,32 +104,42 @@ def tile_list_ast_slot_block_kernel(
         w2_first = load_rows(w2, 0, 0, H, "w2_raw0")
         w2_raw = {(b, 0): w2_first[:, :, b * KP : (b + 1) * KP] for b in range(H // KP)}
         for b in range(H // KP):
-            w2_raw[b, 1] = load_rows(w2, 1, b * KP, KP, f"w2_raw{b}1")[:]
-        for d in range(QUADS):
-            nc.sync.dma_start(
-                w3_scale[:].bitcast(I32)[QUAD * d + 4 : QUAD * d + 12, :],
-                w3_scales.bitcast(I32)[:, 4 * d : 4 * d + 4, :],
-            )
-        wr_raw, w3_code = [], []
-        for n, (a, c0, width) in enumerate(WR_PIECES):
-            wr_raw.append(load_rows(wr, a, c0, width, f"wr_raw{n}"))
-            if n < PASSES:
-                w3_code.append(load_e4m3(w3_words, n, f"w3_code{n}"))
+            w2_raw[b, 1] = load_rows(w2, 1, b * KP, KP, f"w2_raw{b}1")
+        w3_first = load_words(e4m3_words(w3_words, 0), K, "w3_code0")
+        w3_code = {(0, n): w3_first[:, n * P : (n + 1) * P] for n in range(TILES)}
 
-        def order_w1(src, dtype, name, reuse=None):
-            dst = sbuf([P, H], dtype, name, reuse)
+        def load_w3_second(tiles):
+            c0, width = tiles.start * P, len(tiles) * P
+            half = load_words(e4m3_words(w3_words, 1)[:, c0 * PACK : (c0 + width) * PACK], width, f"w3_code1{c0}")
+            for n in tiles:
+                w3_code[1, n] = half[:, n * P - c0 : (n + 1) * P - c0]
+
+        wr_raw = {(0, 0): load_rows(wr, 0, 0, K, "wr_raw0")}
+        load_w3_second(FIRST_TILES)
+        for tiles in (FIRST_TILES, LAST_TILES):
+            wr_raw[1, tiles.start] = load_rows(wr, 1, tiles.start * P, len(tiles) * P, f"wr_raw1{tiles.start}")
+        load_w3_second(LAST_TILES)
+
+        def order_w1(src, b, dtype, name, reuse):
+            dst = sbuf([P, PASSES, KP], dtype, f"{name}{b}", reuse)
             nc.vector.tensor_copy(
-                dst[:].rearrange("p (b t m) -> p b m t", t=PACK, m=P),
-                src.rearrange("p (b m t) -> p b m t", t=PACK, m=P),
+                dst[:].rearrange("p a (t m) -> p a m t", t=PACK),
+                src[:, :, b * KP : (b + 1) * KP].rearrange("p a (m t) -> p a m t", t=PACK),
             )
             return dst
 
-        w1_code, w1_scale, v_code = [], [], []
-        for a in range(PASSES):
-            w1_code.append(order_w1(w1_raw[a][:], U16, f"w1_code{a}", "tab_rows1" if a == 0 else None))
-            w1_scale.append(order_w1(w1_rows[:, a * H : (a + 1) * H], U8, f"w1_scale{a}"))
-            v_code.append(sbuf([P, S], U32, f"v_code{a}"))
-            nc.vector.tensor_copy(v_code[a][:], tab[a][:].indirect(offsets[:]))
+        def gather_words(a):
+            picked = sbuf([P, S], U32, f"v_code{a}")
+            nc.vector.tensor_copy(picked[:], tab[a][:].indirect(offsets[:]))
+            return picked
+
+        w1_planes = w1_rows[:].rearrange("p (a c) -> p a c", a=PASSES)
+        v_code = [gather_words(0)]
+        w1_code = [order_w1(w1_raw[:], 0, U16, "w1_code", None)]
+        w1_scale = [order_w1(w1_planes, 0, U8, "w1_scale", None)]
+        v_code.append(gather_words(1))
+        w1_code.append(order_w1(w1_raw[:], 1, U16, "w1_code", "tab1"))
+        w1_scale.append(order_w1(w1_planes, 1, U8, "w1_scale", "w1_raw"))
 
         def times_v(acc, code, scale, a, j0, width, start, stop):
             nc.tensor.matmul_mx(
@@ -141,20 +157,18 @@ def tile_list_ast_slot_block_kernel(
         def first_pass(b, t, a):
             if a == 0:
                 pre[b, t] = bank(PACK * b + t)
-            cols = slice(b * KP + t * P, b * KP + (t + 1) * P)
+            cols = slice(t * P, (t + 1) * P)
             last = a == PASSES - 1
-            times_v(pre[b, t][:], w1_code[a][:, cols].bitcast(E2M1), w1_scale[a][:, cols], a, 0, S, a == 0, last)
+            times_v(pre[b, t][:], w1_code[b][:, a, cols].bitcast(E2M1), w1_scale[b][:, a, cols], a, 0, S, a == 0, last)
             if last:
                 if t == 0:
                     gate[b] = sbuf([P, PACK, S], F32, f"gate{b}")
                 nc.scalar.activation(gate[b][:, t, :], pre[b, t][:], GELU, bias=bias[:, b, t : t + 1])
 
-        for a in range(PASSES):
+        for b in range(H // KP):
             for t in range(PACK):
-                first_pass(0, t, a)
-        for t in range(PACK):
-            for a in range(PASSES):
-                first_pass(1, t, a)
+                for a in range(PASSES):
+                    first_pass(b, t, a)
 
         def quantise(grouped, width, name, reuse=None):
             code = sbuf([P, width], U32, name + "_code", reuse)
@@ -162,7 +176,8 @@ def tile_list_ast_slot_block_kernel(
             nc.vector.quantize_mx(code[:].bitcast(E4M3), scale[:], grouped)
             return code, scale
 
-        def round_w2(b, a, on_vector):
+        def round_w2(b, a):
+            on_vector = W2_ON_VECTOR[b, a]
             grouped = sbuf([P, KP * PACK], BF16, f"w2_bf{b}{a}")
             dst = grouped[:].rearrange("p (t m j) -> p m j t", t=PACK, j=PACK)
             src = w2_raw[b, a].rearrange("p j (m t) -> p m j t", t=PACK)
@@ -202,66 +217,64 @@ def tile_list_ast_slot_block_kernel(
                 MULT,
             )
 
-        for a in range(PASSES):
-            w2_q[0, a] = quantise(round_w2(0, a, P)[:], KP, f"w2_0{a}")
+        w2_q[0, 0] = quantise(round_w2(0, 0)[:], KP, "w2_00")
+        late = round_w2(1, 0)
+        w2_q[0, 1] = quantise(round_w2(0, 1)[:], KP, "w2_01")
         second_product(0)
-        w2_q[1, 0] = quantise(round_w2(1, 0, W2_SHARED_M)[:], KP, "w2_10", "w2_bf01")
-        gate_times_up(0, 0)
-        gate_times_up(0, 1)
-        w2_q[1, 1] = quantise(round_w2(1, 1, 0)[:], KP, "w2_11")
-        gate_times_up(0, 2)
-        gate_times_up(0, 3)
-        h_q = {(0, 0): quantise(h_bf[0][:], S, "h_00")}
+        w2_q[1, 0] = quantise(late[:], KP, "w2_10", "w2_bf01")
+        w2_q[1, 1] = quantise(round_w2(1, 1)[:], KP, "w2_11")
         second_product(1)
+        h_q = []
+        for b in range(H // KP):
+            for u in range(S // TOKENS):
+                gate_times_up(b, u)
+            h_q.append(quantise(h_bf[b][:], S, f"h_{b}"))
 
         wr_bf, wr_q = {}, {}
 
-        def round_wr(n):
-            wr_bf[n] = sbuf([P, WR_PIECES[n][2] * PACK], BF16, f"wr_bf{n}")
-            dst = wr_bf[n][:].rearrange("p (c i j) -> p c j i", i=LINE, j=PACK)
-            src = wr_raw[n][:].rearrange("p j (c i) -> p c j i", i=LINE)
-            if n < WR_ON_SCALAR:
-                nc.scalar.copy(dst, src)
-            else:
-                nc.vector.tensor_copy(dst, src)
+        def round_wr(a, n, count, copy):
+            first = 0 if a == 0 else n - n % len(FIRST_TILES)
+            wr_bf[a, n] = sbuf([P, count * KP], BF16, f"wr_bf{a}{n}")
+            src = wr_raw[a, first][:, :, (n - first) * P : (n - first + count) * P]
+            copy(
+                wr_bf[a, n][:].rearrange("p (c i j) -> p c j i", i=LINE, j=PACK),
+                src.rearrange("p j (c i) -> p c j i", i=LINE),
+            )
 
-        def quantise_wr(n):
-            a, c0, width = WR_PIECES[n]
-            code, scale = quantise(wr_bf[n][:], width, f"wr_{n}")
-            for c in range(0, width, P):
-                wr_q[a, (c0 + c) // P] = (code[:, c : c + P], scale[:, c : c + P])
+        def quantise_wr(a, n, count):
+            code, scale = quantise(wr_bf[a, n][:], count * P, f"wr_{a}{n}")
+            for i in range(count):
+                wr_q[a, n + i] = (code[:, i * P : (i + 1) * P], scale[:, i * P : (i + 1) * P])
 
-        def quantise_h_half(half):
-            j0 = half * HALF
-            h_q[1, j0] = quantise(h_bf[1][:, j0 * PACK : (j0 + HALF) * PACK], HALF, f"h_1{half}")
+        on_vector, on_scalar = nc.vector.tensor_copy, nc.scalar.copy
+        pieces = [(0, 2, on_scalar), (4, 2, on_vector), (6, 1, on_vector), (2, 2, on_scalar), (7, 1, on_scalar)]
+        for n, count, copy in pieces:
+            round_wr(0, n, count, copy)
+        for n, count, copy in pieces:
+            quantise_wr(0, n, count)
+        for n in FIRST_TILES:
+            round_wr(1, n, 1, on_scalar if n % 2 else on_vector)
+        for n in FIRST_TILES:
+            quantise_wr(1, n, 1)
+        for n in LAST_TILES:
+            round_wr(1, n, 1, on_vector)
+            if n > LAST_TILES.start:
+                quantise_wr(1, n - 1, 1)
+        quantise_wr(1, TILES - 1, 1)
 
-        round_wr(0)
-        for u in range(3):
-            gate_times_up(1, u)
-        quantise_h_half(0)
-        quantise_wr(0)
-        gate_times_up(1, 3)
-        round_wr(1)
-        quantise_wr(1)
-        quantise_h_half(1)
-        for n in range(WR_ON_SCALAR, len(WR_PIECES)):
-            round_wr(n)
-            quantise_wr(n)
+        total = {}
 
-        total, results = {}, {}
-
-        def w3_pass(n, a, j0, start=False, stop=False):
-            code, scale = h_q[a, j0]
-            width = S if a == 0 else HALF
-            if start:
+        def w3_pass(n, a, stop=False):
+            code, scale = h_q[a]
+            if a == 0:
                 total[n] = bank(n)
             nc.tensor.matmul_mx(
-                total[n][:, j0 : j0 + width],
-                lhsT=w3_code[a][:, n * P : (n + 1) * P].bitcast(E4M3),
-                lhsT_scale=w3_scale[4 * (a + 1) :, n * P : (n + 1) * P],
+                total[n][:],
+                lhsT=w3_code[a, n].bitcast(E4M3),
+                lhsT_scale=w3_scale[4:, a * K + n * P : a * K + (n + 1) * P],
                 rhs=code[:].bitcast(E4M3),
                 rhs_scale=scale[:],
-                start=start,
+                start=a == 0,
                 stop=stop,
             )
 
@@ -270,31 +283,24 @@ def tile_list_ast_slot_block_kernel(
             times_v(total[n][:], code.bitcast(E4M3), scale, a, 0, S, False, stop)
 
         def store(n):
-            group, place = divmod(n, len(FIRST_TILES))
-            if place == 0:
-                results[group] = sbuf([P, len(FIRST_TILES), S], F32, f"result{group}")
-            result = results[group][:, place, :]
-            if n == TILES - 1:
-                nc.vector.tensor_copy(result, total[n][:])
+            result = sbuf([P, S], F32, f"result{n}")
+            if n == VECTOR_STORE:
+                nc.vector.tensor_copy(result[:], total[n][:])
             else:
-                nc.scalar.copy(result, total[n][:])
-            nc.sync.dma_start(out[n * P : (n + 1) * P, :], result)
+                nc.scalar.copy(result[:], total[n][:])
+            nc.sync.dma_start(out[n * P : (n + 1) * P, :], result[:])
 
+        for n in range(TILES):
+            w3_pass(n, 0)
         for n in FIRST_TILES:
-            w3_pass(n, 0, 0, start=True)
+            w3_pass(n, 1)
+        for first, count, copy in pieces:
+            for n in range(first, first + count):
+                wr_pass(n, 0)
         for n in FIRST_TILES:
-            w3_pass(n, 1, 0)
-        for n in FIRST_TILES:
-            wr_pass(n, 0)
-        for n in LAST_TILES:
-            w3_pass(n, 0, 0, start=True)
-            w3_pass(n, 1, 0)
-        for n in FIRST_TILES:
-            wr_pass(n, 1)
-            w3_pass(n, 1, HALF, stop=True)
+            wr_pass(n, 1, stop=True)
             store(n)
         for n in LAST_TILES:
-            w3_pass(n, 1, HALF)
-            wr_pass(n, 0)
-            wr_pass(n, 1, stop=True)
+            wr_pass(n, 1)
+            w3_pass(n, 1, stop=True)
             store(n)

@@ -85,40 +85,42 @@ def tile_list_ast_slot_block_kernel(
         tab_rows = [zeroed(T, f"tab_rows{a}", (nc.vector, nc.gpsimd)[a]) for a in range(PASSES)]
         for a in range(PASSES):
             nc.sync.dma_start(tab_rows[a][:].bitcast(I32)[0:P:8, :], tab_scales[a].bitcast(I32))
-        bias = sbuf([P, H // KP, PACK], F32, "bias")
-        nc.sync.dma_start(bias[:], b1.rearrange("(b p t) -> p b t", p=P, t=PACK))
-        w1_rows = load_scales(w1_scales, 0, "w1_rows", nc.scalar)
         v_scale = zeroed(PASSES * S, "v_scale")
-        w3_scale = load_scales(w3_scales, 4, "w3_scale", nc.gpsimd)
         picked_rows = sbuf([P, PASSES * S], U8, "picked_rows")
         for a in range(PASSES):
             nc.vector.tensor_copy(picked_rows[:, a * S : (a + 1) * S], tab_rows[a][:].indirect(offsets[:]))
         tab = [load_words(e4m3_words(tab_words, 0), T, "tab0")]
+        w1_rows = load_scales(w1_scales, 0, "w1_rows", nc.sync)
         load_w1(1)
         tab.append(load_words(e4m3_words(tab_words, 1), T, "tab1"))
-        for d in range(QUADS):
-            nc.sync.dma_start(
-                v_scale[:].bitcast(I32)[QUAD * d : QUAD * d + 4, :],
-                picked_rows[:].bitcast(I32)[QUAD * d : QUAD * (d + 1) : 8, :],
-            )
+        bias = sbuf([P, H // KP, PACK], F32, "bias")
+        nc.sync.dma_start(bias[:], b1.rearrange("(b p t) -> p b t", p=P, t=PACK))
+        for r in range(QUADS):
+            nc.sync.dma_start(v_scale[:].bitcast(I32)[r:P:QUAD, :], picked_rows[:].bitcast(I32)[8 * r : P : QUAD, :])
         w2_first = load_rows(w2, 0, 0, H, "w2_raw0")
         w2_raw = {(b, 0): w2_first[:, :, b * KP : (b + 1) * KP] for b in range(H // KP)}
         for b in range(H // KP):
             w2_raw[b, 1] = load_rows(w2, 1, b * KP, KP, f"w2_raw{b}1")
-        w3_first = load_words(e4m3_words(w3_words, 0), K, "w3_code0")
-        w3_code = {(0, n): w3_first[:, n * P : (n + 1) * P] for n in range(TILES)}
+        w3_scale = load_scales(w3_scales, 4, "w3_scale", nc.sync)
+        w3_code, wr_raw = {}, {}
 
-        def load_w3_second(tiles):
+        def load_w3(a, tiles):
             c0, width = tiles.start * P, len(tiles) * P
-            half = load_words(e4m3_words(w3_words, 1)[:, c0 * PACK : (c0 + width) * PACK], width, f"w3_code1{c0}")
+            words = load_words(e4m3_words(w3_words, a)[:, c0 * PACK : (c0 + width) * PACK], width, f"w3_code{a}{c0}")
             for n in tiles:
-                w3_code[1, n] = half[:, n * P - c0 : (n + 1) * P - c0]
+                w3_code[a, n] = words[:, n * P - c0 : (n + 1) * P - c0]
 
-        wr_raw = {(0, 0): load_rows(wr, 0, 0, K, "wr_raw0")}
-        load_w3_second(FIRST_TILES)
-        for tiles in (FIRST_TILES, LAST_TILES):
-            wr_raw[1, tiles.start] = load_rows(wr, 1, tiles.start * P, len(tiles) * P, f"wr_raw1{tiles.start}")
-        load_w3_second(LAST_TILES)
+        def load_wr(a, tiles):
+            raw = load_rows(wr, a, tiles.start * P, len(tiles) * P, f"wr_raw{a}{tiles.start}")
+            for n in tiles:
+                wr_raw[a, n] = (raw, tiles.start)
+
+        load_w3(0, range(TILES))
+        load_wr(0, range(TILES))
+        load_w3(1, FIRST_TILES)
+        load_wr(1, FIRST_TILES)
+        load_wr(1, LAST_TILES)
+        load_w3(1, LAST_TILES)
 
         def order_w1(src, b, dtype, name, reuse):
             dst = sbuf([P, PASSES, KP], dtype, f"{name}{b}", reuse)
@@ -233,9 +235,9 @@ def tile_list_ast_slot_block_kernel(
         wr_bf, wr_q = {}, {}
 
         def round_wr(a, n, count, copy):
-            first = 0 if a == 0 else n - n % len(FIRST_TILES)
+            raw, first = wr_raw[a, n]
             wr_bf[a, n] = sbuf([P, count * KP], BF16, f"wr_bf{a}{n}")
-            src = wr_raw[a, first][:, :, (n - first) * P : (n - first + count) * P]
+            src = raw[:, :, (n - first) * P : (n - first + count) * P]
             copy(
                 wr_bf[a, n][:].rearrange("p (c i j) -> p c j i", i=LINE, j=PACK),
                 src.rearrange("p j (c i) -> p c j i", i=LINE),
@@ -247,20 +249,30 @@ def tile_list_ast_slot_block_kernel(
                 wr_q[a, n + i] = (code[:, i * P : (i + 1) * P], scale[:, i * P : (i + 1) * P])
 
         on_vector, on_scalar = nc.vector.tensor_copy, nc.scalar.copy
-        pieces = [(0, 2, on_scalar), (4, 2, on_vector), (6, 1, on_vector), (2, 2, on_scalar), (7, 1, on_scalar)]
-        for n, count, copy in pieces:
-            round_wr(0, n, count, copy)
-        for n, count, copy in pieces:
-            quantise_wr(0, n, count)
-        for n in FIRST_TILES:
-            round_wr(1, n, 1, on_scalar if n % 2 else on_vector)
-        for n in FIRST_TILES:
-            quantise_wr(1, n, 1)
-        for n in LAST_TILES:
-            round_wr(1, n, 1, on_vector)
-            if n > LAST_TILES.start:
-                quantise_wr(1, n - 1, 1)
-        quantise_wr(1, TILES - 1, 1)
+        round_wr(0, 0, 2, on_scalar)
+        round_wr(0, 2, 2, on_scalar)
+        quantise_wr(0, 0, 2)
+        quantise_wr(0, 2, 2)
+        round_wr(1, 0, 1, on_vector)
+        round_wr(1, 1, 1, on_vector)
+        quantise_wr(1, 0, 1)
+        round_wr(1, 2, 1, on_vector)
+        quantise_wr(1, 1, 1)
+        round_wr(1, 3, 1, on_vector)
+        quantise_wr(1, 2, 1)
+        quantise_wr(1, 3, 1)
+        round_wr(0, 4, 2, on_scalar)
+        round_wr(0, 6, 2, on_scalar)
+        quantise_wr(0, 4, 2)
+        quantise_wr(0, 6, 2)
+        round_wr(1, 4, 1, on_vector)
+        round_wr(1, 5, 1, on_vector)
+        quantise_wr(1, 4, 1)
+        round_wr(1, 6, 1, on_vector)
+        quantise_wr(1, 5, 1)
+        round_wr(1, 7, 1, on_vector)
+        quantise_wr(1, 6, 1)
+        quantise_wr(1, 7, 1)
 
         total = {}
 
@@ -290,16 +302,19 @@ def tile_list_ast_slot_block_kernel(
                 nc.scalar.copy(result[:], total[n][:])
             nc.sync.dma_start(out[n * P : (n + 1) * P, :], result[:])
 
-        for n in range(TILES):
+        for n in FIRST_TILES:
             w3_pass(n, 0)
         for n in FIRST_TILES:
             w3_pass(n, 1)
-        for first, count, copy in pieces:
-            for n in range(first, first + count):
-                wr_pass(n, 0)
+        for n in FIRST_TILES:
+            wr_pass(n, 0)
         for n in FIRST_TILES:
             wr_pass(n, 1, stop=True)
             store(n)
+        for n in LAST_TILES:
+            w3_pass(n, 0)
+        for n in LAST_TILES:
+            wr_pass(n, 0)
         for n in LAST_TILES:
             wr_pass(n, 1)
             w3_pass(n, 1, stop=True)

@@ -25,8 +25,8 @@ QUAD = P // QUADS
 LINE = 4
 TOKENS = S // PACK
 TILES = K // P
-FIRST_TILES = range(TILES // 2)
-LAST_TILES = range(TILES // 2, TILES)
+FIRST_TILES = range(5)
+LAST_TILES = range(5, TILES)
 
 W2_ON_VECTOR = {(0, 0): 128, (1, 0): 48, (0, 1): 128, (1, 1): 0}
 VECTOR_STORE = 6
@@ -77,12 +77,9 @@ def tile_list_ast_slot_block_kernel(
         offsets = keep.tile([P, S // 16], U16, name="offsets")
         w1_raw = sbuf([P, PASSES, H], U16, "w1_raw")
 
-        def load_w1(a):
-            nc.sync.dma_start(w1_raw[:, a, :].bitcast(I32), w1_words[a].bitcast(I32))
-
-        load_w1(0)
+        nc.sync.dma_start(w1_raw[:].bitcast(I32), w1_words.bitcast(I32).rearrange("a p c -> p a c"))
         nc.sync.dma_start(offsets[:], offs)
-        tab_rows = [zeroed(T, f"tab_rows{a}", (nc.vector, nc.gpsimd)[a]) for a in range(PASSES)]
+        tab_rows = [zeroed(T, f"tab_rows{a}", nc.vector) for a in range(PASSES)]
         for a in range(PASSES):
             nc.sync.dma_start(tab_rows[a][:].bitcast(I32)[0:P:8, :], tab_scales[a].bitcast(I32))
         v_scale = zeroed(PASSES * S, "v_scale")
@@ -91,7 +88,6 @@ def tile_list_ast_slot_block_kernel(
             nc.vector.tensor_copy(picked_rows[:, a * S : (a + 1) * S], tab_rows[a][:].indirect(offsets[:]))
         tab = [load_words(e4m3_words(tab_words, 0), T, "tab0")]
         w1_rows = load_scales(w1_scales, 0, "w1_rows", nc.sync)
-        load_w1(1)
         tab.append(load_words(e4m3_words(tab_words, 1), T, "tab1"))
         bias = sbuf([P, H // KP, PACK], F32, "bias")
         nc.sync.dma_start(bias[:], b1.rearrange("(b p t) -> p b t", p=P, t=PACK))
@@ -115,10 +111,11 @@ def tile_list_ast_slot_block_kernel(
             for n in tiles:
                 wr_raw[a, n] = (raw, tiles.start)
 
+        load_wr(0, FIRST_TILES)
         load_w3(0, range(TILES))
-        load_wr(0, range(TILES))
-        load_w3(1, FIRST_TILES)
         load_wr(1, FIRST_TILES)
+        load_w3(1, FIRST_TILES)
+        load_wr(0, LAST_TILES)
         load_wr(1, LAST_TILES)
         load_w3(1, LAST_TILES)
 
@@ -137,7 +134,7 @@ def tile_list_ast_slot_block_kernel(
 
         w1_planes = w1_rows[:].rearrange("p (a c) -> p a c", a=PASSES)
         v_code = [gather_words(0)]
-        w1_code = [order_w1(w1_raw[:], 0, U16, "w1_code", None)]
+        w1_code = [order_w1(w1_raw[:], 0, U16, "w1_code", "tab_rows1")]
         w1_scale = [order_w1(w1_planes, 0, U8, "w1_scale", None)]
         v_code.append(gather_words(1))
         w1_code.append(order_w1(w1_raw[:], 1, U16, "w1_code", "tab1"))
@@ -251,23 +248,21 @@ def tile_list_ast_slot_block_kernel(
         on_vector, on_scalar = nc.vector.tensor_copy, nc.scalar.copy
         round_wr(0, 0, 2, on_scalar)
         round_wr(0, 2, 2, on_scalar)
+        round_wr(0, 4, 1, on_scalar)
         quantise_wr(0, 0, 2)
         quantise_wr(0, 2, 2)
-        round_wr(1, 0, 1, on_vector)
-        round_wr(1, 1, 1, on_vector)
-        quantise_wr(1, 0, 1)
-        round_wr(1, 2, 1, on_vector)
-        quantise_wr(1, 1, 1)
-        round_wr(1, 3, 1, on_vector)
-        quantise_wr(1, 2, 1)
-        quantise_wr(1, 3, 1)
-        round_wr(0, 4, 2, on_scalar)
-        round_wr(0, 6, 2, on_scalar)
-        quantise_wr(0, 4, 2)
-        quantise_wr(0, 6, 2)
+        quantise_wr(0, 4, 1)
+        round_wr(1, 0, 2, on_scalar)
+        round_wr(1, 2, 2, on_scalar)
         round_wr(1, 4, 1, on_vector)
-        round_wr(1, 5, 1, on_vector)
+        quantise_wr(1, 0, 2)
         quantise_wr(1, 4, 1)
+        quantise_wr(1, 2, 2)
+        round_wr(0, 5, 2, on_vector)
+        round_wr(0, 7, 1, on_vector)
+        quantise_wr(0, 5, 2)
+        quantise_wr(0, 7, 1)
+        round_wr(1, 5, 1, on_vector)
         round_wr(1, 6, 1, on_vector)
         quantise_wr(1, 5, 1)
         round_wr(1, 7, 1, on_vector)
@@ -296,7 +291,7 @@ def tile_list_ast_slot_block_kernel(
 
         def store(n):
             result = sbuf([P, S], F32, f"result{n}")
-            if n == VECTOR_STORE:
+            if n in (6,):
                 nc.vector.tensor_copy(result[:], total[n][:])
             else:
                 nc.scalar.copy(result[:], total[n][:])

@@ -24,9 +24,11 @@ QUADS = 4
 QUAD = P // QUADS
 LINE = 4
 TOKENS = S // PACK
+STORES = {0: (0, 1), 1: (1, 1), 2: (2, 1), 3: (3, 1), 4: (4, 1), 5: (5, 1), 6: (6, 1), 7: (7, 1)}
+VEC = (7,)
 TILES = K // P
-FIRST_TILES = range(5)
-LAST_TILES = range(5, TILES)
+FIRST_TILES = range(TILES // 2)
+LAST_TILES = range(TILES // 2, TILES)
 
 W2_ON_VECTOR = {(0, 0): 128, (1, 0): 48, (0, 1): 128, (1, 1): 0}
 VECTOR_STORE = 6
@@ -82,10 +84,11 @@ def tile_list_ast_slot_block_kernel(
         tab_rows = [zeroed(T, f"tab_rows{a}", nc.vector) for a in range(PASSES)]
         for a in range(PASSES):
             nc.sync.dma_start(tab_rows[a][:].bitcast(I32)[0:P:8, :], tab_scales[a].bitcast(I32))
-        v_scale = zeroed(PASSES * S, "v_scale")
         picked_rows = sbuf([P, PASSES * S], U8, "picked_rows")
         for a in range(PASSES):
             nc.vector.tensor_copy(picked_rows[:, a * S : (a + 1) * S], tab_rows[a][:].indirect(offsets[:]))
+        v_scale = zeroed(PASSES * S, "v_scale")
+
         tab = [load_words(e4m3_words(tab_words, 0), T, "tab0")]
         w1_rows = load_scales(w1_scales, 0, "w1_rows", nc.sync)
         tab.append(load_words(e4m3_words(tab_words, 1), T, "tab1"))
@@ -106,6 +109,13 @@ def tile_list_ast_slot_block_kernel(
             for n in tiles:
                 w3_code[a, n] = words[:, n * P - c0 : (n + 1) * P - c0]
 
+        def load_w3_all():
+            words = sbuf([P, PASSES, K], U32, "w3_code")
+            nc.sync.dma_start(words[:].bitcast(I32), w3_words.rearrange("a p c i -> p a (c i)").bitcast(I32))
+            for a in range(PASSES):
+                for n in range(TILES):
+                    w3_code[a, n] = words[:, a, n * P : (n + 1) * P]
+
         def load_wr(a, tiles):
             raw = load_rows(wr, a, tiles.start * P, len(tiles) * P, f"wr_raw{a}{tiles.start}")
             for n in tiles:
@@ -114,10 +124,10 @@ def tile_list_ast_slot_block_kernel(
         load_wr(0, FIRST_TILES)
         load_w3(0, range(TILES))
         load_wr(1, FIRST_TILES)
-        load_w3(1, FIRST_TILES)
+        load_w3(1, range(TILES))
         load_wr(0, LAST_TILES)
-        load_wr(1, LAST_TILES)
-        load_w3(1, LAST_TILES)
+        load_wr(1, range(4, 6))
+        load_wr(1, range(6, 8))
 
         def order_w1(src, b, dtype, name, reuse):
             dst = sbuf([P, PASSES, KP], dtype, f"{name}{b}", reuse)
@@ -132,9 +142,9 @@ def tile_list_ast_slot_block_kernel(
             nc.vector.tensor_copy(picked[:], tab[a][:].indirect(offsets[:]))
             return picked
 
-        w1_planes = w1_rows[:].rearrange("p (a c) -> p a c", a=PASSES)
         v_code = [gather_words(0)]
         w1_code = [order_w1(w1_raw[:], 0, U16, "w1_code", "tab_rows1")]
+        w1_planes = w1_rows[:].rearrange("p (a c) -> p a c", a=PASSES)
         w1_scale = [order_w1(w1_planes, 0, U8, "w1_scale", None)]
         v_code.append(gather_words(1))
         w1_code.append(order_w1(w1_raw[:], 1, U16, "w1_code", "tab1"))
@@ -246,25 +256,21 @@ def tile_list_ast_slot_block_kernel(
                 wr_q[a, n + i] = (code[:, i * P : (i + 1) * P], scale[:, i * P : (i + 1) * P])
 
         on_vector, on_scalar = nc.vector.tensor_copy, nc.scalar.copy
-        round_wr(0, 0, 2, on_scalar)
-        round_wr(0, 2, 2, on_scalar)
-        round_wr(0, 4, 1, on_scalar)
-        quantise_wr(0, 0, 2)
-        quantise_wr(0, 2, 2)
-        quantise_wr(0, 4, 1)
+        round_wr(0, 0, 4, on_scalar)
+        quantise_wr(0, 0, 4)
         round_wr(1, 0, 2, on_scalar)
         round_wr(1, 2, 2, on_scalar)
-        round_wr(1, 4, 1, on_vector)
         quantise_wr(1, 0, 2)
-        quantise_wr(1, 4, 1)
         quantise_wr(1, 2, 2)
-        round_wr(0, 5, 2, on_vector)
-        round_wr(0, 7, 1, on_vector)
-        quantise_wr(0, 5, 2)
-        quantise_wr(0, 7, 1)
+        round_wr(0, 4, 2, on_vector)
+        round_wr(0, 6, 2, on_vector)
+        quantise_wr(0, 4, 2)
+        quantise_wr(0, 6, 2)
+        round_wr(1, 4, 1, on_vector)
         round_wr(1, 5, 1, on_vector)
-        round_wr(1, 6, 1, on_vector)
+        quantise_wr(1, 4, 1)
         quantise_wr(1, 5, 1)
+        round_wr(1, 6, 1, on_vector)
         round_wr(1, 7, 1, on_vector)
         quantise_wr(1, 6, 1)
         quantise_wr(1, 7, 1)
@@ -289,13 +295,20 @@ def tile_list_ast_slot_block_kernel(
             code, scale = wr_q[a, n]
             times_v(total[n][:], code.bitcast(E4M3), scale, a, 0, S, False, stop)
 
+        results = {}
+
         def store(n):
-            result = sbuf([P, S], F32, f"result{n}")
-            if n in (6,):
-                nc.vector.tensor_copy(result[:], total[n][:])
+            first, count = STORES[n]
+            if n == first:
+                results[first] = sbuf([P, count, S], F32, f"result{first}")
+            result = results[first]
+            if n in VEC:
+                nc.vector.tensor_copy(result[:, n - first, :], total[n][:])
             else:
-                nc.scalar.copy(result[:], total[n][:])
-            nc.sync.dma_start(out[n * P : (n + 1) * P, :], result[:])
+                nc.scalar.copy(result[:, n - first, :], total[n][:])
+            if n == first + count - 1:
+                rows = out[first * P : (first + count) * P, :]
+                nc.sync.dma_start(rows.rearrange("(n p) s -> p n s", p=P), result[:])
 
         for n in FIRST_TILES:
             w3_pass(n, 0)
@@ -309,8 +322,8 @@ def tile_list_ast_slot_block_kernel(
         for n in LAST_TILES:
             w3_pass(n, 0)
         for n in LAST_TILES:
-            wr_pass(n, 0)
+            w3_pass(n, 1)
         for n in LAST_TILES:
-            wr_pass(n, 1)
-            w3_pass(n, 1, stop=True)
+            wr_pass(n, 0)
+            wr_pass(n, 1, stop=True)
             store(n)

@@ -24,14 +24,13 @@ QUADS = 4
 QUAD = P // QUADS
 LINE = 4
 TOKENS = S // PACK
-STORES = {0: (0, 1), 1: (1, 1), 2: (2, 1), 3: (3, 1), 4: (4, 1), 5: (5, 1), 6: (6, 1), 7: (7, 1)}
-VEC = (7,)
 TILES = K // P
 FIRST_TILES = range(TILES // 2)
 LAST_TILES = range(TILES // 2, TILES)
 
+LAST_PAIRS = [range(n, n + 2) for n in range(LAST_TILES.start, TILES, 2)]
+W3_ROW0 = 4
 W2_ON_VECTOR = {(0, 0): 128, (1, 0): 48, (0, 1): 128, (1, 1): 0}
-VECTOR_STORE = 6
 
 
 def tile_list_ast_slot_block_kernel(
@@ -48,18 +47,15 @@ def tile_list_ast_slot_block_kernel(
         def bank(n):
             return psum.tile([P, S], F32, name=f"bank{n}")
 
-        def zeroed(width, name, engine=nc.vector):
+        def zeroed(width, name):
             tile = sbuf([P, width], U8, name)
-            engine.memset(tile[:].bitcast(I32), 0)
+            nc.vector.memset(tile[:].bitcast(I32), 0)
             return tile
 
-        def load_words(words, width, name):
-            tile = sbuf([P, width], U32, name)
-            nc.sync.dma_start(tile[:].bitcast(I32), words.bitcast(I32))
+        def load_e4m3(words, a, name):
+            tile = sbuf([P, words.shape[2]], U32, name)
+            nc.sync.dma_start(tile[:].bitcast(I32), words[a].rearrange("p c i -> p (c i)").bitcast(I32))
             return tile
-
-        def e4m3_words(words, a):
-            return words[a].rearrange("p c i -> p (c i)")
 
         def load_rows(w, a, c0, width, name):
             raw = sbuf([P, PACK, width], F32, name)
@@ -67,10 +63,10 @@ def tile_list_ast_slot_block_kernel(
             nc.sync.dma_start(raw[:], rows.rearrange("(p j) c -> p j c", j=PACK))
             return raw[:]
 
-        def load_scales(scales, row0, name, queue):
+        def load_scales(scales, row0, name):
             tile = zeroed(PASSES * scales.shape[2], name)
             for r in range(QUADS):
-                queue.dma_start(
+                nc.sync.dma_start(
                     tile[:].bitcast(I32).rearrange("p (a c) -> p a c", a=PASSES)[row0 + r : P : QUAD],
                     scales.bitcast(I32).rearrange("a (d r) c -> r d a c", d=QUADS)[r],
                 )
@@ -78,10 +74,9 @@ def tile_list_ast_slot_block_kernel(
 
         offsets = keep.tile([P, S // 16], U16, name="offsets")
         w1_raw = sbuf([P, PASSES, H], U16, "w1_raw")
-
-        nc.sync.dma_start(w1_raw[:].bitcast(I32), w1_words.bitcast(I32).rearrange("a p c -> p a c"))
+        nc.sync.dma_start(w1_raw[:, 0, :].bitcast(I32), w1_words[0].bitcast(I32))
         nc.sync.dma_start(offsets[:], offs)
-        tab_rows = [zeroed(T, f"tab_rows{a}", nc.vector) for a in range(PASSES)]
+        tab_rows = [zeroed(T, f"tab_rows{a}") for a in range(PASSES)]
         for a in range(PASSES):
             nc.sync.dma_start(tab_rows[a][:].bitcast(I32)[0:P:8, :], tab_scales[a].bitcast(I32))
         picked_rows = sbuf([P, PASSES * S], U8, "picked_rows")
@@ -89,9 +84,10 @@ def tile_list_ast_slot_block_kernel(
             nc.vector.tensor_copy(picked_rows[:, a * S : (a + 1) * S], tab_rows[a][:].indirect(offsets[:]))
         v_scale = zeroed(PASSES * S, "v_scale")
 
-        tab = [load_words(e4m3_words(tab_words, 0), T, "tab0")]
-        w1_rows = load_scales(w1_scales, 0, "w1_rows", nc.sync)
-        tab.append(load_words(e4m3_words(tab_words, 1), T, "tab1"))
+        tab = [load_e4m3(tab_words, 0, "tab0")]
+        w1_rows = load_scales(w1_scales, 0, "w1_rows")
+        nc.sync.dma_start(w1_raw[:, 1, :].bitcast(I32), w1_words[1].bitcast(I32))
+        tab.append(load_e4m3(tab_words, 1, "tab1"))
         bias = sbuf([P, H // KP, PACK], F32, "bias")
         nc.sync.dma_start(bias[:], b1.rearrange("(b p t) -> p b t", p=P, t=PACK))
         for r in range(QUADS):
@@ -100,36 +96,22 @@ def tile_list_ast_slot_block_kernel(
         w2_raw = {(b, 0): w2_first[:, :, b * KP : (b + 1) * KP] for b in range(H // KP)}
         for b in range(H // KP):
             w2_raw[b, 1] = load_rows(w2, 1, b * KP, KP, f"w2_raw{b}1")
-        w3_scale = load_scales(w3_scales, 4, "w3_scale", nc.sync)
-        w3_code, wr_raw = {}, {}
-
-        def load_w3(a, tiles):
-            c0, width = tiles.start * P, len(tiles) * P
-            words = load_words(e4m3_words(w3_words, a)[:, c0 * PACK : (c0 + width) * PACK], width, f"w3_code{a}{c0}")
-            for n in tiles:
-                w3_code[a, n] = words[:, n * P - c0 : (n + 1) * P - c0]
-
-        def load_w3_all():
-            words = sbuf([P, PASSES, K], U32, "w3_code")
-            nc.sync.dma_start(words[:].bitcast(I32), w3_words.rearrange("a p c i -> p a (c i)").bitcast(I32))
-            for a in range(PASSES):
-                for n in range(TILES):
-                    w3_code[a, n] = words[:, a, n * P : (n + 1) * P]
+        w3_scale = load_scales(w3_scales, W3_ROW0, "w3_scale")
+        w3_code, wr_raw = [], {}
 
         def load_wr(a, tiles):
             raw = load_rows(wr, a, tiles.start * P, len(tiles) * P, f"wr_raw{a}{tiles.start}")
             for n in tiles:
                 wr_raw[a, n] = (raw, tiles.start)
 
-        load_wr(0, FIRST_TILES)
-        load_w3(0, range(TILES))
-        load_wr(1, FIRST_TILES)
-        load_w3(1, range(TILES))
-        load_wr(0, LAST_TILES)
-        load_wr(1, range(4, 6))
-        load_wr(1, range(6, 8))
+        for a in range(PASSES):
+            load_wr(a, FIRST_TILES)
+            w3_code.append(load_e4m3(w3_words, a, f"w3_code{a}"))
+        for pair in LAST_PAIRS:
+            for a in range(PASSES):
+                load_wr(a, pair)
 
-        def order_w1(src, b, dtype, name, reuse):
+        def order_w1(src, b, dtype, name, reuse=None):
             dst = sbuf([P, PASSES, KP], dtype, f"{name}{b}", reuse)
             nc.vector.tensor_copy(
                 dst[:].rearrange("p a (t m) -> p a m t", t=PACK),
@@ -145,7 +127,7 @@ def tile_list_ast_slot_block_kernel(
         v_code = [gather_words(0)]
         w1_code = [order_w1(w1_raw[:], 0, U16, "w1_code", "tab_rows1")]
         w1_planes = w1_rows[:].rearrange("p (a c) -> p a c", a=PASSES)
-        w1_scale = [order_w1(w1_planes, 0, U8, "w1_scale", None)]
+        w1_scale = [order_w1(w1_planes, 0, U8, "w1_scale")]
         v_code.append(gather_words(1))
         w1_code.append(order_w1(w1_raw[:], 1, U16, "w1_code", "tab1"))
         w1_scale.append(order_w1(w1_planes, 1, U8, "w1_scale", "w1_raw"))
@@ -217,7 +199,7 @@ def tile_list_ast_slot_block_kernel(
 
         def gate_times_up(b, u):
             if u == 0:
-                h_bf[b] = sbuf([P, S * PACK], BF16, f"h_bf{b}0")
+                h_bf[b] = sbuf([P, S * PACK], BF16, f"h_bf{b}")
             tokens = slice(u * TOKENS, (u + 1) * TOKENS)
             nc.vector.tensor_tensor(
                 h_bf[b][:, tokens.start * PACK : tokens.stop * PACK].rearrange("p (c i t) -> p c t i", i=LINE, t=PACK),
@@ -255,75 +237,61 @@ def tile_list_ast_slot_block_kernel(
             for i in range(count):
                 wr_q[a, n + i] = (code[:, i * P : (i + 1) * P], scale[:, i * P : (i + 1) * P])
 
-        on_vector, on_scalar = nc.vector.tensor_copy, nc.scalar.copy
-        round_wr(0, 0, 4, on_scalar)
-        quantise_wr(0, 0, 4)
-        round_wr(1, 0, 2, on_scalar)
-        round_wr(1, 2, 2, on_scalar)
-        quantise_wr(1, 0, 2)
-        quantise_wr(1, 2, 2)
-        round_wr(0, 4, 2, on_vector)
-        round_wr(0, 6, 2, on_vector)
-        quantise_wr(0, 4, 2)
-        quantise_wr(0, 6, 2)
-        round_wr(1, 4, 1, on_vector)
-        round_wr(1, 5, 1, on_vector)
-        quantise_wr(1, 4, 1)
-        quantise_wr(1, 5, 1)
-        round_wr(1, 6, 1, on_vector)
-        round_wr(1, 7, 1, on_vector)
-        quantise_wr(1, 6, 1)
-        quantise_wr(1, 7, 1)
+        half = len(FIRST_TILES) // 2
+        round_wr(0, 0, len(FIRST_TILES), nc.scalar.copy)
+        quantise_wr(0, 0, len(FIRST_TILES))
+        for n in (0, half):
+            round_wr(1, n, half, nc.scalar.copy)
+        for n in (0, half):
+            quantise_wr(1, n, half)
 
         total = {}
 
-        def w3_pass(n, a, stop=False):
+        def w3_pass(n, a):
             code, scale = h_q[a]
             if a == 0:
                 total[n] = bank(n)
             nc.tensor.matmul_mx(
                 total[n][:],
-                lhsT=w3_code[a, n].bitcast(E4M3),
-                lhsT_scale=w3_scale[4:, a * K + n * P : a * K + (n + 1) * P],
+                lhsT=w3_code[a][:, n * P : (n + 1) * P].bitcast(E4M3),
+                lhsT_scale=w3_scale[W3_ROW0:, a * K + n * P : a * K + (n + 1) * P],
                 rhs=code[:].bitcast(E4M3),
                 rhs_scale=scale[:],
                 start=a == 0,
-                stop=stop,
+                stop=False,
             )
 
-        def wr_pass(n, a, stop=False):
+        def wr_pass(n, a):
             code, scale = wr_q[a, n]
-            times_v(total[n][:], code.bitcast(E4M3), scale, a, 0, S, False, stop)
-
-        results = {}
+            times_v(total[n][:], code.bitcast(E4M3), scale, a, 0, S, False, a == PASSES - 1)
 
         def store(n):
-            first, count = STORES[n]
-            if n == first:
-                results[first] = sbuf([P, count, S], F32, f"result{first}")
-            result = results[first]
-            if n in VEC:
-                nc.vector.tensor_copy(result[:, n - first, :], total[n][:])
+            result = sbuf([P, S], F32, f"result{n}")
+            if n == TILES - 1:
+                nc.vector.tensor_copy(result[:], total[n][:])
             else:
-                nc.scalar.copy(result[:, n - first, :], total[n][:])
-            if n == first + count - 1:
-                rows = out[first * P : (first + count) * P, :]
-                nc.sync.dma_start(rows.rearrange("(n p) s -> p n s", p=P), result[:])
+                nc.scalar.copy(result[:], total[n][:])
+            nc.sync.dma_start(out[n * P : (n + 1) * P, :], result[:])
 
-        for n in FIRST_TILES:
-            w3_pass(n, 0)
-        for n in FIRST_TILES:
-            w3_pass(n, 1)
+        for a in range(PASSES):
+            for n in FIRST_TILES:
+                w3_pass(n, a)
         for n in FIRST_TILES:
             wr_pass(n, 0)
         for n in FIRST_TILES:
-            wr_pass(n, 1, stop=True)
+            wr_pass(n, 1)
             store(n)
+        for pair in LAST_PAIRS:
+            round_wr(0, pair.start, len(pair), nc.vector.tensor_copy)
+            quantise_wr(0, pair.start, len(pair))
+            for n in pair:
+                round_wr(1, n, 1, nc.vector.tensor_copy)
+            for n in pair:
+                quantise_wr(1, n, 1)
+        for a in range(PASSES):
+            for n in LAST_TILES:
+                w3_pass(n, a)
         for n in LAST_TILES:
-            w3_pass(n, 0)
-        for n in LAST_TILES:
-            w3_pass(n, 1)
-        for n in LAST_TILES:
-            wr_pass(n, 0)
-            wr_pass(n, 1, stop=True)
+            for a in range(PASSES):
+                wr_pass(n, a)
             store(n)

@@ -30,7 +30,9 @@ LAST_TILES = range(TILES // 2, TILES)
 
 LAST_PAIRS = [range(n, n + 2) for n in range(LAST_TILES.start, TILES, 2)]
 W3_ROW0 = 4
-W2_ON_VECTOR = {(0, 0): 128, (1, 0): 48, (0, 1): 128, (1, 1): 0}
+W2_ON_VECTOR = {(0, 0): 128, (1, 0): 48, (0, 1): 128, (1, 1): 48}
+W3_EARLY = range(TILES - 2)
+STORES = [range(n, n + 1) for n in range(8)]
 
 
 def tile_list_ast_slot_block_kernel(
@@ -96,26 +98,36 @@ def tile_list_ast_slot_block_kernel(
         w2_raw = {(b, 0): w2_first[:, :, b * KP : (b + 1) * KP] for b in range(H // KP)}
         for b in range(H // KP):
             w2_raw[b, 1] = load_rows(w2, 1, b * KP, KP, f"w2_raw{b}1")
-        w3_scale = load_scales(w3_scales, W3_ROW0, "w3_scale")
-        w3_code, wr_raw = [], {}
+        w3_code, wr_raw = {}, {}
 
         def load_wr(a, tiles):
             raw = load_rows(wr, a, tiles.start * P, len(tiles) * P, f"wr_raw{a}{tiles.start}")
             for n in tiles:
                 wr_raw[a, n] = (raw, tiles.start)
 
+        def load_w3(passes, tiles):
+            tile = sbuf([P, len(passes), len(tiles) * P], U32, f"w3_code{passes.start}{tiles.start}")
+            words = w3_words.rearrange("a p c i -> p a (c i)").bitcast(I32)
+            words = words[:, passes.start : passes.stop, tiles.start * P : tiles.stop * P]
+            nc.sync.dma_start(tile[:].bitcast(I32), words)
+            for a in passes:
+                for n in tiles:
+                    w3_code[a, n] = tile[:, a - passes.start, (n - tiles.start) * P : (n - tiles.start + 1) * P]
+
+        w3_scale = load_scales(w3_scales, W3_ROW0, "w3_scale")
         for a in range(PASSES):
             load_wr(a, FIRST_TILES)
-            w3_code.append(load_e4m3(w3_words, a, f"w3_code{a}"))
+            load_w3(range(a, a + 1), range(TILES))
         for pair in LAST_PAIRS:
             for a in range(PASSES):
                 load_wr(a, pair)
 
         def order_w1(src, b, dtype, name, reuse=None):
             dst = sbuf([P, PASSES, KP], dtype, f"{name}{b}", reuse)
+            run = 16 // (2 if dtype is U16 else 1)
             nc.vector.tensor_copy(
-                dst[:].rearrange("p a (t m) -> p a m t", t=PACK),
-                src[:, :, b * KP : (b + 1) * KP].rearrange("p a (m t) -> p a m t", t=PACK),
+                dst[:].rearrange("p a (t c i) -> p a c t i", t=PACK, i=run),
+                src[:, :, b * KP : (b + 1) * KP].rearrange("p a (c i t) -> p a c t i", t=PACK, i=run),
             )
             return dst
 
@@ -197,16 +209,79 @@ def tile_list_ast_slot_block_kernel(
                             a == PASSES - 1 and t == PACK - 1,
                         )
 
-        def gate_times_up(b, u):
-            if u == 0:
-                h_bf[b] = sbuf([P, S * PACK], BF16, f"h_bf{b}")
+        def gate_times_up(b, u, reuse=None):
+            if u % 2 == 0:
+                h_bf[b, u // 2] = sbuf([P, S * PACK // 2], BF16, f"h_bf{b}{u}", reuse)
             tokens = slice(u * TOKENS, (u + 1) * TOKENS)
             nc.vector.tensor_tensor(
-                h_bf[b][:, tokens.start * PACK : tokens.stop * PACK].rearrange("p (c i t) -> p c t i", i=LINE, t=PACK),
+                h_bf[b, u // 2][:, u % 2 * KP : (u % 2 + 1) * KP].rearrange("p (c i t) -> p c t i", i=LINE, t=PACK),
                 up[b][u][:].rearrange("p (t c i) -> p c t i", t=PACK, i=LINE),
                 gate[b][:, :, tokens].rearrange("p t (c i) -> p c t i", i=LINE),
                 MULT,
             )
+
+        def quantise_h(b, half, reuse=None):
+            if half == 0:
+                h_q[b] = (sbuf([P, S], U32, f"h_code{b}", reuse), sbuf([P, S], U8, f"h_scale{b}"))
+            code, scale = h_q[b]
+            cols = slice(half * S // 2, (half + 1) * S // 2)
+            nc.vector.quantize_mx(code[:, cols].bitcast(E4M3), scale[:, cols], h_bf[b, half][:])
+
+        wr_bf, wr_q, h_q, total, result = {}, {}, {}, {}, {}
+
+        def round_wr(a, tiles, on_vector):
+            raw, first = wr_raw[a, tiles.start]
+            grouped = sbuf([P, len(tiles) * KP], BF16, f"wr_bf{a}{tiles.start}")
+            src = raw[:, :, (tiles.start - first) * P : (tiles.stop - first) * P]
+            src = src.rearrange("p j (c i) -> p c j i", i=LINE)
+            dst = grouped[:].rearrange("p (c i j) -> p c j i", i=LINE, j=PACK)
+            cut = on_vector // LINE
+            if cut > 0:
+                nc.vector.tensor_copy(dst[:, :cut], src[:, :cut])
+            if on_vector < len(tiles) * P:
+                nc.scalar.copy(dst[:, cut:], src[:, cut:])
+            wr_bf[a, tiles.start] = grouped
+
+        def quantise_wr(a, tiles):
+            code, scale = quantise(wr_bf[a, tiles.start][:], len(tiles) * P, f"wr_{a}{tiles.start}")
+            for i, n in enumerate(tiles):
+                wr_q[a, n] = (code[:, i * P : (i + 1) * P], scale[:, i * P : (i + 1) * P])
+
+        started = set()
+
+        def opens(n):
+            first = n not in started
+            if first:
+                total[n] = bank(n)
+                started.add(n)
+            return first
+
+        def w3_pass(n, a, stop=False):
+            code, scale = h_q[a]
+            start = opens(n)
+            nc.tensor.matmul_mx(
+                total[n][:],
+                lhsT=w3_code[a, n].bitcast(E4M3),
+                lhsT_scale=w3_scale[W3_ROW0:, a * K + n * P : a * K + (n + 1) * P],
+                rhs=code[:].bitcast(E4M3),
+                rhs_scale=scale[:],
+                start=start,
+                stop=stop,
+            )
+
+        def wr_pass(n, a, stop=False):
+            code, scale = wr_q[a, n]
+            start = opens(n)
+            times_v(total[n][:], code.bitcast(E4M3), scale, a, 0, S, start, stop)
+
+        def empty(n, copy):
+            tiles = [group for group in STORES if n in group][0]
+            if n == tiles.start:
+                result[tiles.start] = sbuf([P, len(tiles), S], F32, f"result{n}")
+            copy(result[tiles.start][:, n - tiles.start, :], total[n][:])
+            if n == tiles.stop - 1:
+                rows = out[tiles.start * P : tiles.stop * P, :]
+                nc.sync.dma_start(rows.rearrange("(n p) j -> p n j", p=P), result[tiles.start][:])
 
         w2_q[0, 0] = quantise(round_w2(0, 0)[:], KP, "w2_00")
         late = round_w2(1, 0)
@@ -215,83 +290,49 @@ def tile_list_ast_slot_block_kernel(
         w2_q[1, 0] = quantise(late[:], KP, "w2_10", "w2_bf01")
         w2_q[1, 1] = quantise(round_w2(1, 1)[:], KP, "w2_11")
         second_product(1)
-        h_q = []
-        for b in range(H // KP):
-            for u in range(S // TOKENS):
-                gate_times_up(b, u)
-            h_q.append(quantise(h_bf[b][:], S, f"h_{b}"))
-
-        wr_bf, wr_q = {}, {}
-
-        def round_wr(a, n, count, copy):
-            raw, first = wr_raw[a, n]
-            wr_bf[a, n] = sbuf([P, count * KP], BF16, f"wr_bf{a}{n}")
-            src = raw[:, :, (n - first) * P : (n - first + count) * P]
-            copy(
-                wr_bf[a, n][:].rearrange("p (c i j) -> p c j i", i=LINE, j=PACK),
-                src.rearrange("p j (c i) -> p c j i", i=LINE),
-            )
-
-        def quantise_wr(a, n, count):
-            code, scale = quantise(wr_bf[a, n][:], count * P, f"wr_{a}{n}")
-            for i in range(count):
-                wr_q[a, n + i] = (code[:, i * P : (i + 1) * P], scale[:, i * P : (i + 1) * P])
-
-        half = len(FIRST_TILES) // 2
-        round_wr(0, 0, len(FIRST_TILES), nc.scalar.copy)
-        quantise_wr(0, 0, len(FIRST_TILES))
-        for n in (0, half):
-            round_wr(1, n, half, nc.scalar.copy)
-        for n in (0, half):
-            quantise_wr(1, n, half)
-
-        total = {}
-
-        def w3_pass(n, a):
-            code, scale = h_q[a]
-            if a == 0:
-                total[n] = bank(n)
-            nc.tensor.matmul_mx(
-                total[n][:],
-                lhsT=w3_code[a][:, n * P : (n + 1) * P].bitcast(E4M3),
-                lhsT_scale=w3_scale[W3_ROW0:, a * K + n * P : a * K + (n + 1) * P],
-                rhs=code[:].bitcast(E4M3),
-                rhs_scale=scale[:],
-                start=a == 0,
-                stop=False,
-            )
-
-        def wr_pass(n, a):
-            code, scale = wr_q[a, n]
-            times_v(total[n][:], code.bitcast(E4M3), scale, a, 0, S, False, a == PASSES - 1)
-
-        def store(n):
-            result = sbuf([P, S], F32, f"result{n}")
-            if n == TILES - 1:
-                nc.vector.tensor_copy(result[:], total[n][:])
-            else:
-                nc.scalar.copy(result[:], total[n][:])
-            nc.sync.dma_start(out[n * P : (n + 1) * P, :], result[:])
-
-        for a in range(PASSES):
-            for n in FIRST_TILES:
-                w3_pass(n, a)
+        for u in range(S // TOKENS):
+            gate_times_up(0, u)
+        for half in range(2):
+            quantise_h(0, half)
+        round_wr(0, FIRST_TILES, 0)
+        quantise_wr(0, FIRST_TILES)
+        for u in range(S // TOKENS):
+            gate_times_up(1, u, "wr_bf00" if u == 2 else None)
+        for n in FIRST_TILES:
+            w3_pass(n, 0)
         for n in FIRST_TILES:
             wr_pass(n, 0)
-        for n in FIRST_TILES:
-            wr_pass(n, 1)
-            store(n)
-        for pair in LAST_PAIRS:
-            round_wr(0, pair.start, len(pair), nc.vector.tensor_copy)
-            quantise_wr(0, pair.start, len(pair))
-            for n in pair:
-                round_wr(1, n, 1, nc.vector.tensor_copy)
-            for n in pair:
-                quantise_wr(1, n, 1)
-        for a in range(PASSES):
-            for n in LAST_TILES:
-                w3_pass(n, a)
         for n in LAST_TILES:
-            for a in range(PASSES):
-                wr_pass(n, a)
-            store(n)
+            w3_pass(n, 0)
+        round_wr(1, range(0, 2), 0)
+        round_wr(1, range(2, 4), 0)
+        quantise_wr(1, range(0, 2))
+        quantise_wr(1, range(2, 4))
+        quantise_h(1, 0, "wr_bf10")
+        quantise_h(1, 1)
+        first, second = LAST_PAIRS
+        round_wr(0, first, 0)
+        round_wr(1, first, 2 * P)
+        for n in range(0, 4):
+            wr_pass(n, 1)
+        for n in range(0, 4):
+            w3_pass(n, 1, True)
+            empty(n, nc.scalar.copy)
+        quantise_wr(0, first)
+        quantise_wr(1, first)
+        for n in first:
+            w3_pass(n, 1)
+            wr_pass(n, 0)
+            wr_pass(n, 1, True)
+            empty(n, nc.scalar.copy)
+        round_wr(0, second, 2 * P)
+        quantise_wr(0, second)
+        for n in second:
+            round_wr(1, range(n, n + 1), P)
+        for n in second:
+            quantise_wr(1, range(n, n + 1))
+        for n in second:
+            w3_pass(n, 1)
+            for a in (0, 1) if n == second.start else (1, 0):
+                wr_pass(n, a, a == (n == second.start))
+            empty(n, nc.vector.tensor_copy if n == TILES - 1 else nc.scalar.copy)

@@ -85,6 +85,12 @@ def tile_list_ast_slot_block_kernel(
         for a in range(PASSES):
             nc.vector.tensor_copy(picked_rows[:, a * S : (a + 1) * S], tab_rows[a][:].indirect(offsets[:]))
         v_scale = zeroed(PASSES * S, "v_scale")
+        w3_scale = zeroed(K, "w3_scale")
+        for d in range(QUADS):
+            nc.gpsimd.dma_start(
+                w3_scale[:].bitcast(I32)[d * QUAD + W3_ROW0 : d * QUAD + W3_ROW0 + PASSES * 4, :],
+                w3_scales.bitcast(I32)[:, 4 * d : 4 * d + 4, :],
+            )
 
         tab = [load_e4m3(tab_words, 0, "tab0")]
         w1_rows = load_scales(w1_scales, 0, "w1_rows")
@@ -114,13 +120,13 @@ def tile_list_ast_slot_block_kernel(
                 for n in tiles:
                     w3_code[a, n] = tile[:, a - passes.start, (n - tiles.start) * P : (n - tiles.start + 1) * P]
 
-        w3_scale = load_scales(w3_scales, W3_ROW0, "w3_scale")
         for a in range(PASSES):
             load_wr(a, FIRST_TILES)
-            load_w3(range(a, a + 1), range(TILES))
+            load_w3(range(a, a + 1), range(TILES - 2 * a))
         for pair in LAST_PAIRS:
             for a in range(PASSES):
                 load_wr(a, pair)
+        load_w3(range(1, 2), LAST_PAIRS[1])
 
         def order_w1(src, b, dtype, name, reuse=None):
             dst = sbuf([P, PASSES, KP], dtype, f"{name}{b}", reuse)
@@ -262,7 +268,7 @@ def tile_list_ast_slot_block_kernel(
             nc.tensor.matmul_mx(
                 total[n][:],
                 lhsT=w3_code[a, n].bitcast(E4M3),
-                lhsT_scale=w3_scale[W3_ROW0:, a * K + n * P : a * K + (n + 1) * P],
+                lhsT_scale=w3_scale[W3_ROW0 + 4 * a :, n * P : (n + 1) * P],
                 rhs=code[:].bitcast(E4M3),
                 rhs_scale=scale[:],
                 start=start,
@@ -332,7 +338,9 @@ def tile_list_ast_slot_block_kernel(
         for n in second:
             quantise_wr(1, range(n, n + 1))
         for n in second:
+            wr_pass(n, 0)
+        for n in second:
             w3_pass(n, 1)
-            for a in (0, 1) if n == second.start else (1, 0):
-                wr_pass(n, a, a == (n == second.start))
+        for n in second:
+            wr_pass(n, 1, True)
             empty(n, nc.vector.tensor_copy if n == TILES - 1 else nc.scalar.copy)

@@ -22,17 +22,18 @@ KP = P * PACK
 PASSES = K // KP
 QUADS = 4
 QUAD = P // QUADS
-LINE = 4
+ROWS = 4
+LINE_BYTES = 16
+LINE = LINE_BYTES // 4
 TOKENS = S // PACK
+HALF = S // 2
 TILES = K // P
 FIRST_TILES = range(TILES // 2)
 LAST_TILES = range(TILES // 2, TILES)
-
+FIRST_PAIRS = [range(n, n + 2) for n in range(0, FIRST_TILES.stop, 2)]
 LAST_PAIRS = [range(n, n + 2) for n in range(LAST_TILES.start, TILES, 2)]
 W3_ROW0 = 4
-W2_ON_VECTOR = {(0, 0): 128, (1, 0): 48, (0, 1): 128, (1, 1): 48}
-W3_EARLY = range(TILES - 2)
-STORES = [range(n, n + 1) for n in range(8)]
+W2_ON_VECTOR = {(0, 0): 128, (1, 0): 128, (0, 1): 80, (1, 1): 64}
 
 
 def tile_list_ast_slot_block_kernel(
@@ -67,7 +68,7 @@ def tile_list_ast_slot_block_kernel(
 
         def load_scales(scales, row0, name):
             tile = zeroed(PASSES * scales.shape[2], name)
-            for r in range(QUADS):
+            for r in range(ROWS):
                 nc.sync.dma_start(
                     tile[:].bitcast(I32).rearrange("p (a c) -> p a c", a=PASSES)[row0 + r : P : QUAD],
                     scales.bitcast(I32).rearrange("a (d r) c -> r d a c", d=QUADS)[r],
@@ -78,19 +79,12 @@ def tile_list_ast_slot_block_kernel(
         w1_raw = sbuf([P, PASSES, H], U16, "w1_raw")
         nc.sync.dma_start(w1_raw[:, 0, :].bitcast(I32), w1_words[0].bitcast(I32))
         nc.sync.dma_start(offsets[:], offs)
-        tab_rows = [zeroed(T, f"tab_rows{a}") for a in range(PASSES)]
-        for a in range(PASSES):
-            nc.sync.dma_start(tab_rows[a][:].bitcast(I32)[0:P:8, :], tab_scales[a].bitcast(I32))
-        picked_rows = sbuf([P, PASSES * S], U8, "picked_rows")
-        for a in range(PASSES):
-            nc.vector.tensor_copy(picked_rows[:, a * S : (a + 1) * S], tab_rows[a][:].indirect(offsets[:]))
+        step = P // (PASSES * QUADS * ROWS)
+        tab_rows = zeroed(T, "tab_rows")
+        nc.sync.dma_start(tab_rows[:].bitcast(I32)[0:P:step, :], tab_scales.bitcast(I32).rearrange("a s c -> s a c"))
+        picked_rows = sbuf([P, S], U8, "picked_rows")
+        nc.vector.tensor_copy(picked_rows[:], tab_rows[:].indirect(offsets[:]))
         v_scale = zeroed(PASSES * S, "v_scale")
-        w3_scale = zeroed(K, "w3_scale")
-        for d in range(QUADS):
-            nc.gpsimd.dma_start(
-                w3_scale[:].bitcast(I32)[d * QUAD + W3_ROW0 : d * QUAD + W3_ROW0 + PASSES * 4, :],
-                w3_scales.bitcast(I32)[:, 4 * d : 4 * d + 4, :],
-            )
 
         tab = [load_e4m3(tab_words, 0, "tab0")]
         w1_rows = load_scales(w1_scales, 0, "w1_rows")
@@ -98,12 +92,16 @@ def tile_list_ast_slot_block_kernel(
         tab.append(load_e4m3(tab_words, 1, "tab1"))
         bias = sbuf([P, H // KP, PACK], F32, "bias")
         nc.sync.dma_start(bias[:], b1.rearrange("(b p t) -> p b t", p=P, t=PACK))
-        for r in range(QUADS):
-            nc.sync.dma_start(v_scale[:].bitcast(I32)[r:P:QUAD, :], picked_rows[:].bitcast(I32)[8 * r : P : QUAD, :])
-        w2_first = load_rows(w2, 0, 0, H, "w2_raw0")
-        w2_raw = {(b, 0): w2_first[:, :, b * KP : (b + 1) * KP] for b in range(H // KP)}
-        for b in range(H // KP):
-            w2_raw[b, 1] = load_rows(w2, 1, b * KP, KP, f"w2_raw{b}1")
+        for d in (0, 2, 1, 3):
+            nc.sync.dma_start(
+                v_scale[:].bitcast(I32)[d * QUAD : d * QUAD + ROWS, :],
+                picked_rows[:].bitcast(I32)[d * QUAD : (d + 1) * QUAD : step, :],
+            )
+        w2_raw = {}
+        for a in range(PASSES):
+            whole = load_rows(w2, a, 0, H, f"w2_raw{a}")
+            for b in range(H // KP):
+                w2_raw[b, a] = whole[:, :, b * KP : (b + 1) * KP]
         w3_code, wr_raw = {}, {}
 
         def load_wr(a, tiles):
@@ -111,26 +109,25 @@ def tile_list_ast_slot_block_kernel(
             for n in tiles:
                 wr_raw[a, n] = (raw, tiles.start)
 
-        def load_w3(passes, tiles):
-            tile = sbuf([P, len(passes), len(tiles) * P], U32, f"w3_code{passes.start}{tiles.start}")
-            words = w3_words.rearrange("a p c i -> p a (c i)").bitcast(I32)
-            words = words[:, passes.start : passes.stop, tiles.start * P : tiles.stop * P]
-            nc.sync.dma_start(tile[:].bitcast(I32), words)
-            for a in passes:
-                for n in tiles:
-                    w3_code[a, n] = tile[:, a - passes.start, (n - tiles.start) * P : (n - tiles.start + 1) * P]
+        def load_w3(a, tiles):
+            tile = sbuf([P, len(tiles) * P], U32, f"w3_code{a}{tiles.start}")
+            words = w3_words[a].rearrange("p c i -> p (c i)").bitcast(I32)
+            nc.sync.dma_start(tile[:].bitcast(I32), words[:, tiles.start * P : tiles.stop * P])
+            for n in tiles:
+                w3_code[a, n] = tile[:, (n - tiles.start) * P : (n - tiles.start + 1) * P]
 
-        for a in range(PASSES):
-            load_wr(a, FIRST_TILES)
-            load_w3(range(a, a + 1), range(TILES - 2 * a))
+        load_wr(0, FIRST_TILES)
+        w3_scale = load_scales(w3_scales, W3_ROW0, "w3_scale")
+        load_w3(0, range(TILES))
+        load_wr(1, FIRST_TILES)
+        load_w3(1, range(LAST_PAIRS[-1].start))
         for pair in LAST_PAIRS:
             for a in range(PASSES):
                 load_wr(a, pair)
-        load_w3(range(1, 2), LAST_PAIRS[1])
+        load_w3(1, LAST_PAIRS[-1])
 
-        def order_w1(src, b, dtype, name, reuse=None):
+        def order_w1(src, b, dtype, run, name, reuse=None):
             dst = sbuf([P, PASSES, KP], dtype, f"{name}{b}", reuse)
-            run = 16 // (2 if dtype is U16 else 1)
             nc.vector.tensor_copy(
                 dst[:].rearrange("p a (t c i) -> p a c t i", t=PACK, i=run),
                 src[:, :, b * KP : (b + 1) * KP].rearrange("p a (c i t) -> p a c t i", t=PACK, i=run),
@@ -143,12 +140,12 @@ def tile_list_ast_slot_block_kernel(
             return picked
 
         v_code = [gather_words(0)]
-        w1_code = [order_w1(w1_raw[:], 0, U16, "w1_code", "tab_rows1")]
+        w1_code = [order_w1(w1_raw[:], 0, U16, LINE_BYTES // 2, "w1_code", "tab_rows")]
         w1_planes = w1_rows[:].rearrange("p (a c) -> p a c", a=PASSES)
-        w1_scale = [order_w1(w1_planes, 0, U8, "w1_scale")]
+        w1_scale = [order_w1(w1_planes, 0, U8, LINE_BYTES, "w1_scale")]
         v_code.append(gather_words(1))
-        w1_code.append(order_w1(w1_raw[:], 1, U16, "w1_code", "tab1"))
-        w1_scale.append(order_w1(w1_planes, 1, U8, "w1_scale", "w1_raw"))
+        w1_code.append(order_w1(w1_raw[:], 1, U16, LINE_BYTES // 2, "w1_code", "tab1"))
+        w1_scale.append(order_w1(w1_planes, 1, U8, LINE_BYTES, "w1_scale", "w1_raw"))
 
         def times_v(acc, code, scale, a, j0, width, start, stop):
             nc.tensor.matmul_mx(
@@ -190,13 +187,12 @@ def tile_list_ast_slot_block_kernel(
             grouped = sbuf([P, KP * PACK], BF16, f"w2_bf{b}{a}")
             dst = grouped[:].rearrange("p (t m j) -> p m j t", t=PACK, j=PACK)
             src = w2_raw[b, a].rearrange("p j (m t) -> p m j t", t=PACK)
-            if on_vector > 0:
-                nc.vector.tensor_copy(dst[:, :on_vector], src[:, :on_vector])
+            nc.vector.tensor_copy(dst[:, :on_vector], src[:, :on_vector])
             if on_vector < P:
                 nc.scalar.copy(dst[:, on_vector:], src[:, on_vector:])
             return grouped
 
-        w2_q, up, h_bf = {}, {}, {}
+        w2_q, up, h_bf, h_q = {}, {}, {}, {}
 
         def second_product(b):
             up[b] = [bank(PACK * b + u) for u in range(S // TOKENS)]
@@ -216,11 +212,13 @@ def tile_list_ast_slot_block_kernel(
                         )
 
         def gate_times_up(b, u, reuse=None):
-            if u % 2 == 0:
-                h_bf[b, u // 2] = sbuf([P, S * PACK // 2], BF16, f"h_bf{b}{u}", reuse)
+            half, part = divmod(u, HALF // TOKENS)
+            if part == 0:
+                h_bf[b, half] = sbuf([P, HALF * PACK], BF16, f"h_bf{b}{half}", reuse)
             tokens = slice(u * TOKENS, (u + 1) * TOKENS)
+            dst = h_bf[b, half][:, part * TOKENS * PACK : (part + 1) * TOKENS * PACK]
             nc.vector.tensor_tensor(
-                h_bf[b, u // 2][:, u % 2 * KP : (u % 2 + 1) * KP].rearrange("p (c i t) -> p c t i", i=LINE, t=PACK),
+                dst.rearrange("p (c i t) -> p c t i", i=LINE, t=PACK),
                 up[b][u][:].rearrange("p (t c i) -> p c t i", t=PACK, i=LINE),
                 gate[b][:, :, tokens].rearrange("p t (c i) -> p c t i", i=LINE),
                 MULT,
@@ -230,117 +228,101 @@ def tile_list_ast_slot_block_kernel(
             if half == 0:
                 h_q[b] = (sbuf([P, S], U32, f"h_code{b}", reuse), sbuf([P, S], U8, f"h_scale{b}"))
             code, scale = h_q[b]
-            cols = slice(half * S // 2, (half + 1) * S // 2)
+            cols = slice(half * HALF, (half + 1) * HALF)
             nc.vector.quantize_mx(code[:, cols].bitcast(E4M3), scale[:, cols], h_bf[b, half][:])
 
-        wr_bf, wr_q, h_q, total, result = {}, {}, {}, {}, {}
+        wr_bf, wr_q, total = {}, {}, {}
 
-        def round_wr(a, tiles, on_vector):
+        def round_wr(a, tiles, copy):
             raw, first = wr_raw[a, tiles.start]
-            grouped = sbuf([P, len(tiles) * KP], BF16, f"wr_bf{a}{tiles.start}")
+            wr_bf[a, tiles.start] = sbuf([P, len(tiles) * KP], BF16, f"wr_bf{a}{tiles.start}")
             src = raw[:, :, (tiles.start - first) * P : (tiles.stop - first) * P]
-            src = src.rearrange("p j (c i) -> p c j i", i=LINE)
-            dst = grouped[:].rearrange("p (c i j) -> p c j i", i=LINE, j=PACK)
-            cut = on_vector // LINE
-            if cut > 0:
-                nc.vector.tensor_copy(dst[:, :cut], src[:, :cut])
-            if on_vector < len(tiles) * P:
-                nc.scalar.copy(dst[:, cut:], src[:, cut:])
-            wr_bf[a, tiles.start] = grouped
+            copy(
+                wr_bf[a, tiles.start][:].rearrange("p (c i j) -> p c j i", i=LINE, j=PACK),
+                src.rearrange("p j (c i) -> p c j i", i=LINE),
+            )
 
         def quantise_wr(a, tiles):
             code, scale = quantise(wr_bf[a, tiles.start][:], len(tiles) * P, f"wr_{a}{tiles.start}")
             for i, n in enumerate(tiles):
                 wr_q[a, n] = (code[:, i * P : (i + 1) * P], scale[:, i * P : (i + 1) * P])
 
-        started = set()
-
-        def opens(n):
-            first = n not in started
-            if first:
-                total[n] = bank(n)
-                started.add(n)
-            return first
-
         def w3_pass(n, a, stop=False):
             code, scale = h_q[a]
-            start = opens(n)
+            if a == 0:
+                total[n] = bank(n)
             nc.tensor.matmul_mx(
                 total[n][:],
                 lhsT=w3_code[a, n].bitcast(E4M3),
-                lhsT_scale=w3_scale[W3_ROW0 + 4 * a :, n * P : (n + 1) * P],
+                lhsT_scale=w3_scale[W3_ROW0:, a * K + n * P : a * K + (n + 1) * P],
                 rhs=code[:].bitcast(E4M3),
                 rhs_scale=scale[:],
-                start=start,
+                start=a == 0,
                 stop=stop,
             )
 
         def wr_pass(n, a, stop=False):
             code, scale = wr_q[a, n]
-            start = opens(n)
-            times_v(total[n][:], code.bitcast(E4M3), scale, a, 0, S, start, stop)
+            times_v(total[n][:], code.bitcast(E4M3), scale, a, 0, S, False, stop)
 
-        def empty(n, copy):
-            tiles = [group for group in STORES if n in group][0]
-            if n == tiles.start:
-                result[tiles.start] = sbuf([P, len(tiles), S], F32, f"result{n}")
-            copy(result[tiles.start][:, n - tiles.start, :], total[n][:])
-            if n == tiles.stop - 1:
-                rows = out[tiles.start * P : tiles.stop * P, :]
-                nc.sync.dma_start(rows.rearrange("(n p) j -> p n j", p=P), result[tiles.start][:])
+        def store(n, copy):
+            result = sbuf([P, S], F32, f"result{n}")
+            copy(result[:], total[n][:])
+            nc.sync.dma_start(out[n * P : (n + 1) * P, :], result[:])
 
-        w2_q[0, 0] = quantise(round_w2(0, 0)[:], KP, "w2_00")
-        late = round_w2(1, 0)
-        w2_q[0, 1] = quantise(round_w2(0, 1)[:], KP, "w2_01")
+        for b, a in ((0, 0), (1, 0), (0, 1)):
+            w2_q[b, a] = quantise(round_w2(b, a)[:], KP, f"w2_{b}{a}")
         second_product(0)
-        w2_q[1, 0] = quantise(late[:], KP, "w2_10", "w2_bf01")
         w2_q[1, 1] = quantise(round_w2(1, 1)[:], KP, "w2_11")
         second_product(1)
         for u in range(S // TOKENS):
             gate_times_up(0, u)
-        for half in range(2):
+        for half in range(S // HALF):
             quantise_h(0, half)
-        round_wr(0, FIRST_TILES, 0)
+        round_wr(0, FIRST_TILES, nc.scalar.copy)
         quantise_wr(0, FIRST_TILES)
         for u in range(S // TOKENS):
-            gate_times_up(1, u, "wr_bf00" if u == 2 else None)
+            gate_times_up(1, u, "wr_bf00" if u == HALF // TOKENS else None)
         for n in FIRST_TILES:
             w3_pass(n, 0)
         for n in FIRST_TILES:
             wr_pass(n, 0)
         for n in LAST_TILES:
             w3_pass(n, 0)
-        round_wr(1, range(0, 2), 0)
-        round_wr(1, range(2, 4), 0)
-        quantise_wr(1, range(0, 2))
-        quantise_wr(1, range(2, 4))
+        for pair in FIRST_PAIRS:
+            round_wr(1, pair, nc.scalar.copy)
+        for pair in FIRST_PAIRS:
+            quantise_wr(1, pair)
         quantise_h(1, 0, "wr_bf10")
         quantise_h(1, 1)
-        first, second = LAST_PAIRS
-        round_wr(0, first, 0)
-        round_wr(1, first, 2 * P)
-        for n in range(0, 4):
+
+        third, fourth = LAST_PAIRS
+        round_wr(0, third, nc.scalar.copy)
+        round_wr(1, third, nc.vector.tensor_copy)
+        for n in FIRST_TILES:
             wr_pass(n, 1)
-        for n in range(0, 4):
+        for n in FIRST_TILES:
             w3_pass(n, 1, True)
-            empty(n, nc.scalar.copy)
-        quantise_wr(0, first)
-        quantise_wr(1, first)
-        for n in first:
+            store(n, nc.scalar.copy)
+        for a in range(PASSES):
+            quantise_wr(a, third)
+        for n in third:
             w3_pass(n, 1)
             wr_pass(n, 0)
             wr_pass(n, 1, True)
-            empty(n, nc.scalar.copy)
-        round_wr(0, second, 2 * P)
-        quantise_wr(0, second)
-        for n in second:
-            round_wr(1, range(n, n + 1), P)
-        for n in second:
+            store(n, nc.scalar.copy)
+        round_wr(0, fourth, nc.vector.tensor_copy)
+        quantise_wr(0, fourth)
+        for n in fourth:
+            round_wr(1, range(n, n + 1), nc.vector.tensor_copy)
+        for n in fourth:
             quantise_wr(1, range(n, n + 1))
-        for n in second:
+        for n in fourth:
             wr_pass(n, 0)
-        for n in second:
-            w3_pass(n, 1)
-        for n in second:
-            wr_pass(n, 1, True)
-            empty(n, nc.vector.tensor_copy if n == TILES - 1 else nc.scalar.copy)
+        before_last, last = fourth
+        w3_pass(before_last, 1)
+        wr_pass(before_last, 1, True)
+        store(before_last, nc.scalar.copy)
+        wr_pass(last, 1)
+        w3_pass(last, 1, True)
+        store(last, nc.vector.tensor_copy)

@@ -20,9 +20,10 @@ P = 128
 PACK = 4
 KP = P * PACK
 PASSES = K // KP
-QUADS = 4
-QUAD = P // QUADS
+GROUPS = H // KP
+QUAD = 32
 ROWS = 4
+BLOCK = 8
 LINE_BYTES = 16
 LINE = LINE_BYTES // 4
 TOKENS = S // PACK
@@ -30,10 +31,8 @@ HALF = S // 2
 TILES = K // P
 FIRST_TILES = range(TILES // 2)
 LAST_TILES = range(TILES // 2, TILES)
-FIRST_PAIRS = [range(n, n + 2) for n in range(0, FIRST_TILES.stop, 2)]
-LAST_PAIRS = [range(n, n + 2) for n in range(LAST_TILES.start, TILES, 2)]
+PAIRS = [range(n, n + 2) for n in range(0, TILES, 2)]
 W3_ROW0 = 4
-W2_ON_VECTOR = {(0, 0): 128, (1, 0): 128, (0, 1): 80, (1, 1): 64}
 
 
 def tile_list_ast_slot_block_kernel(
@@ -45,67 +44,67 @@ def tile_list_ast_slot_block_kernel(
         psum = ctx.enter_context(tc.psum_pool(name="psum", bufs=1))
 
         def sbuf(shape, dtype, name, reuse=None):
-            return keep.tile(shape, dtype, name=name, tag=reuse or name, align_bytes=64)
+            return keep.tile(shape, dtype, name=name, tag=reuse or name, align_bytes=256)
 
         def bank(n):
             return psum.tile([P, S], F32, name=f"bank{n}")
 
-        def zeroed(width, name):
-            tile = sbuf([P, width], U8, name)
-            nc.vector.memset(tile[:].bitcast(I32), 0)
-            return tile
-
-        def load_e4m3(words, a, name):
-            tile = sbuf([P, words.shape[2]], U32, name)
-            nc.sync.dma_start(tile[:].bitcast(I32), words[a].rearrange("p c i -> p (c i)").bitcast(I32))
-            return tile
-
-        def load_rows(w, a, c0, width, name):
-            raw = sbuf([P, PACK, width], F32, name)
-            rows = w[a * KP : (a + 1) * KP, c0 : c0 + width]
+        def load_rows(w, a, cols, name):
+            raw = sbuf([P, PACK, len(cols)], F32, name)
+            rows = w[a * KP : (a + 1) * KP, cols.start : cols.stop]
             nc.sync.dma_start(raw[:], rows.rearrange("(p j) c -> p j c", j=PACK))
             return raw[:]
 
-        def load_scales(scales, row0, name):
-            tile = zeroed(PASSES * scales.shape[2], name)
-            for r in range(ROWS):
-                nc.sync.dma_start(
-                    tile[:].bitcast(I32).rearrange("p (a c) -> p a c", a=PASSES)[row0 + r : P : QUAD],
-                    scales.bitcast(I32).rearrange("a (d r) c -> r d a c", d=QUADS)[r],
-                )
-            return tile
-
-        offsets = keep.tile([P, S // 16], U16, name="offsets")
         w1_raw = sbuf([P, PASSES, H], U16, "w1_raw")
         nc.sync.dma_start(w1_raw[:, 0, :].bitcast(I32), w1_words[0].bitcast(I32))
+        offsets = keep.tile([P, S // 16], U16, name="offsets")
         nc.sync.dma_start(offsets[:], offs)
-        step = P // (PASSES * QUADS * ROWS)
-        tab_rows = zeroed(T, "tab_rows")
+        step = P // (PASSES * ROWS * ROWS)
+        tab_rows = sbuf([P, T], U8, "tab_rows")
+        nc.vector.memset(tab_rows[:].bitcast(I32), 0)
         nc.sync.dma_start(tab_rows[:].bitcast(I32)[0:P:step, :], tab_scales.bitcast(I32).rearrange("a s c -> s a c"))
         picked_rows = sbuf([P, S], U8, "picked_rows")
         nc.vector.tensor_copy(picked_rows[:], tab_rows[:].indirect(offsets[:]))
-        v_scale = zeroed(PASSES * S, "v_scale")
+        v_scale = sbuf([P, PASSES * S], U8, "v_scale")
+        nc.vector.memset(v_scale[:].bitcast(I32), 0)
 
-        tab = [load_e4m3(tab_words, 0, "tab0")]
-        w1_rows = load_scales(w1_scales, 0, "w1_rows")
+        def load_scales(scales, row0, name):
+            tile = sbuf([P, PASSES * scales.shape[2]], U8, name)
+            nc.vector.memset(tile[:].bitcast(I32), 0)
+            for r in range(ROWS):
+                nc.sync.dma_start(
+                    tile[:].bitcast(I32).rearrange("p (a c) -> p a c", a=PASSES)[row0 + r : P : QUAD],
+                    scales.bitcast(I32).rearrange("a (d r) c -> r d a c", r=ROWS)[r],
+                )
+            return tile
+
+        def load_table(a):
+            tile = sbuf([P, T], U32, f"tab{a}")
+            nc.sync.dma_start(tile[:].bitcast(I32), tab_words[a].rearrange("p c i -> p (c i)").bitcast(I32))
+            return tile
+
+        tab = [load_table(0)]
+        w1_rows = load_scales(w1_scales, 0, "w1_rows")[:].rearrange("p (a c) -> p a c", a=PASSES)
         nc.sync.dma_start(w1_raw[:, 1, :].bitcast(I32), w1_words[1].bitcast(I32))
-        tab.append(load_e4m3(tab_words, 1, "tab1"))
-        bias = sbuf([P, H // KP, PACK], F32, "bias")
+        tab.append(load_table(1))
+        bias = sbuf([P, GROUPS, PACK], F32, "bias")
         nc.sync.dma_start(bias[:], b1.rearrange("(b p t) -> p b t", p=P, t=PACK))
+
         for d in (0, 2, 1, 3):
             nc.sync.dma_start(
                 v_scale[:].bitcast(I32)[d * QUAD : d * QUAD + ROWS, :],
                 picked_rows[:].bitcast(I32)[d * QUAD : (d + 1) * QUAD : step, :],
             )
+
         w2_raw = {}
         for a in range(PASSES):
-            whole = load_rows(w2, a, 0, H, f"w2_raw{a}")
-            for b in range(H // KP):
+            whole = load_rows(w2, a, range(H), f"w2_raw{a}")
+            for b in range(GROUPS):
                 w2_raw[b, a] = whole[:, :, b * KP : (b + 1) * KP]
-        w3_code, wr_raw = {}, {}
+        wr_raw, w3_code = {}, {}
 
         def load_wr(a, tiles):
-            raw = load_rows(wr, a, tiles.start * P, len(tiles) * P, f"wr_raw{a}{tiles.start}")
+            raw = load_rows(wr, a, range(tiles.start * P, tiles.stop * P), f"wr_raw{a}{tiles.start}")
             for n in tiles:
                 wr_raw[a, n] = (raw, tiles.start)
 
@@ -120,32 +119,35 @@ def tile_list_ast_slot_block_kernel(
         w3_scale = load_scales(w3_scales, W3_ROW0, "w3_scale")
         load_w3(0, range(TILES))
         load_wr(1, FIRST_TILES)
-        load_w3(1, range(LAST_PAIRS[-1].start))
-        for pair in LAST_PAIRS:
+        load_w3(1, range(PAIRS[3].start))
+        for pair in PAIRS[2:]:
             for a in range(PASSES):
                 load_wr(a, pair)
-        load_w3(1, LAST_PAIRS[-1])
+        load_w3(1, PAIRS[3])
 
-        def order_w1(src, b, dtype, run, name, reuse=None):
-            dst = sbuf([P, PASSES, KP], dtype, f"{name}{b}", reuse)
-            nc.vector.tensor_copy(
-                dst[:].rearrange("p a (t c i) -> p a c t i", t=PACK, i=run),
-                src[:, :, b * KP : (b + 1) * KP].rearrange("p a (c i t) -> p a c t i", t=PACK, i=run),
+        run = LINE_BYTES // 2
+        w1_code = sbuf([P, PASSES, H], U16, "w1_code")
+        for a in range(PASSES):
+            nc.scalar.copy(
+                w1_code[:, a, :].rearrange("p (b t c i) -> p b c t i", t=PACK, i=run, b=GROUPS),
+                w1_raw[:, a, :].rearrange("p (b c i t) -> p b c t i", t=PACK, i=run, b=GROUPS),
             )
-            return dst
-
         def gather_words(a):
             picked = sbuf([P, S], U32, f"v_code{a}")
             nc.vector.tensor_copy(picked[:], tab[a][:].indirect(offsets[:]))
             return picked
 
+        def order_w1_scale(b):
+            tile = sbuf([P, PASSES, KP], U8, f"w1_scale{b}")
+            nc.vector.tensor_copy(
+                tile[:].rearrange("p a (t c i) -> p a c t i", t=PACK, i=LINE_BYTES),
+                w1_rows[:, :, b * KP : (b + 1) * KP].rearrange("p a (c i t) -> p a c t i", t=PACK, i=LINE_BYTES),
+            )
+            return tile
+
         v_code = [gather_words(0)]
-        w1_code = [order_w1(w1_raw[:], 0, U16, LINE_BYTES // 2, "w1_code", "tab_rows")]
-        w1_planes = w1_rows[:].rearrange("p (a c) -> p a c", a=PASSES)
-        w1_scale = [order_w1(w1_planes, 0, U8, LINE_BYTES, "w1_scale")]
+        w1_scale = [order_w1_scale(b) for b in range(GROUPS)]
         v_code.append(gather_words(1))
-        w1_code.append(order_w1(w1_raw[:], 1, U16, LINE_BYTES // 2, "w1_code", "tab1"))
-        w1_scale.append(order_w1(w1_planes, 1, U8, LINE_BYTES, "w1_scale", "w1_raw"))
 
         def times_v(acc, code, scale, a, j0, width, start, stop):
             nc.tensor.matmul_mx(
@@ -158,23 +160,17 @@ def tile_list_ast_slot_block_kernel(
                 stop=stop,
             )
 
-        pre, gate = {}, {}
+        gate = {}
 
-        def first_pass(b, t, a):
-            if a == 0:
-                pre[b, t] = bank(PACK * b + t)
-            cols = slice(t * P, (t + 1) * P)
-            last = a == PASSES - 1
-            times_v(pre[b, t][:], w1_code[b][:, a, cols].bitcast(E2M1), w1_scale[b][:, a, cols], a, 0, S, a == 0, last)
-            if last:
-                if t == 0:
-                    gate[b] = sbuf([P, PACK, S], F32, f"gate{b}")
-                nc.scalar.activation(gate[b][:, t, :], pre[b, t][:], GELU, bias=bias[:, b, t : t + 1])
-
-        for b in range(H // KP):
+        def first_product(b):
+            gate[b] = sbuf([P, PACK, S], F32, f"gate{b}")
             for t in range(PACK):
+                pre = bank(PACK * b + t)
+                c0 = b * KP + t * P
                 for a in range(PASSES):
-                    first_pass(b, t, a)
+                    scale = w1_scale[b][:, a, t * P : (t + 1) * P]
+                    times_v(pre[:], w1_code[:, a, c0 : c0 + P].bitcast(E2M1), scale, a, 0, S, a == 0, a == PASSES - 1)
+                nc.scalar.activation(gate[b][:, t, :], pre[:], GELU, bias=bias[:, b, t : t + 1])
 
         def quantise(grouped, width, name, reuse=None):
             code = sbuf([P, width], U32, name + "_code", reuse)
@@ -182,34 +178,33 @@ def tile_list_ast_slot_block_kernel(
             nc.vector.quantize_mx(code[:].bitcast(E4M3), scale[:], grouped)
             return code, scale
 
-        def round_w2(b, a):
-            on_vector = W2_ON_VECTOR[b, a]
-            grouped = sbuf([P, KP * PACK], BF16, f"w2_bf{b}{a}")
-            dst = grouped[:].rearrange("p (t m j) -> p m j t", t=PACK, j=PACK)
+        w2_bf, w2_q, up, h_bf, h_q = {}, {}, {}, {}, {}
+
+        def round_w2(b, a, copy, m0=0, m1=P):
+            if m0 == 0:
+                w2_bf[b, a] = sbuf([P, KP * PACK], BF16, f"w2_bf{b}{a}")
+            dst = w2_bf[b, a][:].rearrange("p (t m j) -> p m j t", t=PACK, j=PACK)
             src = w2_raw[b, a].rearrange("p j (m t) -> p m j t", t=PACK)
-            nc.vector.tensor_copy(dst[:, :on_vector], src[:, :on_vector])
-            if on_vector < P:
-                nc.scalar.copy(dst[:, on_vector:], src[:, on_vector:])
-            return grouped
+            copy(dst[:, m0:m1], src[:, m0:m1])
 
-        w2_q, up, h_bf, h_q = {}, {}, {}, {}
+        def quantise_w2(b, a):
+            w2_q[b, a] = quantise(w2_bf[b, a][:], KP, f"w2_{b}{a}")
 
-        def second_product(b):
-            up[b] = [bank(PACK * b + u) for u in range(S // TOKENS)]
-            for u in range(S // TOKENS):
-                for a in range(PASSES):
-                    code, scale = w2_q[b, a]
-                    for t in range(PACK):
-                        times_v(
-                            up[b][u][:, t * TOKENS : (t + 1) * TOKENS],
-                            code[:, t * P : (t + 1) * P].bitcast(E4M3),
-                            scale[:, t * P : (t + 1) * P],
-                            a,
-                            u * TOKENS,
-                            TOKENS,
-                            a == 0 and t == 0,
-                            a == PASSES - 1 and t == PACK - 1,
-                        )
+        def second_pass(b, a, u):
+            if a == 0:
+                up[b, u] = bank(PACK * b + u)
+            code, scale = w2_q[b, a]
+            for t in range(PACK):
+                times_v(
+                    up[b, u][:, t * TOKENS : (t + 1) * TOKENS],
+                    code[:, t * P : (t + 1) * P].bitcast(E4M3),
+                    scale[:, t * P : (t + 1) * P],
+                    a,
+                    u * TOKENS,
+                    TOKENS,
+                    a == 0 and t == 0,
+                    a == PASSES - 1 and t == PACK - 1,
+                )
 
         def gate_times_up(b, u, reuse=None):
             half, part = divmod(u, HALF // TOKENS)
@@ -219,7 +214,7 @@ def tile_list_ast_slot_block_kernel(
             dst = h_bf[b, half][:, part * TOKENS * PACK : (part + 1) * TOKENS * PACK]
             nc.vector.tensor_tensor(
                 dst.rearrange("p (c i t) -> p c t i", i=LINE, t=PACK),
-                up[b][u][:].rearrange("p (t c i) -> p c t i", t=PACK, i=LINE),
+                up[b, u][:].rearrange("p (t c i) -> p c t i", t=PACK, i=LINE),
                 gate[b][:, :, tokens].rearrange("p t (c i) -> p c t i", i=LINE),
                 MULT,
             )
@@ -231,98 +226,137 @@ def tile_list_ast_slot_block_kernel(
             cols = slice(half * HALF, (half + 1) * HALF)
             nc.vector.quantize_mx(code[:, cols].bitcast(E4M3), scale[:, cols], h_bf[b, half][:])
 
-        wr_bf, wr_q, total = {}, {}, {}
+        wr_bf, wr_q, total, done = {}, {}, {}, {}
 
-        def round_wr(a, tiles, copy):
+        def round_wr(a, tiles, copy, reuse=None):
             raw, first = wr_raw[a, tiles.start]
-            wr_bf[a, tiles.start] = sbuf([P, len(tiles) * KP], BF16, f"wr_bf{a}{tiles.start}")
+            wr_bf[a, tiles.start] = sbuf([P, len(tiles) * KP], BF16, f"wr_bf{a}{tiles.start}", reuse)
             src = raw[:, :, (tiles.start - first) * P : (tiles.stop - first) * P]
             copy(
                 wr_bf[a, tiles.start][:].rearrange("p (c i j) -> p c j i", i=LINE, j=PACK),
                 src.rearrange("p j (c i) -> p c j i", i=LINE),
             )
 
-        def quantise_wr(a, tiles):
-            code, scale = quantise(wr_bf[a, tiles.start][:], len(tiles) * P, f"wr_{a}{tiles.start}")
+        def quantise_wr(a, tiles, reuse=None):
+            code, scale = quantise(wr_bf[a, tiles.start][:], len(tiles) * P, f"wr_{a}{tiles.start}", reuse)
             for i, n in enumerate(tiles):
                 wr_q[a, n] = (code[:, i * P : (i + 1) * P], scale[:, i * P : (i + 1) * P])
 
-        def w3_pass(n, a, stop=False):
+        def flags(n):
+            start = n not in total
+            if start:
+                total[n], done[n] = bank(n), 0
+            return start
+
+        def w3_pass(n, a, j0=0, width=S):
+            start = flags(n)
+            done[n] = done[n] + width
             code, scale = h_q[a]
-            if a == 0:
-                total[n] = bank(n)
+            c0 = a * K + n * P
             nc.tensor.matmul_mx(
-                total[n][:],
+                total[n][:, j0 : j0 + width],
                 lhsT=w3_code[a, n].bitcast(E4M3),
-                lhsT_scale=w3_scale[W3_ROW0:, a * K + n * P : a * K + (n + 1) * P],
-                rhs=code[:].bitcast(E4M3),
-                rhs_scale=scale[:],
-                start=a == 0,
-                stop=stop,
+                lhsT_scale=w3_scale[W3_ROW0:, c0 : c0 + P],
+                rhs=code[:, j0 : j0 + width].bitcast(E4M3),
+                rhs_scale=scale[:, j0 : j0 + width],
+                start=start,
+                stop=done[n] == 2 * PASSES * S,
             )
 
-        def wr_pass(n, a, stop=False):
+        def wr_pass(n, a, j0=0, width=S):
+            start = flags(n)
+            done[n] = done[n] + width
             code, scale = wr_q[a, n]
-            times_v(total[n][:], code.bitcast(E4M3), scale, a, 0, S, False, stop)
+            acc = total[n][:, j0 : j0 + width]
+            times_v(acc, code.bitcast(E4M3), scale, a, j0, width, start, done[n] == 2 * PASSES * S)
 
         def store(n, copy):
             result = sbuf([P, S], F32, f"result{n}")
             copy(result[:], total[n][:])
             nc.sync.dma_start(out[n * P : (n + 1) * P, :], result[:])
 
-        for b, a in ((0, 0), (1, 0), (0, 1)):
-            w2_q[b, a] = quantise(round_w2(b, a)[:], KP, f"w2_{b}{a}")
-        second_product(0)
-        w2_q[1, 1] = quantise(round_w2(1, 1)[:], KP, "w2_11")
-        second_product(1)
-        for u in range(S // TOKENS):
-            gate_times_up(0, u)
-        for half in range(S // HALF):
-            quantise_h(0, half)
-        round_wr(0, FIRST_TILES, nc.scalar.copy)
-        quantise_wr(0, FIRST_TILES)
-        for u in range(S // TOKENS):
-            gate_times_up(1, u, "wr_bf00" if u == HALF // TOKENS else None)
-        for n in FIRST_TILES:
-            w3_pass(n, 0)
-        for n in FIRST_TILES:
+        units = range(S // TOKENS)
+        one = lambda n: range(n, n + 1)
+        for b in range(GROUPS):
+            first_product(b)
+        for b in range(GROUPS):
+            round_w2(b, 0, nc.vector.tensor_copy)
+        for b in range(GROUPS):
+            quantise_w2(b, 0)
+            for u in units:
+                second_pass(b, 0, u)
+        for b, share in ((0, 80), (1, 64)):
+            round_w2(b, 1, nc.vector.tensor_copy, 0, share)
+            round_w2(b, 1, nc.scalar.copy, share)
+        for b in range(GROUPS):
+            quantise_w2(b, 1)
+            for u in units:
+                second_pass(b, 1, u)
+        for tiles in (one(0), one(1), PAIRS[1]):
+            round_wr(0, tiles, nc.scalar.copy)
+        gate_times_up(0, 0)
+        gate_times_up(0, 1)
+        for n in PAIRS[0]:
+            quantise_wr(0, one(n))
             wr_pass(n, 0)
-        for n in LAST_TILES:
-            w3_pass(n, 0)
-        for pair in FIRST_PAIRS:
-            round_wr(1, pair, nc.scalar.copy)
-        for pair in FIRST_PAIRS:
-            quantise_wr(1, pair)
-        quantise_h(1, 0, "wr_bf10")
-        quantise_h(1, 1)
-
-        third, fourth = LAST_PAIRS
-        round_wr(0, third, nc.scalar.copy)
-        round_wr(1, third, nc.vector.tensor_copy)
+        quantise_h(0, 0, "wr_bf00")
+        for n in PAIRS[0]:
+            w3_pass(n, 0, 0, HALF)
+        gate_times_up(0, 2, "wr_bf01")
+        gate_times_up(0, 3)
+        for n in PAIRS[1]:
+            w3_pass(n, 0, 0, HALF)
+        quantise_wr(0, PAIRS[1], "h_bf00")
+        for n in PAIRS[1]:
+            for half in range(2):
+                wr_pass(n, 0, half * HALF, HALF)
+        quantise_h(0, 1)
         for n in FIRST_TILES:
+            w3_pass(n, 0, HALF, HALF)
+        gate_times_up(1, 0, "wr_bf02")
+        gate_times_up(1, 1)
+        gate_times_up(1, 2, "wr_bf01")
+        for n in range(4, 7):
+            w3_pass(n, 0)
+        for tiles in (one(0), one(1), PAIRS[1]):
+            round_wr(1, tiles, nc.scalar.copy)
+        round_wr(0, PAIRS[2], nc.scalar.copy)
+        gate_times_up(1, 3)
+        w3_pass(7, 0)
+        for n in PAIRS[0]:
+            quantise_wr(1, one(n))
             wr_pass(n, 1)
-        for n in FIRST_TILES:
-            w3_pass(n, 1, True)
+        quantise_h(1, 0, "wr_bf10")
+        for n in PAIRS[0]:
+            w3_pass(n, 1, 0, HALF)
+        quantise_h(1, 1)
+        quantise_wr(1, PAIRS[1], "wr_bf02")
+        for n in PAIRS[0]:
+            w3_pass(n, 1, HALF, HALF)
             store(n, nc.scalar.copy)
-        for a in range(PASSES):
-            quantise_wr(a, third)
-        for n in third:
+        for n in PAIRS[1]:
             w3_pass(n, 1)
-            wr_pass(n, 0)
-            wr_pass(n, 1, True)
+            wr_pass(n, 1)
             store(n, nc.scalar.copy)
-        round_wr(0, fourth, nc.vector.tensor_copy)
-        quantise_wr(0, fourth)
-        for n in fourth:
-            round_wr(1, range(n, n + 1), nc.vector.tensor_copy)
-        for n in fourth:
-            quantise_wr(1, range(n, n + 1))
-        for n in fourth:
+        round_wr(1, PAIRS[2], nc.vector.tensor_copy, "wr_bf01")
+        for a in range(PASSES):
+            quantise_wr(a, PAIRS[2])
+        for n in PAIRS[2]:
+            w3_pass(n, 1)
+            for a in range(PASSES):
+                wr_pass(n, a)
+            store(n, nc.scalar.copy)
+        round_wr(0, PAIRS[3], nc.vector.tensor_copy, "wr_bf04")
+        quantise_wr(0, PAIRS[3])
+        for n in PAIRS[3]:
             wr_pass(n, 0)
-        before_last, last = fourth
-        w3_pass(before_last, 1)
-        wr_pass(before_last, 1, True)
-        store(before_last, nc.scalar.copy)
-        wr_pass(last, 1)
-        w3_pass(last, 1, True)
-        store(last, nc.vector.tensor_copy)
+        round_wr(1, one(6), nc.vector.tensor_copy, "wr_raw06")
+        round_wr(1, one(7), nc.vector.tensor_copy, "wr_bf04")
+        for n in PAIRS[3]:
+            quantise_wr(1, one(n))
+        w3_pass(6, 1)
+        wr_pass(6, 1)
+        store(6, nc.scalar.copy)
+        wr_pass(7, 1)
+        w3_pass(7, 1)
+        store(7, nc.vector.tensor_copy)

@@ -33,6 +33,7 @@ FIRST_TILES = range(TILES // 2)
 LAST_TILES = range(TILES // 2, TILES)
 PAIRS = [range(n, n + 2) for n in range(0, TILES, 2)]
 W3_ROW0 = 4
+MOVED_BY_DMA = ("w1_r", "tab", "v_scale", "w2_raw", "wr_raw", "w3_", "result")
 
 
 def tile_list_ast_slot_block_kernel(
@@ -44,7 +45,9 @@ def tile_list_ast_slot_block_kernel(
         psum = ctx.enter_context(tc.psum_pool(name="psum", bufs=1))
 
         def sbuf(shape, dtype, name, reuse=None):
-            return keep.tile(shape, dtype, name=name, tag=reuse or name, align_bytes=256)
+            tag = reuse or name
+            align = 1024 if any(tag.startswith(word) for word in MOVED_BY_DMA) else 256
+            return keep.tile(shape, dtype, name=name, tag=tag, align_bytes=align)
 
         def bank(n):
             return psum.tile([P, S], F32, name=f"bank{n}")

@@ -59,7 +59,7 @@ def tile_list_ast_slot_block_kernel(
             return raw[:]
 
         w1_raw = sbuf([P, PASSES, H], U16, "w1_raw")
-        nc.sync.dma_start(w1_raw[:, 0, :].bitcast(I32), w1_words[0].bitcast(I32))
+        nc.sync.dma_start(w1_raw[:].bitcast(I32), w1_words.bitcast(I32).rearrange("a p c -> p a c"))
         offsets = keep.tile([P, S // 16], U16, name="offsets")
         nc.sync.dma_start(offsets[:], offs)
         step = P // (PASSES * ROWS * ROWS)
@@ -88,7 +88,6 @@ def tile_list_ast_slot_block_kernel(
 
         tab = [load_table(0)]
         w1_rows = load_scales(w1_scales, 0, "w1_rows")[:].rearrange("p (a c) -> p a c", a=PASSES)
-        nc.sync.dma_start(w1_raw[:, 1, :].bitcast(I32), w1_words[1].bitcast(I32))
         tab.append(load_table(1))
         bias = sbuf([P, GROUPS, PACK], F32, "bias")
         nc.sync.dma_start(bias[:], b1.rearrange("(b p t) -> p b t", p=P, t=PACK))
@@ -118,14 +117,14 @@ def tile_list_ast_slot_block_kernel(
             for n in tiles:
                 w3_code[a, n] = tile[:, (n - tiles.start) * P : (n - tiles.start + 1) * P]
 
-        load_wr(0, FIRST_TILES)
+        for a in range(PASSES):
+            load_wr(a, FIRST_TILES)
         w3_scale = load_scales(w3_scales, W3_ROW0, "w3_scale")
         load_w3(0, range(TILES))
-        load_wr(1, FIRST_TILES)
+        load_wr(0, LAST_TILES)
         load_w3(1, range(PAIRS[3].start))
         for pair in PAIRS[2:]:
-            for a in range(PASSES):
-                load_wr(a, pair)
+            load_wr(1, pair)
         load_w3(1, PAIRS[3])
 
         run = LINE_BYTES // 2
@@ -210,24 +209,21 @@ def tile_list_ast_slot_block_kernel(
                 )
 
         def gate_times_up(b, u, reuse=None):
-            half, part = divmod(u, HALF // TOKENS)
-            if part == 0:
-                h_bf[b, half] = sbuf([P, HALF * PACK], BF16, f"h_bf{b}{half}", reuse)
+            h_bf[b, u] = sbuf([P, TOKENS * PACK], BF16, f"h_bf{b}{u}", reuse)
             tokens = slice(u * TOKENS, (u + 1) * TOKENS)
-            dst = h_bf[b, half][:, part * TOKENS * PACK : (part + 1) * TOKENS * PACK]
             nc.vector.tensor_tensor(
-                dst.rearrange("p (c i t) -> p c t i", i=LINE, t=PACK),
+                h_bf[b, u][:].rearrange("p (c i t) -> p c t i", i=LINE, t=PACK),
                 up[b, u][:].rearrange("p (t c i) -> p c t i", t=PACK, i=LINE),
                 gate[b][:, :, tokens].rearrange("p t (c i) -> p c t i", i=LINE),
                 MULT,
             )
 
-        def quantise_h(b, half, reuse=None):
-            if half == 0:
-                h_q[b] = (sbuf([P, S], U32, f"h_code{b}", reuse), sbuf([P, S], U8, f"h_scale{b}"))
+        def quantise_h(b, u):
+            if u == 0:
+                h_q[b] = (sbuf([P, S], U32, f"h_code{b}"), sbuf([P, S], U8, f"h_scale{b}"))
             code, scale = h_q[b]
-            cols = slice(half * HALF, (half + 1) * HALF)
-            nc.vector.quantize_mx(code[:, cols].bitcast(E4M3), scale[:, cols], h_bf[b, half][:])
+            cols = slice(u * TOKENS, (u + 1) * TOKENS)
+            nc.vector.quantize_mx(code[:, cols].bitcast(E4M3), scale[:, cols], h_bf[b, u][:])
 
         wr_bf, wr_q, total, done = {}, {}, {}, {}
 
@@ -273,8 +269,10 @@ def tile_list_ast_slot_block_kernel(
             acc = total[n][:, j0 : j0 + width]
             times_v(acc, code.bitcast(E4M3), scale, a, j0, width, start, done[n] == 2 * PASSES * S)
 
+        spent = ("tab0", "tab1", "w1_raw", "tab_rows", "w1_rows")
+
         def store(n, copy):
-            result = sbuf([P, S], F32, f"result{n}")
+            result = sbuf([P, S], F32, f"result{n}", spent[n] if n < len(spent) else None)
             copy(result[:], total[n][:])
             nc.sync.dma_start(out[n * P : (n + 1) * P, :], result[:])
 
@@ -288,78 +286,74 @@ def tile_list_ast_slot_block_kernel(
             quantise_w2(b, 0)
             for u in units:
                 second_pass(b, 0, u)
-        for b, share in ((0, 80), (1, 64)):
+        for b, share in ((0, 80), (1, 72)):
             round_w2(b, 1, nc.vector.tensor_copy, 0, share)
             round_w2(b, 1, nc.scalar.copy, share)
         for b in range(GROUPS):
             quantise_w2(b, 1)
             for u in units:
                 second_pass(b, 1, u)
-        for tiles in (one(0), one(1), PAIRS[1]):
-            round_wr(0, tiles, nc.scalar.copy)
-        gate_times_up(0, 0)
-        gate_times_up(0, 1)
-        for n in PAIRS[0]:
-            quantise_wr(0, one(n))
-            wr_pass(n, 0)
-        quantise_h(0, 0, "wr_bf00")
-        for n in PAIRS[0]:
-            w3_pass(n, 0, 0, HALF)
-        gate_times_up(0, 2, "wr_bf01")
-        gate_times_up(0, 3)
-        for n in PAIRS[1]:
-            w3_pass(n, 0, 0, HALF)
-        quantise_wr(0, PAIRS[1], "h_bf00")
-        for n in PAIRS[1]:
-            for half in range(2):
-                wr_pass(n, 0, half * HALF, HALF)
-        quantise_h(0, 1)
         for n in FIRST_TILES:
-            w3_pass(n, 0, HALF, HALF)
-        gate_times_up(1, 0, "wr_bf02")
-        gate_times_up(1, 1)
-        gate_times_up(1, 2, "wr_bf01")
-        for n in range(4, 7):
-            w3_pass(n, 0)
+            round_wr(0, one(n), nc.scalar.copy)
         for tiles in (one(0), one(1), PAIRS[1]):
             round_wr(1, tiles, nc.scalar.copy)
         round_wr(0, PAIRS[2], nc.scalar.copy)
+
+        def wr_tile(n, a):
+            quantise_wr(a, one(n))
+            wr_pass(n, a)
+
+        gate_times_up(0, 0)
+        gate_times_up(0, 1)
+        wr_tile(0, 0)
+        wr_tile(1, 0)
+        gate_times_up(0, 2)
+        quantise_h(0, 0)
+        wr_tile(2, 0)
+        gate_times_up(0, 3)
+        quantise_h(0, 1)
+        wr_tile(3, 0)
+        quantise_h(0, 2)
+        wr_tile(0, 1)
+        quantise_h(0, 3)
+        for n in FIRST_TILES:
+            w3_pass(n, 0)
+        gate_times_up(1, 0)
+        w3_pass(4, 0)
+        gate_times_up(1, 1)
+        w3_pass(5, 0)
+        wr_tile(1, 1)
+        gate_times_up(1, 2)
+        w3_pass(6, 0)
+        quantise_wr(1, PAIRS[1])
+        for n in PAIRS[1]:
+            wr_pass(n, 1)
         gate_times_up(1, 3)
         w3_pass(7, 0)
-        for n in PAIRS[0]:
-            quantise_wr(1, one(n))
-            wr_pass(n, 1)
-        quantise_h(1, 0, "wr_bf10")
-        for n in PAIRS[0]:
-            w3_pass(n, 1, 0, HALF)
-        quantise_h(1, 1)
-        quantise_wr(1, PAIRS[1], "wr_bf02")
-        for n in PAIRS[0]:
-            w3_pass(n, 1, HALF, HALF)
-            store(n, nc.scalar.copy)
-        for n in PAIRS[1]:
+        for u in units:
+            quantise_h(1, u)
+        for n in FIRST_TILES:
             w3_pass(n, 1)
-            wr_pass(n, 1)
             store(n, nc.scalar.copy)
-        round_wr(1, PAIRS[2], nc.vector.tensor_copy, "wr_bf01")
-        for a in range(PASSES):
-            quantise_wr(a, PAIRS[2])
+        round_wr(0, PAIRS[3], nc.vector.tensor_copy)
+        quantise_wr(0, PAIRS[2])
         for n in PAIRS[2]:
             w3_pass(n, 1)
-            for a in range(PASSES):
-                wr_pass(n, a)
-            store(n, nc.scalar.copy)
-        round_wr(0, PAIRS[3], nc.vector.tensor_copy, "wr_bf04")
-        quantise_wr(0, PAIRS[3])
-        for n in PAIRS[3]:
             wr_pass(n, 0)
-        round_wr(1, one(6), nc.vector.tensor_copy, "wr_raw06")
-        round_wr(1, one(7), nc.vector.tensor_copy, "wr_bf04")
-        for n in PAIRS[3]:
-            quantise_wr(1, one(n))
+        quantise_wr(0, PAIRS[3])
+        for n in PAIRS[2]:
+            round_wr(1, one(n), nc.vector.tensor_copy)
+        wr_tile(4, 1)
+        store(4, nc.scalar.copy)
+        wr_pass(6, 0)
+        wr_tile(5, 1)
+        store(5, nc.scalar.copy)
+        wr_pass(7, 0)
+        round_wr(1, one(6), nc.vector.tensor_copy)
+        round_wr(1, one(7), nc.vector.tensor_copy)
         w3_pass(6, 1)
-        wr_pass(6, 1)
+        wr_tile(6, 1)
         store(6, nc.scalar.copy)
-        wr_pass(7, 1)
         w3_pass(7, 1)
+        wr_tile(7, 1)
         store(7, nc.vector.tensor_copy)

from contextlib import ExitStack

import concourse.mybir as mybir

K, H, T, S = 1024, 1024, 2048, 512
FLOPS = 2 * S * (K * H + K * H + H * K + K * K)

F32 = mybir.dt.float32
BF16 = mybir.dt.bfloat16
I32 = mybir.dt.int32
U32 = mybir.dt.uint32
U16 = mybir.dt.uint16
U8 = mybir.dt.uint8
E4M3 = mybir.dt.float8_e4m3fn_x4
E2M1 = mybir.dt.float4_e2m1fn_x4
GELU = mybir.ActivationFunctionType.Gelu_apprx_tanh
MULT = mybir.AluOpType.mult

P = 128
PACK = 4
KP = P * PACK
PASSES = K // KP
GROUPS = H // KP
QUAD = 32
ROWS = 4
BLOCK = 8
LINE_BYTES = 16
LINE = LINE_BYTES // 4
TOKENS = S // PACK
HALF = S // 2
TILES = K // P
FIRST_TILES = range(TILES // 2)
LAST_TILES = range(TILES // 2, TILES)
PAIRS = [range(n, n + 2) for n in range(0, TILES, 2)]
W3_ROW0 = 4
MOVED_BY_DMA = ("w1_r", "tab", "v_scale", "w2_raw", "wr_raw", "w3_", "result")


def tile_list_ast_slot_block_kernel(
    tc, tab_words, tab_scales, offs, w1_words, w1_scales, b1, w2, w3_words, w3_scales, wr, out
):
    nc = tc.nc
    with ExitStack() as ctx:
        keep = ctx.enter_context(tc.tile_pool(name="keep", bufs=1))
        psum = ctx.enter_context(tc.psum_pool(name="psum", bufs=1))

        def sbuf(shape, dtype, name, reuse=None):
            tag = reuse or name
            align = 1024 if any(tag.startswith(word) for word in MOVED_BY_DMA) else 256
            return keep.tile(shape, dtype, name=name, tag=tag, align_bytes=align)

        def bank(n):
            return psum.tile([P, S], F32, name=f"bank{n}")

        def load_rows(w, a, cols, name):
            raw = sbuf([P, PACK, len(cols)], F32, name)
            rows = w[a * KP : (a + 1) * KP, cols.start : cols.stop]
            nc.sync.dma_start(raw[:], rows.rearrange("(p j) c -> p j c", j=PACK))
            return raw[:]

        w1_raw = sbuf([P, PASSES, H], U16, "w1_raw")
        nc.sync.dma_start(w1_raw[:].bitcast(I32), w1_words.bitcast(I32).rearrange("a p c -> p a c"))
        offsets = keep.tile([P, S // 16], U16, name="offsets")
        nc.sync.dma_start(offsets[:], offs)
        step = P // (PASSES * ROWS * ROWS)
        tab_rows = sbuf([P, T], U8, "tab_rows")
        nc.vector.memset(tab_rows[:].bitcast(I32), 0)
        nc.sync.dma_start(tab_rows[:].bitcast(I32)[0:P:step, :], tab_scales.bitcast(I32).rearrange("a s c -> s a c"))
        picked_rows = sbuf([P, S], U8, "picked_rows")
        nc.vector.tensor_copy(picked_rows[:], tab_rows[:].indirect(offsets[:]))
        v_scale = sbuf([P, PASSES * S], U8, "v_scale")
        nc.vector.memset(v_scale[:].bitcast(I32), 0)

        def load_scales(scales, row0, name):
            tile = sbuf([P, PASSES * scales.shape[2]], U8, name)
            nc.vector.memset(tile[:].bitcast(I32), 0)
            for r in range(ROWS):
                nc.sync.dma_start(
                    tile[:].bitcast(I32).rearrange("p (a c) -> p a c", a=PASSES)[row0 + r : P : QUAD],
                    scales.bitcast(I32).rearrange("a (d r) c -> r d a c", r=ROWS)[r],
                )
            return tile

        def load_table(a):
            tile = sbuf([P, T], U32, f"tab{a}")
            nc.sync.dma_start(tile[:].bitcast(I32), tab_words[a].rearrange("p c i -> p (c i)").bitcast(I32))
            return tile

        tab = [load_table(0)]
        w1_rows = load_scales(w1_scales, 0, "w1_rows")[:].rearrange("p (a c) -> p a c", a=PASSES)
        tab.append(load_table(1))
        bias = sbuf([P, GROUPS, PACK], F32, "bias")
        nc.sync.dma_start(bias[:], b1.rearrange("(b p t) -> p b t", p=P, t=PACK))

        for d in (0, 2, 1, 3):
            nc.sync.dma_start(
                v_scale[:].bitcast(I32)[d * QUAD : d * QUAD + ROWS, :],
                picked_rows[:].bitcast(I32)[d * QUAD : (d + 1) * QUAD : step, :],
            )

        w2_raw = {}
        for a in range(PASSES):
            whole = load_rows(w2, a, range(H), f"w2_raw{a}")
            for b in range(GROUPS):
                w2_raw[b, a] = whole[:, :, b * KP : (b + 1) * KP]
        wr_raw, w3_code = {}, {}

        def load_wr(a, tiles):
            raw = load_rows(wr, a, range(tiles.start * P, tiles.stop * P), f"wr_raw{a}{tiles.start}")
            for n in tiles:
                wr_raw[a, n] = (raw, tiles.start)

        def load_w3(a, tiles):
            tile = sbuf([P, len(tiles) * P], U32, f"w3_code{a}{tiles.start}")
            words = w3_words[a].rearrange("p c i -> p (c i)").bitcast(I32)
            nc.sync.dma_start(tile[:].bitcast(I32), words[:, tiles.start * P : tiles.stop * P])
            for n in tiles:
                w3_code[a, n] = tile[:, (n - tiles.start) * P : (n - tiles.start + 1) * P]

        for a in range(PASSES):
            load_wr(a, FIRST_TILES)
        w3_scale = load_scales(w3_scales, W3_ROW0, "w3_scale")
        load_w3(0, range(TILES))
        load_wr(0, LAST_TILES)
        load_w3(1, range(PAIRS[3].start))
        for pair in PAIRS[2:]:
            load_wr(1, pair)
        load_w3(1, PAIRS[3])

        run = LINE_BYTES // 2
        w1_code = sbuf([P, PASSES, H], U16, "w1_code")
        for a in range(PASSES):
            nc.scalar.copy(
                w1_code[:, a, :].rearrange("p (b t c i) -> p b c t i", t=PACK, i=run, b=GROUPS),
                w1_raw[:, a, :].rearrange("p (b c i t) -> p b c t i", t=PACK, i=run, b=GROUPS),
            )
        def gather_words(a):
            picked = sbuf([P, S], U32, f"v_code{a}")
            nc.vector.tensor_copy(picked[:], tab[a][:].indirect(offsets[:]))
            return picked

        def order_w1_scale(b):
            tile = sbuf([P, PASSES, KP], U8, f"w1_scale{b}")
            nc.vector.tensor_copy(
                tile[:].rearrange("p a (t c i) -> p a c t i", t=PACK, i=LINE_BYTES),
                w1_rows[:, :, b * KP : (b + 1) * KP].rearrange("p a (c i t) -> p a c t i", t=PACK, i=LINE_BYTES),
            )
            return tile

        v_code = [gather_words(0)]
        w1_scale = [order_w1_scale(b) for b in range(GROUPS)]
        v_code.append(gather_words(1))

        def times_v(acc, code, scale, a, j0, width, start, stop):
            nc.tensor.matmul_mx(
                acc,
                lhsT=code,
                lhsT_scale=scale,
                rhs=v_code[a][:, j0 : j0 + width].bitcast(E4M3),
                rhs_scale=v_scale[:, a * S + j0 : a * S + j0 + width],
                start=start,
                stop=stop,
            )

        gate = {}

        def first_product(b):
            gate[b] = sbuf([P, PACK, S], F32, f"gate{b}")
            for t in range(PACK):
                pre = bank(PACK * b + t)
                c0 = b * KP + t * P
                for a in range(PASSES):
                    scale = w1_scale[b][:, a, t * P : (t + 1) * P]
                    times_v(pre[:], w1_code[:, a, c0 : c0 + P].bitcast(E2M1), scale, a, 0, S, a == 0, a == PASSES - 1)
                nc.scalar.activation(gate[b][:, t, :], pre[:], GELU, bias=bias[:, b, t : t + 1])

        def quantise(grouped, width, name, reuse=None):
            code = sbuf([P, width], U32, name + "_code", reuse)
            scale = sbuf([P, width], U8, name + "_scale")
            nc.vector.quantize_mx(code[:].bitcast(E4M3), scale[:], grouped)
            return code, scale

        w2_bf, w2_q, up, h_bf, h_q = {}, {}, {}, {}, {}

        def round_w2(b, a, copy, m0=0, m1=P):
            if m0 == 0:
                w2_bf[b, a] = sbuf([P, KP * PACK], BF16, f"w2_bf{b}{a}")
            dst = w2_bf[b, a][:].rearrange("p (t m j) -> p m j t", t=PACK, j=PACK)
            src = w2_raw[b, a].rearrange("p j (m t) -> p m j t", t=PACK)
            copy(dst[:, m0:m1], src[:, m0:m1])

        def quantise_w2(b, a):
            w2_q[b, a] = quantise(w2_bf[b, a][:], KP, f"w2_{b}{a}")

        def second_pass(b, a, u):
            if a == 0:
                up[b, u] = bank(PACK * b + u)
            code, scale = w2_q[b, a]
            for t in range(PACK):
                times_v(
                    up[b, u][:, t * TOKENS : (t + 1) * TOKENS],
                    code[:, t * P : (t + 1) * P].bitcast(E4M3),
                    scale[:, t * P : (t + 1) * P],
                    a,
                    u * TOKENS,
                    TOKENS,
                    a == 0 and t == 0,
                    a == PASSES - 1 and t == PACK - 1,
                )

        def gate_times_up(b, u, reuse=None):
            h_bf[b, u] = sbuf([P, TOKENS * PACK], BF16, f"h_bf{b}{u}", reuse)
            tokens = slice(u * TOKENS, (u + 1) * TOKENS)
            nc.vector.tensor_tensor(
                h_bf[b, u][:].rearrange("p (c i t) -> p c t i", i=LINE, t=PACK),
                up[b, u][:].rearrange("p (t c i) -> p c t i", t=PACK, i=LINE),
                gate[b][:, :, tokens].rearrange("p t (c i) -> p c t i", i=LINE),
                MULT,
            )

        def quantise_h(b, u):
            if u == 0:
                h_q[b] = (sbuf([P, S], U32, f"h_code{b}"), sbuf([P, S], U8, f"h_scale{b}"))
            code, scale = h_q[b]
            cols = slice(u * TOKENS, (u + 1) * TOKENS)
            nc.vector.quantize_mx(code[:, cols].bitcast(E4M3), scale[:, cols], h_bf[b, u][:])

        wr_bf, wr_q, total, done = {}, {}, {}, {}

        def round_wr(a, tiles, copy, reuse=None):
            raw, first = wr_raw[a, tiles.start]
            wr_bf[a, tiles.start] = sbuf([P, len(tiles) * KP], BF16, f"wr_bf{a}{tiles.start}", reuse)
            src = raw[:, :, (tiles.start - first) * P : (tiles.stop - first) * P]
            copy(
                wr_bf[a, tiles.start][:].rearrange("p (c i j) -> p c j i", i=LINE, j=PACK),
                src.rearrange("p j (c i) -> p c j i", i=LINE),
            )

        def quantise_wr(a, tiles, reuse=None):
            code, scale = quantise(wr_bf[a, tiles.start][:], len(tiles) * P, f"wr_{a}{tiles.start}", reuse)
            for i, n in enumerate(tiles):
                wr_q[a, n] = (code[:, i * P : (i + 1) * P], scale[:, i * P : (i + 1) * P])

        def flags(n):
            start = n not in total
            if start:
                total[n], done[n] = bank(n), 0
            return start

        def w3_pass(n, a, j0=0, width=S):
            start = flags(n)
            done[n] = done[n] + width
            code, scale = h_q[a]
            c0 = a * K + n * P
            nc.tensor.matmul_mx(
                total[n][:, j0 : j0 + width],
                lhsT=w3_code[a, n].bitcast(E4M3),
                lhsT_scale=w3_scale[W3_ROW0:, c0 : c0 + P],
                rhs=code[:, j0 : j0 + width].bitcast(E4M3),
                rhs_scale=scale[:, j0 : j0 + width],
                start=start,
                stop=done[n] == 2 * PASSES * S,
            )

        def wr_pass(n, a, j0=0, width=S):
            start = flags(n)
            done[n] = done[n] + width
            code, scale = wr_q[a, n]
            acc = total[n][:, j0 : j0 + width]
            times_v(acc, code.bitcast(E4M3), scale, a, j0, width, start, done[n] == 2 * PASSES * S)

        spent = ("tab0", "tab1", "w1_raw", "tab_rows", "w1_rows")

        def store(n, copy):
            result = sbuf([P, S], F32, f"result{n}", spent[n] if n < len(spent) else None)
            copy(result[:], total[n][:])
            nc.sync.dma_start(out[n * P : (n + 1) * P, :], result[:])

        units = range(S // TOKENS)
        one = lambda n: range(n, n + 1)
        for b in range(GROUPS):
            first_product(b)
        for b in range(GROUPS):
            round_w2(b, 0, nc.vector.tensor_copy)
        for b in range(GROUPS):
            quantise_w2(b, 0)
            for u in units:
                second_pass(b, 0, u)
        for b, share in ((0, 80), (1, 72)):
            round_w2(b, 1, nc.vector.tensor_copy, 0, share)
            round_w2(b, 1, nc.scalar.copy, share)
        for b in range(GROUPS):
            quantise_w2(b, 1)
            for u in units:
                second_pass(b, 1, u)
        for n in FIRST_TILES:
            round_wr(0, one(n), nc.scalar.copy)
        for tiles in (one(0), one(1), PAIRS[1]):
            round_wr(1, tiles, nc.scalar.copy)
        round_wr(0, PAIRS[2], nc.scalar.copy)

        def wr_tile(n, a):
            quantise_wr(a, one(n))
            wr_pass(n, a)

        gate_times_up(0, 0)
        gate_times_up(0, 1)
        wr_tile(0, 0)
        wr_tile(1, 0)
        gate_times_up(0, 2)
        quantise_h(0, 0)
        wr_tile(2, 0)
        gate_times_up(0, 3)
        quantise_h(0, 1)
        wr_tile(3, 0)
        quantise_h(0, 2)
        wr_tile(0, 1)
        quantise_h(0, 3)
        for n in FIRST_TILES:
            w3_pass(n, 0)
        gate_times_up(1, 0)
        w3_pass(4, 0)
        gate_times_up(1, 1)
        w3_pass(5, 0)
        wr_tile(1, 1)
        gate_times_up(1, 2)
        w3_pass(6, 0)
        quantise_wr(1, PAIRS[1])
        for n in PAIRS[1]:
            wr_pass(n, 1)
        gate_times_up(1, 3)
        w3_pass(7, 0)
        for u in units:
            quantise_h(1, u)
        for n in FIRST_TILES:
            w3_pass(n, 1)
            store(n, nc.scalar.copy)
        round_wr(0, PAIRS[3], nc.vector.tensor_copy)
        quantise_wr(0, PAIRS[2])
        for n in PAIRS[2]:
            w3_pass(n, 1)
            wr_pass(n, 0)
        quantise_wr(0, PAIRS[3])
        for n in PAIRS[2]:
            round_wr(1, one(n), nc.vector.tensor_copy)
        wr_tile(4, 1)
        store(4, nc.scalar.copy)
        wr_pass(6, 0)
        wr_tile(5, 1)
        store(5, nc.scalar.copy)
        wr_pass(7, 0)
        round_wr(1, one(6), nc.vector.tensor_copy)
        round_wr(1, one(7), nc.vector.tensor_copy)
        w3_pass(6, 1)
        wr_tile(6, 1)
        store(6, nc.scalar.copy)
        w3_pass(7, 1)
        wr_tile(7, 1)
        store(7, nc.vector.tensor_copy)
